import numpy as np
import ml_dtypes


def mxq(x, axis, fmt="e4m3"):
    dtype, down = {"e4m3": (ml_dtypes.float8_e4m3fn, 7), "e5m2": (ml_dtypes.float8_e5m2, 14)}[fmt]
    v = np.moveaxis(np.asarray(x, np.float32).astype(ml_dtypes.bfloat16).astype(np.float64), axis, -1)
    blocks = v.reshape(v.shape[:-1] + (-1, 32))
    amax = np.abs(blocks).max(-1, keepdims=True)
    byte = np.maximum(np.where(amax > 0, np.frexp(amax)[1] - 1 + 127, 0) - down, 1)
    scale = np.exp2(byte - 127.0)
    codes = (blocks / scale).astype(np.float32).astype(dtype).astype(np.float64)
    return np.moveaxis((codes * scale).reshape(v.shape), -1, axis)


WIDE = False


def mx_kscale(k):
    if not WIDE:
        return np.ones(k)
    levels = np.array([30, -30])
    if k % 512:
        return np.exp2(np.random.permutation(np.resize(levels, k // 32))).repeat(32)
    a = np.empty((k // 512, 16))
    for p in range(k // 512):
        a[p, :8] = np.random.permutation(np.resize(levels, 8))
        for g in range(8):
            far = levels[np.abs(levels - a[p, g]) >= 10]
            a[p, g + 8] = far[np.random.randint(len(far))]
    return np.exp2(a.ravel()).repeat(32)


def f64(x):
    return np.asarray(x).astype(np.float64)


def striped(idx):
    return np.tile(idx.reshape(-1, 16).T, (8, 1)).astype(np.uint16)


def unstriped(offs):
    return offs[:16].T.reshape(-1).astype(np.int64)


E2M1 = np.array([0.0, 0.5, 1.0, 1.5, 2.0, 3.0, 4.0, 6.0, -0.0, -0.5, -1.0, -1.5, -2.0, -3.0, -4.0, -6.0])


def pack_weight(w, fmt):
    k, n = w.shape
    w = f64(np.asarray(w, np.float32).astype(ml_dtypes.bfloat16)).reshape(k // 32, 32, n)
    amax = np.abs(w).max(1)
    if fmt == "e4m3":
        byte = np.frexp(amax)[1] - 1 + 127 - 7
    else:
        mant, ex = np.frexp(amax / 6.0)
        byte = np.where(mant > 0.5, ex, ex - 1) + 127
    byte = np.clip(np.where(amax > 0, byte, 1), 1, 254)
    scaled = (w * np.exp2(127.0 - byte)[:, None, :]).reshape(k, n).astype(np.float32)
    by_word = np.ascontiguousarray(scaled.reshape(k // 512, 128, 4, n).transpose(0, 1, 3, 2))
    if fmt == "e4m3":
        words = by_word.astype(ml_dtypes.float8_e4m3fn).view(np.uint8)
    else:
        c = by_word.astype(ml_dtypes.float4_e2m1fn).view(np.uint8) & 0xF
        words = (c[..., 0::2] | (c[..., 1::2] << 4)).reshape(k // 512, 128, 2 * n)
    return np.ascontiguousarray(words), np.ascontiguousarray(byte.astype(np.uint8).reshape(k // 512, 16, n))


def unpack_weight(words, scales, fmt):
    g, _, n = scales.shape
    words = np.ascontiguousarray(words).reshape(g, 128, n, -1)
    if fmt == "e4m3":
        vals = words.view(ml_dtypes.float8_e4m3fn).astype(np.float64)
    else:
        nib = np.empty((g, 128, n, 4), np.uint8)
        nib[..., 0::2] = words & 0xF
        nib[..., 1::2] = words >> 4
        vals = E2M1[nib]
    vals = vals * np.repeat(np.exp2(scales.astype(np.float64) - 127.0), 8, axis=1)[..., None]
    return vals.transpose(0, 1, 3, 2).reshape(g * 512, n)


K, N, T, J = 1024, 512, 2048, 1024


def setup_inputs():
    n = np.random.standard_normal
    s = mx_kscale(K)[:, None]
    m = np.exp(0.5 * n((1, J)))
    p_w = pack_weight(n((K, N)) / np.sqrt(K) / s, "e4m3")
    return {
        "dy": (m * n((K, J)) * s).astype(np.float32),
        "w_words": p_w[0],
        "w_scales": p_w[1],
        "res": (n((N, J))).astype(np.float32),
        "wgo": np.tile(np.random.uniform(0.5, 2.0, J), (128, 1)).astype(np.float32),
        "offs": striped(np.random.permutation(T)[:J]),
    }


def reference(dy, w_words, w_scales, res, wgo, offs):
    idx = unstriped(offs)
    dy_q_ = mxq(f64(dy), 0, "e5m2")
    dy_r_ = mxq(f64(dy) - dy_q_, 0, "e4m3")
    w_ = unpack_weight(w_words, w_scales, "e4m3")
    dx = w_.T @ dy_q_ + w_.T @ dy_r_
    out = np.zeros((N, T))
    out[:, idx] = f64(wgo)[0] * (dx + f64(res))
    return out

@@ -1,0 +1,203 @@
+from contextlib import ExitStack
+
+import concourse.mybir as mybir
+from concourse.masks import make_identity
+
+K, N, T, J = 1024, 512, 2048, 1024
+FLOPS = 3221225472
+
+F32 = mybir.dt.float32
+BF16 = mybir.dt.bfloat16
+I32 = mybir.dt.int32
+U32 = mybir.dt.uint32
+U16 = mybir.dt.uint16
+U8 = mybir.dt.uint8
+E4M3 = mybir.dt.float8_e4m3fn_x4
+E5M2 = mybir.dt.float8_e5m2_x4
+ALU = mybir.AluOpType
+
+P = 128
+PACK = 4
+K_PASS = P * PACK
+PASSES = K // K_PASS
+CHUNK = 512
+HALF = CHUNK // 2
+ROW_TILES = N // P
+RUN = 4
+
+
+def tile_list_embg_tgq8_res_kernel(tc, dy, w_words, w_scales, res, wgo, offs, out):
+    nc = tc.nc
+
+    with ExitStack() as ctx:
+        keep = ctx.enter_context(tc.tile_pool(name="keep", bufs=1))
+        psum = ctx.enter_context(tc.psum_pool(name="psum", bufs=1))
+        banks = [psum.tile([P, CHUNK], F32, name=f"bank{b}") for b in range(8)]
+
+        def sb(name, shape, dtype, tag=None):
+            return keep.tile(shape, dtype, name=name, tag=tag or name, align_bytes=64)
+
+        def load_dy(name, a, j0, width):
+            raw = sb(name, [P, PACK, width], F32)
+            rows = dy[a * K_PASS : (a + 1) * K_PASS, j0 : j0 + width]
+            nc.sync.dma_start(out=raw[:], in_=rows.rearrange("(p t) j -> p t j", t=PACK))
+            return raw
+
+        def weave(engine, dst, src):
+            d = dst.rearrange("p (c i t) -> p c t i", i=RUN, t=PACK)
+            s = src.rearrange("p t (c i) -> p c t i", i=RUN)
+            if engine == "scalar":
+                nc.scalar.copy(out=d, in_=s)
+            else:
+                nc.vector.tensor_copy(out=d, in_=s)
+
+        raw_a = [[load_dy(f"raw_a{a}{h}", a, h * HALF, HALF) for h in range(2)] for a in range(PASSES)]
+        w_codes = sb("w_codes", [P, PASSES, N], U32)
+        nc.sync.dma_start(
+            out=w_codes[:].bitcast(I32),
+            in_=w_words.rearrange("a p n i -> p a (n i)").bitcast(I32),
+        )
+        w_sc = sb("w_sc", [P, PASSES, N], U8)
+        nc.vector.memset(w_sc[:].rearrange("p a n -> p (a n)").bitcast(I32), 0)
+        for q in range(4):
+            nc.sync.dma_start(
+                out=w_sc[32 * q : 32 * q + 4, :, :].bitcast(I32),
+                in_=w_scales[:, 4 * q : 4 * q + 4, :].rearrange("a r n -> r a n").bitcast(I32),
+            )
+        raw_b = [load_dy(f"raw_b{a}", a, CHUNK, CHUNK) for a in range(PASSES)]
+        offsets = keep.tile([P, J // 16], U16, name="offsets")
+        nc.sync.dma_start(offsets[:], offs)
+        wgo_sb = sb("wgo_sb", [P, J], F32)
+        res_sb = {}
+
+        def load_res(c, r):
+            res_sb[c, r] = sb(f"res{c}{r}", [P, CHUNK], F32)
+            nc.sync.dma_start(out=res_sb[c, r][:], in_=res[r * P : (r + 1) * P, c * CHUNK : (c + 1) * CHUNK])
+
+        load_res(0, 0)
+        nc.sync.dma_start(out=wgo_sb[:], in_=wgo)
+        for c in range(2):
+            for r in range(ROW_TILES):
+                if (c, r) != (0, 0):
+                    load_res(c, r)
+
+        eye = sb("eye", [P, P], BF16)
+        make_identity(nc, eye[:])
+        eye_in = sb("eye_in", [P, PACK * K_PASS], BF16)
+        nc.vector.memset(eye_in[:].bitcast(I32), 0)
+        for t in range(PACK):
+            nc.vector.tensor_copy(out=eye_in[:, t * K_PASS + t : (t + 1) * K_PASS : PACK], in_=eye[:])
+        eye_codes = sb("eye_codes", [P, K_PASS], U32)
+        eye_sc = sb("eye_sc", [P, K_PASS], U8)
+        nc.vector.quantize_mx(out=eye_codes[:].bitcast(E4M3), scales=eye_sc[:], in_=eye_in[:])
+
+        def quantise(name, src, fmt):
+            codes = sb(name + "_codes", [P, CHUNK], U32)
+            scales = sb(name + "_sc", [P, CHUNK], U8)
+            nc.vector.quantize_mx(out=codes[:].bitcast(fmt), scales=scales[:], in_=src[:])
+            return codes, scales
+
+        def decode(bank, t, q):
+            cols = slice(t * P, (t + 1) * P)
+            nc.tensor.matmul_mx(
+                out=bank[:],
+                lhsT=eye_codes[:, cols].bitcast(E4M3),
+                lhsT_scale=eye_sc[:, cols],
+                rhs=q[0][:].bitcast(E5M2),
+                rhs_scale=q[1][:],
+                start=True,
+                stop=True,
+            )
+
+        def product(bank, r, operands):
+            cols = slice(r * P, (r + 1) * P)
+            for i, (a, q, fmt) in enumerate(operands):
+                nc.tensor.matmul_mx(
+                    out=bank[:],
+                    lhsT=w_codes[:, a, cols].bitcast(E4M3),
+                    lhsT_scale=w_sc[:, a, cols],
+                    rhs=q[0][:].bitcast(fmt),
+                    rhs_scale=q[1][:],
+                    start=(i == 0),
+                    stop=(i == len(operands) - 1),
+                )
+
+        q_a = []
+        for a in range(PASSES):
+            hi = sb(f"hi_a{a}", [P, CHUNK * PACK], BF16)
+            weave("scalar", hi[:, : HALF * PACK], raw_a[a][0][:])
+            weave("vector", hi[:, HALF * PACK :], raw_a[a][1][:])
+            q_a.append(quantise(f"q_a{a}", hi, E5M2))
+            for t in range(PACK):
+                decode(banks[4 * a + t], t, q_a[a])
+        r_a = []
+        for a in range(PASSES):
+            lo = sb(f"lo_a{a}", [P, CHUNK * PACK], BF16)
+            for h in range(2):
+                planes = sb(f"pl_a{a}{h}", [P, PACK, HALF], BF16)
+                for t in range(PACK):
+                    nc.vector.tensor_tensor(
+                        planes[:, t, :], raw_a[a][h][:, t, :], banks[4 * a + t][:, h * HALF : (h + 1) * HALF], ALU.subtract
+                    )
+                last = (a, h) == (PASSES - 1, 1)
+                weave("vector" if last else "scalar", lo[:, h * HALF * PACK : (h + 1) * HALF * PACK], planes[:])
+            r_a.append(lo)
+        r_a = [quantise(f"r_a{a}", r_a[a], E4M3) for a in range(PASSES)]
+        ops_a = [(a, q_a[a], E5M2) for a in range(PASSES)] + [(a, r_a[a], E4M3) for a in range(PASSES)]
+        for r in range(ROW_TILES):
+            product(banks[r], r, ops_a)
+
+        pages = []
+
+        def clear_page(tag):
+            page = sb(f"page{len(pages)}", [P, T], F32, tag=tag)
+            nc.gpsimd.memset(page[:], 0.0)
+            pages.append(page)
+
+        clear_page("hi_a1")
+
+        def finish(c, r, bank, tag):
+            total = sb(f"total{c}{r}", [P, CHUNK], F32, tag=tag)
+            nc.vector.tensor_tensor(total[:], bank[:], res_sb[c, r][:], ALU.add)
+            nc.vector.tensor_tensor(
+                pages[r][:].indirect(offsets[:, c * CHUNK // 16 : (c + 1) * CHUNK // 16]),
+                total[:],
+                wgo_sb[:, c * CHUNK : (c + 1) * CHUNK],
+                ALU.mult,
+            )
+
+        clear_page("lo_a1")
+        finish(0, 0, banks[0], None)
+
+        q_b = []
+        for a in range(PASSES):
+            hi = sb(f"hi_b{a}", [P, CHUNK * PACK], BF16)
+            for h in range(2):
+                weave("scalar", hi[:, h * HALF * PACK : (h + 1) * HALF * PACK], raw_b[a][:, :, h * HALF : (h + 1) * HALF])
+            q_b.append(quantise(f"q_b{a}", hi, E5M2))
+        clear_page("hi_b0")
+        for t in range(PACK):
+            decode(banks[4 + t], t, q_b[0])
+        finish(0, 1, banks[1], "hi_b1")
+        dec_banks = [[4, 5, 6, 7], [0, 1, 4, 5]]
+        r_b = []
+        for a in range(PASSES):
+            planes = sb(f"pl_b{a}", [P, PACK, CHUNK], BF16)
+            for t in range(PACK):
+                if a == 1:
+                    decode(banks[dec_banks[a][t]], t, q_b[1])
+                nc.vector.tensor_tensor(planes[:, t, :], raw_b[a][:, t, :], banks[dec_banks[a][t]][:], ALU.subtract)
+            lo = sb(f"lo_b{a}", [P, CHUNK * PACK], BF16)
+            weave("scalar", lo[:], planes[:])
+            r_b.append(lo)
+        clear_page("raw_b0")
+        finish(0, 2, banks[2], "raw_b1")
+        r_b = [quantise(f"r_b{a}", r_b[a], E4M3) for a in range(PASSES)]
+        finish(0, 3, banks[3], "lo_b1")
+        ops_b = [(a, q_b[a], E5M2) for a in range(PASSES)] + [(a, r_b[a], E4M3) for a in range(PASSES)]
+        main_banks = [6, 7, 0, 1]
+        for r in range(ROW_TILES):
+            product(banks[main_banks[r]], r, ops_b)
+        for r in range(ROW_TILES):
+            finish(1, r, banks[main_banks[r]], None)
+            nc.sync.dma_start(out=out[r * P : (r + 1) * P, :], in_=pages[r][:])

@@ -1,7 +1,6 @@
 from contextlib import ExitStack
 
 import concourse.mybir as mybir
-from concourse.masks import make_identity
 
 K, N, T, J = 1024, 512, 2048, 1024
 FLOPS = 3221225472
@@ -51,101 +50,88 @@ def tile_list_embg_tgq8_res_kernel(tc, dy, w_words, w_scales, res, wgo, offs, ou
             else:
                 nc.vector.tensor_copy(out=d, in_=s)
 
+        ones = sb("ones", [P, P], F32)
+        nc.vector.memset(ones[:], 1.0)
+        column = sb("column", [P, P], F32)
+        nc.vector.tensor_tensor_scan(column[:], ones[:], ones[:], -1.0, ALU.mult, ALU.add)
+        in_quadrant = sb("in_quadrant", [P, 32], F32)
+        nc.vector.transpose(in_quadrant[:], column[:, 0:32])
+        quadrant = sb("quadrant", [P, 1], F32)
+        for q in range(4):
+            nc.vector.memset(quadrant[32 * q : 32 * q + 32, :], float(32 * q))
+        eye_in = sb("eye_in", [P, PACK * K_PASS], BF16)
+        nc.gpsimd.memset(eye_in[:].bitcast(I32), 0)
+        for t in range(PACK):
+            nc.vector.tensor_scalar(
+                eye_in[:, t * K_PASS + t : (t + 1) * K_PASS : PACK],
+                column[:],
+                quadrant[:],
+                in_quadrant[:, 0:1],
+                ALU.subtract,
+                ALU.is_equal,
+            )
+        eye_codes = sb("eye_codes", [P, K_PASS], U32)
+        eye_sc = sb("eye_sc", [P, K_PASS], U8)
+        nc.vector.quantize_mx(out=eye_codes[:].bitcast(E4M3), scales=eye_sc[:], in_=eye_in[:])
+
+        w_sc = sb("w_sc", [P, PASSES, N], U8)
+        nc.gpsimd.memset(w_sc[:].rearrange("p a n -> p (a n)").bitcast(I32), 0)
+        for q in range(4):
+            nc.scalar.dma_start(
+                out=w_sc[32 * q : 32 * q + 4, :, :].bitcast(I32),
+                in_=w_scales[:, 4 * q : 4 * q + 4, :].rearrange("a r n -> r a n").bitcast(I32),
+            )
         raw_a = [[load_dy(f"raw_a{a}{h}", a, h * HALF, HALF) for h in range(2)] for a in range(PASSES)]
         w_codes = sb("w_codes", [P, PASSES, N], U32)
         nc.sync.dma_start(
             out=w_codes[:].bitcast(I32),
             in_=w_words.rearrange("a p n i -> p a (n i)").bitcast(I32),
         )
-        w_sc = sb("w_sc", [P, PASSES, N], U8)
-        nc.vector.memset(w_sc[:].rearrange("p a n -> p (a n)").bitcast(I32), 0)
-        for q in range(4):
-            nc.sync.dma_start(
-                out=w_sc[32 * q : 32 * q + 4, :, :].bitcast(I32),
-                in_=w_scales[:, 4 * q : 4 * q + 4, :].rearrange("a r n -> r a n").bitcast(I32),
-            )
-        raw_b = [load_dy(f"raw_b{a}", a, CHUNK, CHUNK) for a in range(PASSES)]
+        res_sb = []
+
+        def load_res(r):
+            res_sb.append(sb(f"res{r}", [P, J], F32))
+            nc.sync.dma_start(out=res_sb[r][:], in_=res[r * P : (r + 1) * P, :])
+
+        raw_b = [load_dy("raw_b0", 0, CHUNK, CHUNK)]
         offsets = keep.tile([P, J // 16], U16, name="offsets")
         nc.sync.dma_start(offsets[:], offs)
+        load_res(0)
         wgo_sb = sb("wgo_sb", [P, J], F32)
-        res_sb = {}
-
-        def load_res(c, r):
-            res_sb[c, r] = sb(f"res{c}{r}", [P, CHUNK], F32)
-            nc.sync.dma_start(out=res_sb[c, r][:], in_=res[r * P : (r + 1) * P, c * CHUNK : (c + 1) * CHUNK])
-
-        load_res(0, 0)
         nc.sync.dma_start(out=wgo_sb[:], in_=wgo)
-        for c in range(2):
-            for r in range(ROW_TILES):
-                if (c, r) != (0, 0):
-                    load_res(c, r)
+        raw_b.append(load_dy("raw_b1", 1, CHUNK, CHUNK))
+        for r in range(1, ROW_TILES):
+            load_res(r)
 
-        eye = sb("eye", [P, P], BF16)
-        make_identity(nc, eye[:])
-        eye_in = sb("eye_in", [P, PACK * K_PASS], BF16)
-        nc.vector.memset(eye_in[:].bitcast(I32), 0)
-        for t in range(PACK):
-            nc.vector.tensor_copy(out=eye_in[:, t * K_PASS + t : (t + 1) * K_PASS : PACK], in_=eye[:])
-        eye_codes = sb("eye_codes", [P, K_PASS], U32)
-        eye_sc = sb("eye_sc", [P, K_PASS], U8)
-        nc.vector.quantize_mx(out=eye_codes[:].bitcast(E4M3), scales=eye_sc[:], in_=eye_in[:])
+        def operand(name, tag=None):
+            return sb(name + "_codes", [P, CHUNK], U32, tag=tag), sb(name + "_sc", [P, CHUNK], U8)
 
-        def quantise(name, src, fmt):
-            codes = sb(name + "_codes", [P, CHUNK], U32)
-            scales = sb(name + "_sc", [P, CHUNK], U8)
-            nc.vector.quantize_mx(out=codes[:].bitcast(fmt), scales=scales[:], in_=src[:])
-            return codes, scales
+        def quantise(q, src, fmt, j0=0, j1=CHUNK):
+            nc.vector.quantize_mx(out=q[0][:, j0:j1].bitcast(fmt), scales=q[1][:, j0:j1], in_=src[:, j0 * PACK : j1 * PACK])
 
-        def decode(bank, t, q):
+        def decode(bank, t, q, j0=0):
             cols = slice(t * P, (t + 1) * P)
             nc.tensor.matmul_mx(
                 out=bank[:],
                 lhsT=eye_codes[:, cols].bitcast(E4M3),
                 lhsT_scale=eye_sc[:, cols],
-                rhs=q[0][:].bitcast(E5M2),
-                rhs_scale=q[1][:],
+                rhs=q[0][:, j0 : j0 + CHUNK].bitcast(E5M2),
+                rhs_scale=q[1][:, j0 : j0 + CHUNK],
                 start=True,
                 stop=True,
             )
 
-        def product(bank, r, operands):
+        def product(bank, r, a, q, fmt, start=False, stop=False, j0=0, j1=CHUNK, base=0):
             cols = slice(r * P, (r + 1) * P)
-            for i, (a, q, fmt) in enumerate(operands):
-                nc.tensor.matmul_mx(
-                    out=bank[:],
-                    lhsT=w_codes[:, a, cols].bitcast(E4M3),
-                    lhsT_scale=w_sc[:, a, cols],
-                    rhs=q[0][:].bitcast(fmt),
-                    rhs_scale=q[1][:],
-                    start=(i == 0),
-                    stop=(i == len(operands) - 1),
-                )
-
-        q_a = []
-        for a in range(PASSES):
-            hi = sb(f"hi_a{a}", [P, CHUNK * PACK], BF16)
-            weave("scalar", hi[:, : HALF * PACK], raw_a[a][0][:])
-            weave("vector", hi[:, HALF * PACK :], raw_a[a][1][:])
-            q_a.append(quantise(f"q_a{a}", hi, E5M2))
-            for t in range(PACK):
-                decode(banks[4 * a + t], t, q_a[a])
-        r_a = []
-        for a in range(PASSES):
-            lo = sb(f"lo_a{a}", [P, CHUNK * PACK], BF16)
-            for h in range(2):
-                planes = sb(f"pl_a{a}{h}", [P, PACK, HALF], BF16)
-                for t in range(PACK):
-                    nc.vector.tensor_tensor(
-                        planes[:, t, :], raw_a[a][h][:, t, :], banks[4 * a + t][:, h * HALF : (h + 1) * HALF], ALU.subtract
-                    )
-                last = (a, h) == (PASSES - 1, 1)
-                weave("vector" if last else "scalar", lo[:, h * HALF * PACK : (h + 1) * HALF * PACK], planes[:])
-            r_a.append(lo)
-        r_a = [quantise(f"r_a{a}", r_a[a], E4M3) for a in range(PASSES)]
-        ops_a = [(a, q_a[a], E5M2) for a in range(PASSES)] + [(a, r_a[a], E4M3) for a in range(PASSES)]
-        for r in range(ROW_TILES):
-            product(banks[r], r, ops_a)
+            nc.tensor.matmul_mx(
+                out=bank[:, j0:j1],
+                lhsT=w_codes[:, a, cols].bitcast(E4M3),
+                lhsT_scale=w_sc[:, a, cols],
+                rhs=q[0][:, base + j0 : base + j1].bitcast(fmt),
+                rhs_scale=q[1][:, base + j0 : base + j1],
+                start=start,
+                stop=stop,
+            )
 
         pages = []
 
@@ -154,50 +140,106 @@ def tile_list_embg_tgq8_res_kernel(tc, dy, w_words, w_scales, res, wgo, offs, ou
             nc.gpsimd.memset(page[:], 0.0)
             pages.append(page)
 
-        clear_page("hi_a1")
-
         def finish(c, r, bank, tag):
+            cols = slice(c * CHUNK, (c + 1) * CHUNK)
             total = sb(f"total{c}{r}", [P, CHUNK], F32, tag=tag)
-            nc.vector.tensor_tensor(total[:], bank[:], res_sb[c, r][:], ALU.add)
+            nc.vector.tensor_tensor(total[:], bank[:], res_sb[r][:, cols], ALU.add)
             nc.vector.tensor_tensor(
                 pages[r][:].indirect(offsets[:, c * CHUNK // 16 : (c + 1) * CHUNK // 16]),
                 total[:],
-                wgo_sb[:, c * CHUNK : (c + 1) * CHUNK],
+                wgo_sb[:, cols],
                 ALU.mult,
             )
 
-        clear_page("lo_a1")
-        finish(0, 0, banks[0], None)
+        def halves(tile, h):
+            return tile[:, h * HALF * PACK : (h + 1) * HALF * PACK]
 
-        q_b = []
-        for a in range(PASSES):
-            hi = sb(f"hi_b{a}", [P, CHUNK * PACK], BF16)
-            for h in range(2):
-                weave("scalar", hi[:, h * HALF * PACK : (h + 1) * HALF * PACK], raw_b[a][:, :, h * HALF : (h + 1) * HALF])
-            q_b.append(quantise(f"q_b{a}", hi, E5M2))
-        clear_page("hi_b0")
+        pieces = [raw_a[a][h] for a in range(PASSES) for h in range(2)]
+        qa = (sb("q_a_codes", [P, 6 * HALF], U32), sb("q_a_sc", [P, 6 * HALF], U8))
+        for j0 in (0, 5 * HALF):
+            nc.gpsimd.memset(qa[0][:, j0 : j0 + HALF], 0)
+            nc.gpsimd.memset(qa[1][:, j0 : j0 + HALF].bitcast(I32), 0)
+        hi_0 = sb("hi_a0", [P, HALF * PACK], BF16, tag="eye_in")
+        hi_12 = sb("hi_a12", [P, CHUNK * PACK], BF16)
+        hi_3 = sb("hi_a3", [P, HALF * PACK], BF16)
+        lo_a = [sb(f"lo_a{a}", [P, CHUNK * PACK], BF16) for a in range(PASSES)]
+        weave("vector", hi_0[:], pieces[0][:])
+        weave("scalar", halves(hi_12, 0), pieces[1][:])
+        weave("scalar", halves(hi_12, 1), pieces[2][:])
+        weave("scalar", hi_3[:], pieces[3][:])
+
+        def quantise_hi(src, first, count):
+            cols = slice((first + 1) * HALF, (first + 1 + count) * HALF)
+            nc.vector.quantize_mx(out=qa[0][:, cols].bitcast(E5M2), scales=qa[1][:, cols], in_=src[:])
+
+        def leftover_a(i, bank0):
+            a, h = divmod(i, 2)
+            side = 1 - h
+            planes = sb(f"pl_a{a}{h}", [P, PACK, HALF], BF16)
+            for t in range(PACK):
+                nc.vector.tensor_tensor(
+                    planes[:, t, :], pieces[i][:, t, :], banks[bank0 + t][:, side * HALF : (side + 1) * HALF], ALU.subtract
+                )
+            weave("scalar", halves(lo_a[a], h), planes[:])
+
+        quantise_hi(hi_0, 0, 1)
         for t in range(PACK):
-            decode(banks[4 + t], t, q_b[0])
-        finish(0, 1, banks[1], "hi_b1")
-        dec_banks = [[4, 5, 6, 7], [0, 1, 4, 5]]
-        r_b = []
+            decode(banks[t], t, qa, 0)
+        leftover_a(0, 0)
+        quantise_hi(hi_12, 1, 2)
+        for t in range(PACK):
+            decode(banks[4 + t], t, qa, 2 * HALF)
+        quantise_hi(hi_3, 3, 1)
+        clear_page("hi_a3")
+        for t in range(PACK):
+            decode(banks[t], t, qa, 4 * HALF)
+        leftover_a(1, 4)
+        clear_page("raw_a01")
+        leftover_a(2, 4)
+        leftover_a(3, 0)
+        r_a = [operand(f"r_a{a}") for a in range(PASSES)]
+        quantise(r_a[0], lo_a[0], E4M3)
+        quantise(r_a[1], lo_a[1], E4M3, 0, HALF)
+        quantise(r_a[1], lo_a[1], E4M3, HALF, CHUNK)
+        for r in range(ROW_TILES):
+            product(banks[4 + r], r, 0, qa, E5M2, start=True, base=HALF)
+            product(banks[4 + r], r, 1, qa, E5M2, base=3 * HALF)
+            product(banks[4 + r], r, 0, r_a[0], E4M3)
+            product(banks[4 + r], r, 1, r_a[1], E4M3, j1=HALF)
+            product(banks[4 + r], r, 1, r_a[1], E4M3, stop=True, j0=HALF)
+        clear_page("lo_a1")
+        finish(0, 0, banks[4], None)
+
+        hi_b = [sb(f"hi_b{a}", [P, CHUNK * PACK], BF16, tag="pl_a11" if a == 0 else "r_a1_codes") for a in range(PASSES)]
+        q_b = [operand(f"q_b{a}") for a in range(PASSES)]
         for a in range(PASSES):
-            planes = sb(f"pl_b{a}", [P, PACK, CHUNK], BF16)
+            weave("scalar", hi_b[a][:], raw_b[a][:])
+        quantise(q_b[0], hi_b[0], E5M2)
+        for t in range(PACK):
+            decode(banks[t], t, q_b[0])
+        finish(0, 1, banks[5], "pl_a11")
+        clear_page("pl_a11")
+        quantise(q_b[1], hi_b[1], E5M2)
+        dec_banks = [[0, 1, 2, 3], [4, 5, 0, 1]]
+        lo_b = []
+        for a in range(PASSES):
+            planes = sb(f"pl_b{a}", [P, PACK, CHUNK], BF16, tag="r_a1_codes" if a == 0 else None)
             for t in range(PACK):
                 if a == 1:
                     decode(banks[dec_banks[a][t]], t, q_b[1])
                 nc.vector.tensor_tensor(planes[:, t, :], raw_b[a][:, t, :], banks[dec_banks[a][t]][:], ALU.subtract)
-            lo = sb(f"lo_b{a}", [P, CHUNK * PACK], BF16)
-            weave("scalar", lo[:], planes[:])
-            r_b.append(lo)
-        clear_page("raw_b0")
-        finish(0, 2, banks[2], "raw_b1")
-        r_b = [quantise(f"r_b{a}", r_b[a], E4M3) for a in range(PASSES)]
-        finish(0, 3, banks[3], "lo_b1")
+            lo_b.append(sb(f"lo_b{a}", [P, CHUNK * PACK], BF16))
+            weave("scalar", lo_b[a][:], planes[:])
+        finish(0, 2, banks[6], "raw_b1")
+        r_b = [operand(f"r_b{a}") for a in range(PASSES)]
+        for a in range(PASSES):
+            quantise(r_b[a], lo_b[a], E4M3)
+        finish(0, 3, banks[7], "lo_b1")
         ops_b = [(a, q_b[a], E5M2) for a in range(PASSES)] + [(a, r_b[a], E4M3) for a in range(PASSES)]
-        main_banks = [6, 7, 0, 1]
+        main_banks = [2, 3, 4, 5]
         for r in range(ROW_TILES):
-            product(banks[main_banks[r]], r, ops_b)
+            for i, (a, q, fmt) in enumerate(ops_b):
+                product(banks[main_banks[r]], r, a, q, fmt, start=(i == 0), stop=(i == len(ops_b) - 1))
         for r in range(ROW_TILES):
             finish(1, r, banks[main_banks[r]], None)
             nc.sync.dma_start(out=out[r * P : (r + 1) * P, :], in_=pages[r][:])

@@ -70,6 +70,8 @@ def tile_list_embg_tgq8_res_kernel(tc, dy, w_words, w_scales, res, wgo, offs, ou
                 ALU.subtract,
                 ALU.is_equal,
             )
+        eye32 = sb("eye32", [P, P], F32)
+        nc.vector.tensor_scalar(eye32[:], column[:], quadrant[:], in_quadrant[:, 0:1], ALU.subtract, ALU.is_equal)
         eye_codes = sb("eye_codes", [P, K_PASS], U32)
         eye_sc = sb("eye_sc", [P, K_PASS], U8)
         nc.vector.quantize_mx(out=eye_codes[:].bitcast(E4M3), scales=eye_sc[:], in_=eye_in[:])
@@ -140,16 +142,37 @@ def tile_list_embg_tgq8_res_kernel(tc, dy, w_words, w_scales, res, wgo, offs, ou
             nc.gpsimd.memset(page[:], 0.0)
             pages.append(page)
 
-        def finish(c, r, bank, tag):
-            cols = slice(c * CHUNK, (c + 1) * CHUNK)
-            total = sb(f"total{c}{r}", [P, CHUNK], F32, tag=tag)
-            nc.vector.tensor_tensor(total[:], bank[:], res_sb[r][:, cols], ALU.add)
+        def scatter(c, r, total):
             nc.vector.tensor_tensor(
                 pages[r][:].indirect(offsets[:, c * CHUNK // 16 : (c + 1) * CHUNK // 16]),
                 total[:],
-                wgo_sb[:, cols],
+                wgo_sb[:, c * CHUNK : (c + 1) * CHUNK],
                 ALU.mult,
             )
+
+        def add_on_vector(c, r, bank):
+            total = sb(f"total{c}{r}", [P, CHUNK], F32)
+            nc.vector.tensor_tensor(total[:], bank[:], res_sb[r][:, c * CHUNK : (c + 1) * CHUNK], ALU.add)
+            return total
+
+        def add_on_tensor(c, r, bank, spare):
+            dx = sb(f"dx{c}{r}", [P, CHUNK], F32)
+            nc.scalar.copy(out=dx[:], in_=bank[:])
+            for b in range(CHUNK // P):
+                cols = slice(b * P, (b + 1) * P)
+                res_cols = slice(c * CHUNK + b * P, c * CHUNK + (b + 1) * P)
+                nc.tensor.matmul(spare[:, cols], lhsT=res_sb[r][:, res_cols], rhs=eye32[:], is_transpose=True, start=True, stop=False)
+                nc.tensor.matmul(spare[:, cols], lhsT=dx[:, cols], rhs=eye32[:], is_transpose=True, start=False, stop=True)
+            turned = sb(f"turned{c}{r}", [P, CHUNK], F32)
+            nc.scalar.copy(out=turned[:], in_=spare[:])
+            for b in range(CHUNK // P):
+                cols = slice(b * P, (b + 1) * P)
+                nc.tensor.transpose(bank[:, cols], turned[:, cols], eye32[:])
+
+        def fetch(c, r, bank, tag=None):
+            total = sb(f"total{c}{r}", [P, CHUNK], F32, tag=tag)
+            nc.scalar.copy(out=total[:], in_=bank[:])
+            return total
 
         def halves(tile, h):
             return tile[:, h * HALF * PACK : (h + 1) * HALF * PACK]
@@ -208,38 +231,52 @@ def tile_list_embg_tgq8_res_kernel(tc, dy, w_words, w_scales, res, wgo, offs, ou
             product(banks[4 + r], r, 1, r_a[1], E4M3, j1=HALF)
             product(banks[4 + r], r, 1, r_a[1], E4M3, stop=True, j0=HALF)
         clear_page("lo_a1")
-        finish(0, 0, banks[4], None)
+        scatter(0, 0, add_on_vector(0, 0, banks[4]))
 
-        hi_b = [sb(f"hi_b{a}", [P, CHUNK * PACK], BF16, tag="pl_a11" if a == 0 else "r_a1_codes") for a in range(PASSES)]
-        q_b = [operand(f"q_b{a}") for a in range(PASSES)]
-        for a in range(PASSES):
-            weave("scalar", hi_b[a][:], raw_b[a][:])
+        hi_b = [sb("hi_b0", [P, CHUNK * PACK], BF16, tag="pl_a11")]
+        weave("scalar", hi_b[0][:], raw_b[0][:])
+        add_on_tensor(0, 1, banks[5], banks[0])
+        total = fetch(0, 1, banks[5], "pl_a10")
+        for r in (2, 3):
+            add_on_tensor(0, r, banks[4 + r], banks[r - 1])
+        q_b = [operand("q_b0", tag="turned01"), operand("q_b1")]
         quantise(q_b[0], hi_b[0], E5M2)
         for t in range(PACK):
             decode(banks[t], t, q_b[0])
-        finish(0, 1, banks[5], "pl_a11")
-        clear_page("pl_a11")
+        scatter(0, 1, total)
+        clear_page("pl_a10")
+        hi_b.append(sb("hi_b1", [P, CHUNK * PACK], BF16, tag="pl_a11"))
+        weave("scalar", hi_b[1][:], raw_b[1][:])
         quantise(q_b[1], hi_b[1], E5M2)
         dec_banks = [[0, 1, 2, 3], [4, 5, 0, 1]]
         lo_b = []
         for a in range(PASSES):
-            planes = sb(f"pl_b{a}", [P, PACK, CHUNK], BF16, tag="r_a1_codes" if a == 0 else None)
+            planes = sb(f"pl_b{a}", [P, PACK, CHUNK], BF16, tag="pl_a11" if a == 0 else None)
             for t in range(PACK):
                 if a == 1:
                     decode(banks[dec_banks[a][t]], t, q_b[1])
                 nc.vector.tensor_tensor(planes[:, t, :], raw_b[a][:, t, :], banks[dec_banks[a][t]][:], ALU.subtract)
+            if a == 0:
+                total = fetch(0, 2, banks[6], "raw_b0")
             lo_b.append(sb(f"lo_b{a}", [P, CHUNK * PACK], BF16))
             weave("scalar", lo_b[a][:], planes[:])
-        finish(0, 2, banks[6], "raw_b1")
+        scatter(0, 2, total)
         r_b = [operand(f"r_b{a}") for a in range(PASSES)]
-        for a in range(PASSES):
-            quantise(r_b[a], lo_b[a], E4M3)
-        finish(0, 3, banks[7], "lo_b1")
+        quantise(r_b[0], lo_b[0], E4M3)
+        total = fetch(0, 3, banks[7], "lo_b0")
+        quantise(r_b[1], lo_b[1], E4M3)
+        scatter(0, 3, total)
         ops_b = [(a, q_b[a], E5M2) for a in range(PASSES)] + [(a, r_b[a], E4M3) for a in range(PASSES)]
         main_banks = [2, 3, 4, 5]
+        spare_banks = [None, 0, 1, 6]
         for r in range(ROW_TILES):
+            bank = banks[main_banks[r]]
             for i, (a, q, fmt) in enumerate(ops_b):
-                product(banks[main_banks[r]], r, a, q, fmt, start=(i == 0), stop=(i == len(ops_b) - 1))
-        for r in range(ROW_TILES):
-            finish(1, r, banks[main_banks[r]], None)
+                product(bank, r, a, q, fmt, start=(i == 0), stop=(i == len(ops_b) - 1))
+            if r == 0:
+                total = add_on_vector(1, r, bank)
+            else:
+                add_on_tensor(1, r, bank, banks[spare_banks[r]])
+                total = fetch(1, r, bank)
+            scatter(1, r, total)
             nc.sync.dma_start(out=out[r * P : (r + 1) * P, :], in_=pages[r][:])

@@ -78,38 +78,46 @@ def tile_list_embg_tgq8_res_kernel(tc, dy, w_words, w_scales, res, wgo, offs, ou
 
         w_sc = sb("w_sc", [P, PASSES, N], U8)
         nc.gpsimd.memset(w_sc[:].rearrange("p a n -> p (a n)").bitcast(I32), 0)
-        for q in range(4):
-            nc.scalar.dma_start(
-                out=w_sc[32 * q : 32 * q + 4, :, :].bitcast(I32),
-                in_=w_scales[:, 4 * q : 4 * q + 4, :].rearrange("a r n -> r a n").bitcast(I32),
-            )
         raw_a = [[load_dy(f"raw_a{a}{h}", a, h * HALF, HALF) for h in range(2)] for a in range(PASSES)]
         w_codes = sb("w_codes", [P, PASSES, N], U32)
         nc.sync.dma_start(
             out=w_codes[:].bitcast(I32),
             in_=w_words.rearrange("a p n i -> p a (n i)").bitcast(I32),
         )
-        res_sb = []
-
-        def load_res(r):
-            res_sb.append(sb(f"res{r}", [P, J], F32))
-            nc.sync.dma_start(out=res_sb[r][:], in_=res[r * P : (r + 1) * P, :])
-
+        for q in range(4):
+            nc.sync.dma_start(
+                out=w_sc[32 * q : 32 * q + 4, :, :].bitcast(I32),
+                in_=w_scales[:, 4 * q : 4 * q + 4, :].rearrange("a r n -> r a n").bitcast(I32),
+            )
         raw_b = [load_dy("raw_b0", 0, CHUNK, CHUNK)]
+        res_sb = {}
+        wgo_sb = []
+
+        def load_res(c, r):
+            res_sb[c, r] = sb(f"res{c}{r}", [P, CHUNK], F32)
+            nc.sync.dma_start(out=res_sb[c, r][:], in_=res[r * P : (r + 1) * P, c * CHUNK : (c + 1) * CHUNK])
+
+        def load_wgo(c):
+            wgo_sb.append(sb(f"wgo{c}", [P, CHUNK], F32))
+            nc.sync.dma_start(out=wgo_sb[c][:], in_=wgo[:, c * CHUNK : (c + 1) * CHUNK])
+
         offsets = keep.tile([P, J // 16], U16, name="offsets")
         nc.sync.dma_start(offsets[:], offs)
-        load_res(0)
-        wgo_sb = sb("wgo_sb", [P, J], F32)
-        nc.sync.dma_start(out=wgo_sb[:], in_=wgo)
+        load_res(0, 0)
+        load_wgo(0)
+        load_res(0, 1)
         raw_b.append(load_dy("raw_b1", 1, CHUNK, CHUNK))
-        for r in range(1, ROW_TILES):
-            load_res(r)
+        for r in range(2, ROW_TILES):
+            load_res(0, r)
+        load_wgo(1)
+        for r in range(ROW_TILES):
+            load_res(1, r)
 
         def operand(name, tag=None):
             return sb(name + "_codes", [P, CHUNK], U32, tag=tag), sb(name + "_sc", [P, CHUNK], U8)
 
         def quantise(q, src, fmt, j0=0, j1=CHUNK):
-            nc.vector.quantize_mx(out=q[0][:, j0:j1].bitcast(fmt), scales=q[1][:, j0:j1], in_=src[:, j0 * PACK : j1 * PACK])
+            nc.vector.quantize_mx(out=q[0][:, j0:j1].bitcast(fmt), scales=q[1][:, j0:j1], in_=src[:])
 
         def decode(bank, t, q, j0=0):
             cols = slice(t * P, (t + 1) * P)
@@ -146,25 +154,27 @@ def tile_list_embg_tgq8_res_kernel(tc, dy, w_words, w_scales, res, wgo, offs, ou
             nc.vector.tensor_tensor(
                 pages[r][:].indirect(offsets[:, c * CHUNK // 16 : (c + 1) * CHUNK // 16]),
                 total[:],
-                wgo_sb[:, c * CHUNK : (c + 1) * CHUNK],
+                wgo_sb[c][:],
                 ALU.mult,
             )
 
         def add_on_vector(c, r, bank):
             total = sb(f"total{c}{r}", [P, CHUNK], F32)
-            nc.vector.tensor_tensor(total[:], bank[:], res_sb[r][:, c * CHUNK : (c + 1) * CHUNK], ALU.add)
+            nc.vector.tensor_tensor(total[:], bank[:], res_sb[c, r][:], ALU.add)
             return total
 
-        def add_on_tensor(c, r, bank, spare):
+        def take_dx(c, r, bank):
             dx = sb(f"dx{c}{r}", [P, CHUNK], F32)
             nc.scalar.copy(out=dx[:], in_=bank[:])
+            return dx
+
+        def add_on_tensor(c, r, dx, bank):
             for b in range(CHUNK // P):
                 cols = slice(b * P, (b + 1) * P)
-                res_cols = slice(c * CHUNK + b * P, c * CHUNK + (b + 1) * P)
-                nc.tensor.matmul(spare[:, cols], lhsT=res_sb[r][:, res_cols], rhs=eye32[:], is_transpose=True, start=True, stop=False)
-                nc.tensor.matmul(spare[:, cols], lhsT=dx[:, cols], rhs=eye32[:], is_transpose=True, start=False, stop=True)
+                nc.tensor.matmul(bank[:, cols], lhsT=res_sb[c, r][:, cols], rhs=eye32[:], is_transpose=True, start=True, stop=False)
+                nc.tensor.matmul(bank[:, cols], lhsT=dx[:, cols], rhs=eye32[:], is_transpose=True, start=False, stop=True)
             turned = sb(f"turned{c}{r}", [P, CHUNK], F32)
-            nc.scalar.copy(out=turned[:], in_=spare[:])
+            nc.scalar.copy(out=turned[:], in_=bank[:])
             for b in range(CHUNK // P):
                 cols = slice(b * P, (b + 1) * P)
                 nc.tensor.transpose(bank[:, cols], turned[:, cols], eye32[:])
@@ -185,7 +195,9 @@ def tile_list_embg_tgq8_res_kernel(tc, dy, w_words, w_scales, res, wgo, offs, ou
         hi_0 = sb("hi_a0", [P, HALF * PACK], BF16, tag="eye_in")
         hi_12 = sb("hi_a12", [P, CHUNK * PACK], BF16)
         hi_3 = sb("hi_a3", [P, HALF * PACK], BF16)
-        lo_a = [sb(f"lo_a{a}", [P, CHUNK * PACK], BF16) for a in range(PASSES)]
+        lo_a0 = sb("lo_a0", [P, CHUNK * PACK], BF16)
+        lo_a1 = [sb(f"lo_a1{h}", [P, HALF * PACK], BF16) for h in range(2)]
+        lo_pieces = [halves(lo_a0, 0), halves(lo_a0, 1), lo_a1[0][:], lo_a1[1][:]]
         weave("vector", hi_0[:], pieces[0][:])
         weave("scalar", halves(hi_12, 0), pieces[1][:])
         weave("scalar", halves(hi_12, 1), pieces[2][:])
@@ -203,7 +215,7 @@ def tile_list_embg_tgq8_res_kernel(tc, dy, w_words, w_scales, res, wgo, offs, ou
                 nc.vector.tensor_tensor(
                     planes[:, t, :], pieces[i][:, t, :], banks[bank0 + t][:, side * HALF : (side + 1) * HALF], ALU.subtract
                 )
-            weave("scalar", halves(lo_a[a], h), planes[:])
+            weave("scalar", lo_pieces[i], planes[:])
 
         quantise_hi(hi_0, 0, 1)
         for t in range(PACK):
@@ -217,49 +229,64 @@ def tile_list_embg_tgq8_res_kernel(tc, dy, w_words, w_scales, res, wgo, offs, ou
         for t in range(PACK):
             decode(banks[t], t, qa, 4 * HALF)
         leftover_a(1, 4)
-        clear_page("raw_a01")
         leftover_a(2, 4)
         leftover_a(3, 0)
         r_a = [operand(f"r_a{a}") for a in range(PASSES)]
-        quantise(r_a[0], lo_a[0], E4M3)
-        quantise(r_a[1], lo_a[1], E4M3, 0, HALF)
-        quantise(r_a[1], lo_a[1], E4M3, HALF, CHUNK)
+        quantise(r_a[0], lo_a0, E4M3)
+        quantise(r_a[1], lo_a1[0], E4M3, 0, HALF)
+        quantise(r_a[1], lo_a1[1], E4M3, HALF, CHUNK)
         for r in range(ROW_TILES):
             product(banks[4 + r], r, 0, qa, E5M2, start=True, base=HALF)
             product(banks[4 + r], r, 1, qa, E5M2, base=3 * HALF)
             product(banks[4 + r], r, 0, r_a[0], E4M3)
             product(banks[4 + r], r, 1, r_a[1], E4M3, j1=HALF)
             product(banks[4 + r], r, 1, r_a[1], E4M3, stop=True, j0=HALF)
-        clear_page("lo_a1")
+        clear_page("lo_a11")
         scatter(0, 0, add_on_vector(0, 0, banks[4]))
 
-        hi_b = [sb("hi_b0", [P, CHUNK * PACK], BF16, tag="pl_a11")]
-        weave("scalar", hi_b[0][:], raw_b[0][:])
-        add_on_tensor(0, 1, banks[5], banks[0])
-        total = fetch(0, 1, banks[5], "pl_a10")
+        hi_b0 = sb("hi_b0", [P, CHUNK * PACK], BF16, tag="pl_a11")
+        weave("scalar", halves(hi_b0, 0), raw_b[0][:, :, 0:HALF])
+        add_on_tensor(0, 1, take_dx(0, 1, banks[5]), banks[5])
+        total = fetch(0, 1, banks[5])
+        weave("scalar", halves(hi_b0, 1), raw_b[0][:, :, HALF:CHUNK])
         for r in (2, 3):
-            add_on_tensor(0, r, banks[4 + r], banks[r - 1])
-        q_b = [operand("q_b0", tag="turned01"), operand("q_b1")]
-        quantise(q_b[0], hi_b[0], E5M2)
+            add_on_tensor(0, r, take_dx(0, r, banks[4 + r]), banks[4 + r])
+        hi_b1 = sb("hi_b1", [P, CHUNK * PACK], BF16, tag="lo_a10")
+        for h in range(2):
+            weave("scalar", halves(hi_b1, h), raw_b[1][:, :, h * HALF : (h + 1) * HALF])
+        dec_banks = [[1, 2, 3, 4], [0, 5, 1, 2]]
+        decoded = []
+
+        def decode_b(a, t):
+            bank = banks[dec_banks[a][t]]
+            decode(bank, t, q_b[a])
+            if t == 0:
+                decoded.append(sb(f"dec_b{a}", [P, CHUNK], F32))
+                nc.scalar.copy(out=decoded[a][:], in_=bank[:])
+
+        q_b = [operand("q_b0", tag="turned01")]
+        quantise(q_b[0], hi_b0, E5M2)
         for t in range(PACK):
-            decode(banks[t], t, q_b[0])
+            decode_b(0, t)
+        clear_page("pl_a11")
         scatter(0, 1, total)
-        clear_page("pl_a10")
-        hi_b.append(sb("hi_b1", [P, CHUNK * PACK], BF16, tag="pl_a11"))
-        weave("scalar", hi_b[1][:], raw_b[1][:])
-        quantise(q_b[1], hi_b[1], E5M2)
-        dec_banks = [[0, 1, 2, 3], [4, 5, 0, 1]]
+        q_b.append(operand("q_b1", tag="total01"))
+        quantise(q_b[1], hi_b1, E5M2)
         lo_b = []
         for a in range(PASSES):
-            planes = sb(f"pl_b{a}", [P, PACK, CHUNK], BF16, tag="pl_a11" if a == 0 else None)
+            planes = sb(f"pl_b{a}", [P, PACK, CHUNK], BF16, tag=["lo_a10", "dec_b0"][a])
             for t in range(PACK):
                 if a == 1:
-                    decode(banks[dec_banks[a][t]], t, q_b[1])
-                nc.vector.tensor_tensor(planes[:, t, :], raw_b[a][:, t, :], banks[dec_banks[a][t]][:], ALU.subtract)
+                    decode_b(a, t)
+                if t == 0:
+                    nc.gpsimd.tensor_tensor(planes[:, t, :], raw_b[a][:, t, :], decoded[a][:], ALU.subtract)
+                else:
+                    nc.vector.tensor_tensor(planes[:, t, :], raw_b[a][:, t, :], banks[dec_banks[a][t]][:], ALU.subtract)
             if a == 0:
                 total = fetch(0, 2, banks[6], "raw_b0")
             lo_b.append(sb(f"lo_b{a}", [P, CHUNK * PACK], BF16))
             weave("scalar", lo_b[a][:], planes[:])
+        clear_page("dec_b1")
         scatter(0, 2, total)
         r_b = [operand(f"r_b{a}") for a in range(PASSES)]
         quantise(r_b[0], lo_b[0], E4M3)
@@ -267,8 +294,7 @@ def tile_list_embg_tgq8_res_kernel(tc, dy, w_words, w_scales, res, wgo, offs, ou
         quantise(r_b[1], lo_b[1], E4M3)
         scatter(0, 3, total)
         ops_b = [(a, q_b[a], E5M2) for a in range(PASSES)] + [(a, r_b[a], E4M3) for a in range(PASSES)]
-        main_banks = [2, 3, 4, 5]
-        spare_banks = [None, 0, 1, 6]
+        main_banks = [3, 4, 0, 5]
         for r in range(ROW_TILES):
             bank = banks[main_banks[r]]
             for i, (a, q, fmt) in enumerate(ops_b):
@@ -276,7 +302,7 @@ def tile_list_embg_tgq8_res_kernel(tc, dy, w_words, w_scales, res, wgo, offs, ou
             if r == 0:
                 total = add_on_vector(1, r, bank)
             else:
-                add_on_tensor(1, r, bank, banks[spare_banks[r]])
+                add_on_tensor(1, r, take_dx(1, r, bank), bank)
                 total = fetch(1, r, bank)
             scatter(1, r, total)
             nc.sync.dma_start(out=out[r * P : (r + 1) * P, :], in_=pages[r][:])

@@ -193,7 +193,8 @@ def tile_list_embg_tgq8_res_kernel(tc, dy, w_words, w_scales, res, wgo, offs, ou
             nc.gpsimd.memset(qa[0][:, j0 : j0 + HALF], 0)
             nc.gpsimd.memset(qa[1][:, j0 : j0 + HALF].bitcast(I32), 0)
         hi_0 = sb("hi_a0", [P, HALF * PACK], BF16, tag="eye_in")
-        hi_12 = sb("hi_a12", [P, CHUNK * PACK], BF16)
+        shared = sb("shared", [P, CHUNK + CHUNK * PACK], BF16)
+        hi_12 = shared[:, CHUNK:]
         hi_3 = sb("hi_a3", [P, HALF * PACK], BF16)
         lo_a0 = sb("lo_a0", [P, CHUNK * PACK], BF16)
         lo_a1 = [sb(f"lo_a1{h}", [P, HALF * PACK], BF16) for h in range(2)]
@@ -205,26 +206,31 @@ def tile_list_embg_tgq8_res_kernel(tc, dy, w_words, w_scales, res, wgo, offs, ou
 
         def quantise_hi(src, first, count):
             cols = slice((first + 1) * HALF, (first + 1 + count) * HALF)
-            nc.vector.quantize_mx(out=qa[0][:, cols].bitcast(E5M2), scales=qa[1][:, cols], in_=src[:])
+            nc.vector.quantize_mx(out=qa[0][:, cols].bitcast(E5M2), scales=qa[1][:, cols], in_=src)
 
-        def leftover_a(i, bank0):
-            a, h = divmod(i, 2)
-            side = 1 - h
-            planes = sb(f"pl_a{a}{h}", [P, PACK, HALF], BF16)
-            for t in range(PACK):
+        def subtract_a(i, bank0, planes, ts):
+            side = 1 - i % 2
+            for t in ts:
                 nc.vector.tensor_tensor(
                     planes[:, t, :], pieces[i][:, t, :], banks[bank0 + t][:, side * HALF : (side + 1) * HALF], ALU.subtract
                 )
+
+        def leftover_a(i, bank0):
+            planes = sb(f"pl_a{i // 2}{i % 2}", [P, PACK, HALF], BF16)
+            subtract_a(i, bank0, planes, range(PACK))
             weave("scalar", lo_pieces[i], planes[:])
 
-        quantise_hi(hi_0, 0, 1)
+        quantise_hi(hi_0[:], 0, 1)
         for t in range(PACK):
             decode(banks[t], t, qa, 0)
-        leftover_a(0, 0)
+        planes_0 = shared[:, 0 : PACK * HALF].rearrange("p (t j) -> p t j", t=PACK)
+        subtract_a(0, 0, planes_0, (0, 1))
         quantise_hi(hi_12, 1, 2)
+        subtract_a(0, 0, planes_0, (2, 3))
+        weave("scalar", lo_pieces[0], planes_0)
         for t in range(PACK):
             decode(banks[4 + t], t, qa, 2 * HALF)
-        quantise_hi(hi_3, 3, 1)
+        quantise_hi(hi_3[:], 3, 1)
         clear_page("hi_a3")
         for t in range(PACK):
             decode(banks[t], t, qa, 4 * HALF)
@@ -274,7 +280,7 @@ def tile_list_embg_tgq8_res_kernel(tc, dy, w_words, w_scales, res, wgo, offs, ou
         quantise(q_b[1], hi_b1, E5M2)
         lo_b = []
         for a in range(PASSES):
-            planes = sb(f"pl_b{a}", [P, PACK, CHUNK], BF16, tag=["lo_a10", "dec_b0"][a])
+            planes = sb(f"pl_b{a}", [P, PACK, CHUNK], BF16, tag=["lo_a10", "pl_b1"][a])
             for t in range(PACK):
                 if a == 1:
                     decode_b(a, t)

@@ -14,6 +14,7 @@ U8 = mybir.dt.uint8
 E4M3 = mybir.dt.float8_e4m3fn_x4
 E5M2 = mybir.dt.float8_e5m2_x4
 ALU = mybir.AluOpType
+COPY = mybir.ActivationFunctionType.Copy
 
 P = 128
 PACK = 4
@@ -30,11 +31,15 @@ def tile_list_embg_tgq8_res_kernel(tc, dy, w_words, w_scales, res, wgo, offs, ou
 
     with ExitStack() as ctx:
         keep = ctx.enter_context(tc.tile_pool(name="keep", bufs=1))
+        laid = ctx.enter_context(tc.tile_pool(name="laid", bufs=1))
         psum = ctx.enter_context(tc.psum_pool(name="psum", bufs=1))
         banks = [psum.tile([P, CHUNK], F32, name=f"bank{b}") for b in range(8)]
 
         def sb(name, shape, dtype, tag=None):
             return keep.tile(shape, dtype, name=name, tag=tag or name, align_bytes=64)
+
+        def sb_at(name, shape, dtype, offset):
+            return laid.tile(shape, dtype, name=name, tag=name, align_bytes=64, offset=offset)
 
         def load_dy(name, a, j0, width):
             raw = sb(name, [P, PACK, width], F32)
@@ -78,7 +83,11 @@ def tile_list_embg_tgq8_res_kernel(tc, dy, w_words, w_scales, res, wgo, offs, ou
 
         w_sc = sb("w_sc", [P, PASSES, N], U8)
         nc.gpsimd.memset(w_sc[:].rearrange("p a n -> p (a n)").bitcast(I32), 0)
-        raw_a = [[load_dy(f"raw_a{a}{h}", a, h * HALF, HALF) for h in range(2)] for a in range(PASSES)]
+        pieces = [load_dy("raw_a00", 0, 0, HALF)]
+        wgo_rows = sb("wgo_rows", [P, P], F32)
+        nc.sync.dma_start(out=wgo_rows[:], in_=wgo[0:16, :].rearrange("r (c j) -> (r c) j", j=P))
+        pieces.extend(load_dy(f"raw_a{a}{h}", a, h * HALF, HALF) for a, h in ((0, 1), (1, 0), (1, 1)))
+        raw_b = [load_dy("raw_b0", 0, CHUNK, CHUNK)]
         w_codes = sb("w_codes", [P, PASSES, N], U32)
         nc.sync.dma_start(
             out=w_codes[:].bitcast(I32),
@@ -89,7 +98,6 @@ def tile_list_embg_tgq8_res_kernel(tc, dy, w_words, w_scales, res, wgo, offs, ou
                 out=w_sc[32 * q : 32 * q + 4, :, :].bitcast(I32),
                 in_=w_scales[:, 4 * q : 4 * q + 4, :].rearrange("a r n -> r a n").bitcast(I32),
             )
-        raw_b = [load_dy("raw_b0", 0, CHUNK, CHUNK)]
         res_sb = {}
         wgo_sb = []
 
@@ -146,7 +154,7 @@ def tile_list_embg_tgq8_res_kernel(tc, dy, w_words, w_scales, res, wgo, offs, ou
         pages = []
 
         def clear_page(tag):
-            page = sb(f"page{len(pages)}", [P, T], F32, tag=tag)
+            page = sb(f"page{len(pages)}", [P, T], F32, tag=tag) if tag else sb_at("page1", [P, T], F32, 0)
             nc.gpsimd.memset(page[:], 0.0)
             pages.append(page)
 
@@ -158,8 +166,11 @@ def tile_list_embg_tgq8_res_kernel(tc, dy, w_words, w_scales, res, wgo, offs, ou
                 ALU.mult,
             )
 
+        def scatter_copy(c, r, total):
+            nc.vector.tensor_copy(pages[r][:].indirect(offsets[:, c * CHUNK // 16 : (c + 1) * CHUNK // 16]), total[:])
+
         def add_on_vector(c, r, bank):
-            total = sb(f"total{c}{r}", [P, CHUNK], F32)
+            total = sb(f"total{c}{r}", [P, CHUNK], F32) if c else sb_at("total00", [P, CHUNK], F32, 8192)
             nc.vector.tensor_tensor(total[:], bank[:], res_sb[c, r][:], ALU.add)
             return total
 
@@ -168,13 +179,19 @@ def tile_list_embg_tgq8_res_kernel(tc, dy, w_words, w_scales, res, wgo, offs, ou
             nc.scalar.copy(out=dx[:], in_=bank[:])
             return dx
 
-        def add_on_tensor(c, r, dx, bank):
+        def add_on_tensor(c, r, dx, bank, weighted=False):
             for b in range(CHUNK // P):
                 cols = slice(b * P, (b + 1) * P)
                 nc.tensor.matmul(bank[:, cols], lhsT=res_sb[c, r][:, cols], rhs=eye32[:], is_transpose=True, start=True, stop=False)
                 nc.tensor.matmul(bank[:, cols], lhsT=dx[:, cols], rhs=eye32[:], is_transpose=True, start=False, stop=True)
             turned = sb(f"turned{c}{r}", [P, CHUNK], F32)
-            nc.scalar.copy(out=turned[:], in_=bank[:])
+            if weighted:
+                for b in range(CHUNK // P):
+                    cols = slice(b * P, (b + 1) * P)
+                    g = c * (CHUNK // P) + b
+                    nc.scalar.activation(turned[:, cols], bank[:, cols], COPY, scale=wgo_col[:, g : g + 1])
+            else:
+                nc.scalar.copy(out=turned[:], in_=bank[:])
             for b in range(CHUNK // P):
                 cols = slice(b * P, (b + 1) * P)
                 nc.tensor.transpose(bank[:, cols], turned[:, cols], eye32[:])
@@ -187,15 +204,16 @@ def tile_list_embg_tgq8_res_kernel(tc, dy, w_words, w_scales, res, wgo, offs, ou
         def halves(tile, h):
             return tile[:, h * HALF * PACK : (h + 1) * HALF * PACK]
 
-        pieces = [raw_a[a][h] for a in range(PASSES) for h in range(2)]
-        qa = (sb("q_a_codes", [P, 6 * HALF], U32), sb("q_a_sc", [P, 6 * HALF], U8))
-        for j0 in (0, 5 * HALF):
-            nc.gpsimd.memset(qa[0][:, j0 : j0 + HALF], 0)
-            nc.gpsimd.memset(qa[1][:, j0 : j0 + HALF].bitcast(I32), 0)
+        nc.tensor.transpose(banks[7][:, 0:P], wgo_rows[:], eye32[:])
+        wgo_col = sb("wgo_col", [P, J // P], F32)
+        nc.scalar.copy(out=wgo_col[:], in_=banks[7][:, 0 : J // P])
+        qa = (sb("q_a_codes", [P, 5 * HALF], U32), sb("q_a_sc", [P, 5 * HALF], U8))
+        nc.gpsimd.memset(qa[0][:, 0:HALF], 0)
+        nc.gpsimd.memset(qa[1][:, 0:HALF].bitcast(I32), 0)
         hi_0 = sb("hi_a0", [P, HALF * PACK], BF16, tag="eye_in")
         shared = sb("shared", [P, CHUNK + CHUNK * PACK], BF16)
         hi_12 = shared[:, CHUNK:]
-        hi_3 = sb("hi_a3", [P, HALF * PACK], BF16)
+        hi_3 = sb_at("hi_a3", [P, HALF * PACK], BF16, 6144)
         lo_a0 = sb("lo_a0", [P, CHUNK * PACK], BF16)
         lo_a1 = [sb(f"lo_a1{h}", [P, HALF * PACK], BF16) for h in range(2)]
         lo_pieces = [halves(lo_a0, 0), halves(lo_a0, 1), lo_a1[0][:], lo_a1[1][:]]
@@ -209,7 +227,7 @@ def tile_list_embg_tgq8_res_kernel(tc, dy, w_words, w_scales, res, wgo, offs, ou
             nc.vector.quantize_mx(out=qa[0][:, cols].bitcast(E5M2), scales=qa[1][:, cols], in_=src)
 
         def subtract_a(i, bank0, planes, ts):
-            side = 1 - i % 2
+            side = (1, 0, 1, 1)[i]
             for t in ts:
                 nc.vector.tensor_tensor(
                     planes[:, t, :], pieces[i][:, t, :], banks[bank0 + t][:, side * HALF : (side + 1) * HALF], ALU.subtract
@@ -221,6 +239,7 @@ def tile_list_embg_tgq8_res_kernel(tc, dy, w_words, w_scales, res, wgo, offs, ou
             weave("scalar", lo_pieces[i], planes[:])
 
         quantise_hi(hi_0[:], 0, 1)
+        clear_page("eye_in")
         for t in range(PACK):
             decode(banks[t], t, qa, 0)
         planes_0 = shared[:, 0 : PACK * HALF].rearrange("p (t j) -> p t j", t=PACK)
@@ -231,9 +250,18 @@ def tile_list_embg_tgq8_res_kernel(tc, dy, w_words, w_scales, res, wgo, offs, ou
         for t in range(PACK):
             decode(banks[4 + t], t, qa, 2 * HALF)
         quantise_hi(hi_3[:], 3, 1)
-        clear_page("hi_a3")
+        hi_b0 = sb_at("hi_b0", [P, CHUNK * PACK], BF16, 6144)
+        for h in range(2):
+            nc.gpsimd.tensor_scalar(
+                halves(hi_b0, h).rearrange("p (j t) -> p j t", t=PACK),
+                raw_b[0][:, :, h * HALF : (h + 1) * HALF].rearrange("p t j -> p j t"),
+                1.0,
+                0.0,
+                ALU.mult,
+                ALU.add,
+            )
         for t in range(PACK):
-            decode(banks[t], t, qa, 4 * HALF)
+            decode(banks[t], t, qa, 3 * HALF)
         leftover_a(1, 4)
         leftover_a(2, 4)
         leftover_a(3, 0)
@@ -241,68 +269,79 @@ def tile_list_embg_tgq8_res_kernel(tc, dy, w_words, w_scales, res, wgo, offs, ou
         quantise(r_a[0], lo_a0, E4M3)
         quantise(r_a[1], lo_a1[0], E4M3, 0, HALF)
         quantise(r_a[1], lo_a1[1], E4M3, HALF, CHUNK)
-        for r in range(ROW_TILES):
-            product(banks[4 + r], r, 0, qa, E5M2, start=True, base=HALF)
-            product(banks[4 + r], r, 1, qa, E5M2, base=3 * HALF)
-            product(banks[4 + r], r, 0, r_a[0], E4M3)
-            product(banks[4 + r], r, 1, r_a[1], E4M3, j1=HALF)
-            product(banks[4 + r], r, 1, r_a[1], E4M3, stop=True, j0=HALF)
-        clear_page("lo_a11")
-        scatter(0, 0, add_on_vector(0, 0, banks[4]))
 
-        hi_b0 = sb("hi_b0", [P, CHUNK * PACK], BF16, tag="pl_a11")
-        weave("scalar", halves(hi_b0, 0), raw_b[0][:, :, 0:HALF])
-        add_on_tensor(0, 1, take_dx(0, 1, banks[5]), banks[5])
-        total = fetch(0, 1, banks[5])
-        weave("scalar", halves(hi_b0, 1), raw_b[0][:, :, HALF:CHUNK])
-        for r in (2, 3):
-            add_on_tensor(0, r, take_dx(0, r, banks[4 + r]), banks[4 + r])
-        hi_b1 = sb("hi_b1", [P, CHUNK * PACK], BF16, tag="lo_a10")
-        for h in range(2):
-            weave("scalar", halves(hi_b1, h), raw_b[1][:, :, h * HALF : (h + 1) * HALF])
-        dec_banks = [[1, 2, 3, 4], [0, 5, 1, 2]]
-        decoded = []
+        def product_a(r, early):
+            passes = [
+                (0, qa, E5M2, 0, CHUNK, HALF),
+                (1, qa, E5M2, 0, CHUNK, 3 * HALF),
+                (0, r_a[0], E4M3, 0, CHUNK, 0),
+                (1, r_a[1], E4M3, 0, HALF, 0),
+                (1, r_a[1], E4M3, HALF, CHUNK, 0),
+            ]
+            if not early:
+                passes.reverse()
+            for i, (a, q, fmt, j0, j1, base) in enumerate(passes):
+                product(banks[4 + r], r, a, q, fmt, start=(i == 0), stop=(i == len(passes) - 1), j0=j0, j1=j1, base=base)
 
-        def decode_b(a, t):
-            bank = banks[dec_banks[a][t]]
-            decode(bank, t, q_b[a])
-            if t == 0:
-                decoded.append(sb(f"dec_b{a}", [P, CHUNK], F32))
-                nc.scalar.copy(out=decoded[a][:], in_=bank[:])
-
-        q_b = [operand("q_b0", tag="turned01")]
+        product_a(0, True)
+        product_a(1, True)
+        q_b = [operand("q_b0", tag="lo_a11")]
         quantise(q_b[0], hi_b0, E5M2)
-        for t in range(PACK):
-            decode_b(0, t)
-        clear_page("pl_a11")
-        scatter(0, 1, total)
+        clear_page(None)
+        total = add_on_vector(0, 0, banks[4])
+        clear_page("res00")
+        scatter(0, 0, total)
+
+        lo_b = [sb(f"lo_b{a}", [P, CHUNK * PACK], BF16) for a in range(PASSES)]
+
+        def take_decoded(a, width):
+            decoded = sb(f"dec_b{a}", [P, PACK, width], F32)
+            for t in range(PACK):
+                decode(banks[t], t, q_b[a])
+                nc.scalar.copy(out=decoded[:, t, :], in_=banks[t][:, 0:width])
+            return decoded
+
+        def leftover_on_gpsimd(a, decoded, width):
+            for h in range(width // P):
+                cols = slice(h * P, (h + 1) * P)
+                nc.gpsimd.tensor_tensor(
+                    lo_b[a][:, h * P * PACK : (h + 1) * P * PACK].rearrange("p (c i t) -> p c t i", i=RUN, t=PACK),
+                    raw_b[a][:, :, cols].rearrange("p t (c i) -> p c t i", i=RUN),
+                    decoded[:, :, cols].rearrange("p t (c i) -> p c t i", i=RUN),
+                    ALU.subtract,
+                )
+
+        add_on_tensor(0, 1, take_dx(0, 1, banks[5]), banks[5], True)
+        total = fetch(0, 1, banks[5])
+        leftover_on_gpsimd(0, take_decoded(0, CHUNK), CHUNK)
+        product_a(2, False)
+        product_a(3, False)
+        scatter_copy(0, 1, total)
+        hi_b1 = sb("hi_b1", [P, CHUNK * PACK], BF16)
+        dx = take_dx(0, 2, banks[6])
+        weave("scalar", halves(hi_b1, 0), raw_b[1][:, :, 0:HALF])
+        add_on_tensor(0, 2, dx, banks[6], True)
+        weave("scalar", halves(hi_b1, 1), raw_b[1][:, :, HALF:CHUNK])
         q_b.append(operand("q_b1", tag="total01"))
         quantise(q_b[1], hi_b1, E5M2)
-        lo_b = []
-        for a in range(PASSES):
-            planes = sb(f"pl_b{a}", [P, PACK, CHUNK], BF16, tag=["lo_a10", "pl_b1"][a])
-            for t in range(PACK):
-                if a == 1:
-                    decode_b(a, t)
-                if t == 0:
-                    nc.gpsimd.tensor_tensor(planes[:, t, :], raw_b[a][:, t, :], decoded[a][:], ALU.subtract)
-                else:
-                    nc.vector.tensor_tensor(planes[:, t, :], raw_b[a][:, t, :], banks[dec_banks[a][t]][:], ALU.subtract)
-            if a == 0:
-                total = fetch(0, 2, banks[6], "raw_b0")
-            lo_b.append(sb(f"lo_b{a}", [P, CHUNK * PACK], BF16))
-            weave("scalar", lo_b[a][:], planes[:])
-        clear_page("dec_b1")
-        scatter(0, 2, total)
-        r_b = [operand(f"r_b{a}") for a in range(PASSES)]
+        total = fetch(0, 2, banks[6])
+        clear_page("dec_b0")
+        leftover_on_gpsimd(1, take_decoded(1, HALF), HALF)
+        scatter_copy(0, 2, total)
+        planes = sb("pl_b1", [P, PACK, HALF], BF16, tag="total02")
+        for t in range(PACK):
+            nc.vector.tensor_tensor(planes[:, t, :], raw_b[1][:, t, HALF:CHUNK], banks[t][:, HALF:CHUNK], ALU.subtract)
+        add_on_tensor(0, 3, take_dx(0, 3, banks[7]), banks[7], True)
+        total = fetch(0, 3, banks[7])
+        weave("scalar", halves(lo_b[1], 1), planes[:])
+        scatter_copy(0, 3, total)
+        r_b = [operand("r_b0", tag="total02")]
         quantise(r_b[0], lo_b[0], E4M3)
-        total = fetch(0, 3, banks[7], "lo_b0")
+        r_b.append(operand("r_b1", tag="total03"))
         quantise(r_b[1], lo_b[1], E4M3)
-        scatter(0, 3, total)
         ops_b = [(a, q_b[a], E5M2) for a in range(PASSES)] + [(a, r_b[a], E4M3) for a in range(PASSES)]
-        main_banks = [3, 4, 0, 5]
         for r in range(ROW_TILES):
-            bank = banks[main_banks[r]]
+            bank = banks[4 + r]
             for i, (a, q, fmt) in enumerate(ops_b):
                 product(bank, r, a, q, fmt, start=(i == 0), stop=(i == len(ops_b) - 1))
             if r == 0:

@@ -113,10 +113,10 @@ def tile_list_embg_tgq8_res_kernel(tc, dy, w_words, w_scales, res, wgo, offs, ou
         nc.sync.dma_start(offsets[:], offs)
         load_res(0, 0)
         load_wgo(0)
-        load_res(0, 1)
         raw_b.append(load_dy("raw_b1", 1, CHUNK, CHUNK))
-        for r in range(2, ROW_TILES):
-            load_res(0, r)
+        load_res(0, 1)
+        load_res(0, 2)
+        load_res(0, 3)
         load_wgo(1)
         for r in range(ROW_TILES):
             load_res(1, r)
@@ -153,8 +153,9 @@ def tile_list_embg_tgq8_res_kernel(tc, dy, w_words, w_scales, res, wgo, offs, ou
 
         pages = []
 
-        def clear_page(tag):
-            page = sb(f"page{len(pages)}", [P, T], F32, tag=tag) if tag else sb_at("page1", [P, T], F32, 0)
+        def clear_page(tag=None, offset=None):
+            name = f"page{len(pages)}"
+            page = sb(name, [P, T], F32, tag=tag) if tag else sb_at(name, [P, T], F32, offset)
             nc.gpsimd.memset(page[:], 0.0)
             pages.append(page)
 
@@ -169,8 +170,9 @@ def tile_list_embg_tgq8_res_kernel(tc, dy, w_words, w_scales, res, wgo, offs, ou
         def scatter_copy(c, r, total):
             nc.vector.tensor_copy(pages[r][:].indirect(offsets[:, c * CHUNK // 16 : (c + 1) * CHUNK // 16]), total[:])
 
-        def add_on_vector(c, r, bank):
-            total = sb(f"total{c}{r}", [P, CHUNK], F32) if c else sb_at("total00", [P, CHUNK], F32, 8192)
+        def add_on_vector(c, r, bank, offset=None):
+            name = f"total{c}{r}"
+            total = sb(name, [P, CHUNK], F32) if offset is None else sb_at(name, [P, CHUNK], F32, offset)
             nc.vector.tensor_tensor(total[:], bank[:], res_sb[c, r][:], ALU.add)
             return total
 
@@ -179,12 +181,14 @@ def tile_list_embg_tgq8_res_kernel(tc, dy, w_words, w_scales, res, wgo, offs, ou
             nc.scalar.copy(out=dx[:], in_=bank[:])
             return dx
 
-        def add_on_tensor(c, r, dx, bank, weighted=False):
+        def add_on_tensor(c, r, dx, bank, weighted=False, back=None, offset=None):
+            back = bank if back is None else back
             for b in range(CHUNK // P):
                 cols = slice(b * P, (b + 1) * P)
                 nc.tensor.matmul(bank[:, cols], lhsT=res_sb[c, r][:, cols], rhs=eye32[:], is_transpose=True, start=True, stop=False)
                 nc.tensor.matmul(bank[:, cols], lhsT=dx[:, cols], rhs=eye32[:], is_transpose=True, start=False, stop=True)
-            turned = sb(f"turned{c}{r}", [P, CHUNK], F32)
+            name = f"turned{c}{r}"
+            turned = sb(name, [P, CHUNK], F32) if offset is None else sb_at(name, [P, CHUNK], F32, offset)
             if weighted:
                 for b in range(CHUNK // P):
                     cols = slice(b * P, (b + 1) * P)
@@ -194,7 +198,7 @@ def tile_list_embg_tgq8_res_kernel(tc, dy, w_words, w_scales, res, wgo, offs, ou
                 nc.scalar.copy(out=turned[:], in_=bank[:])
             for b in range(CHUNK // P):
                 cols = slice(b * P, (b + 1) * P)
-                nc.tensor.transpose(bank[:, cols], turned[:, cols], eye32[:])
+                nc.tensor.transpose(back[:, cols], turned[:, cols], eye32[:])
 
         def fetch(c, r, bank, tag=None):
             total = sb(f"total{c}{r}", [P, CHUNK], F32, tag=tag)
@@ -234,7 +238,8 @@ def tile_list_embg_tgq8_res_kernel(tc, dy, w_words, w_scales, res, wgo, offs, ou
                 )
 
         def leftover_a(i, bank0):
-            planes = sb(f"pl_a{i // 2}{i % 2}", [P, PACK, HALF], BF16)
+            name = f"pl_a{i // 2}{i % 2}"
+            planes = sb(name, [P, PACK, HALF], BF16) if i < 3 else sb_at(name, [P, PACK, HALF], BF16, 16384)
             subtract_a(i, bank0, planes, range(PACK))
             weave("scalar", lo_pieces[i], planes[:])
 
@@ -287,19 +292,15 @@ def tile_list_embg_tgq8_res_kernel(tc, dy, w_words, w_scales, res, wgo, offs, ou
         product_a(1, True)
         q_b = [operand("q_b0", tag="lo_a11")]
         quantise(q_b[0], hi_b0, E5M2)
-        clear_page(None)
-        total = add_on_vector(0, 0, banks[4])
+        clear_page(offset=0)
+        total = add_on_vector(0, 0, banks[4], 8192)
         clear_page("res00")
         scatter(0, 0, total)
 
-        lo_b = [sb(f"lo_b{a}", [P, CHUNK * PACK], BF16) for a in range(PASSES)]
-
-        def take_decoded(a, width):
-            decoded = sb(f"dec_b{a}", [P, PACK, width], F32)
+        def take_decoded(a, decoded, width):
             for t in range(PACK):
                 decode(banks[t], t, q_b[a])
                 nc.scalar.copy(out=decoded[:, t, :], in_=banks[t][:, 0:width])
-            return decoded
 
         def leftover_on_gpsimd(a, decoded, width):
             for h in range(width // P):
@@ -311,37 +312,40 @@ def tile_list_embg_tgq8_res_kernel(tc, dy, w_words, w_scales, res, wgo, offs, ou
                     ALU.subtract,
                 )
 
-        add_on_tensor(0, 1, take_dx(0, 1, banks[5]), banks[5], True)
-        total = fetch(0, 1, banks[5])
-        leftover_on_gpsimd(0, take_decoded(0, CHUNK), CHUNK)
+        dx = take_dx(0, 1, banks[5])
+        hi_b1 = sb_at("hi_b1", [P, CHUNK * PACK], BF16, 16384)
+        for h in range(2):
+            weave("scalar", halves(hi_b1, h), raw_b[1][:, :, h * HALF : (h + 1) * HALF])
+        q_b.append((sb_at("q_b1_codes", [P, CHUNK], U32, 8192), sb("q_b1_sc", [P, CHUNK], U8)))
+        quantise(q_b[1], hi_b1, E5M2)
+        clear_page(offset=18432)
+        add_on_tensor(0, 1, dx, banks[6], True, banks[7], 10240)
+        total = fetch(0, 1, banks[7])
+        decoded = sb_at("dec_b0", [P, PACK, CHUNK], F32, 10240)
+        take_decoded(0, decoded, CHUNK)
+        lo_b = [sb("lo_b0", [P, CHUNK * PACK], BF16)]
+        leftover_on_gpsimd(0, decoded, CHUNK)
         product_a(2, False)
         product_a(3, False)
         scatter_copy(0, 1, total)
-        hi_b1 = sb("hi_b1", [P, CHUNK * PACK], BF16)
-        dx = take_dx(0, 2, banks[6])
-        weave("scalar", halves(hi_b1, 0), raw_b[1][:, :, 0:HALF])
-        add_on_tensor(0, 2, dx, banks[6], True)
-        weave("scalar", halves(hi_b1, 1), raw_b[1][:, :, HALF:CHUNK])
-        q_b.append(operand("q_b1", tag="total01"))
-        quantise(q_b[1], hi_b1, E5M2)
-        total = fetch(0, 2, banks[6])
-        clear_page("dec_b0")
-        leftover_on_gpsimd(1, take_decoded(1, HALF), HALF)
-        scatter_copy(0, 2, total)
-        planes = sb("pl_b1", [P, PACK, HALF], BF16, tag="total02")
+        planes = sb("pl_b1", [P, PACK, CHUNK], BF16, tag="total01")
         for t in range(PACK):
-            nc.vector.tensor_tensor(planes[:, t, :], raw_b[1][:, t, HALF:CHUNK], banks[t][:, HALF:CHUNK], ALU.subtract)
+            decode(banks[t], t, q_b[1])
+            nc.vector.tensor_tensor(planes[:, t, :], raw_b[1][:, t, :], banks[t][:], ALU.subtract)
+        add_on_tensor(0, 2, take_dx(0, 2, banks[6]), banks[6], True, banks[0])
+        total = fetch(0, 2, banks[0])
         add_on_tensor(0, 3, take_dx(0, 3, banks[7]), banks[7], True)
-        total = fetch(0, 3, banks[7])
-        weave("scalar", halves(lo_b[1], 1), planes[:])
-        scatter_copy(0, 3, total)
-        r_b = [operand("r_b0", tag="total02")]
+        lo_b.append(sb("lo_b1", [P, CHUNK * PACK], BF16, tag="turned03"))
+        weave("scalar", lo_b[1][:], planes[:])
+        scatter_copy(0, 2, total)
+        r_b = [operand("r_b0", tag="total02"), operand("r_b1")]
         quantise(r_b[0], lo_b[0], E4M3)
-        r_b.append(operand("r_b1", tag="total03"))
+        total = fetch(0, 3, banks[7], "lo_b0")
         quantise(r_b[1], lo_b[1], E4M3)
+        scatter_copy(0, 3, total)
         ops_b = [(a, q_b[a], E5M2) for a in range(PASSES)] + [(a, r_b[a], E4M3) for a in range(PASSES)]
         for r in range(ROW_TILES):
-            bank = banks[4 + r]
+            bank = banks[(4, 5, 6, 1)[r]]
             for i, (a, q, fmt) in enumerate(ops_b):
                 product(bank, r, a, q, fmt, start=(i == 0), stop=(i == len(ops_b) - 1))
             if r == 0:

@@ -183,10 +183,12 @@ def tile_list_embg_tgq8_res_kernel(tc, dy, w_words, w_scales, res, wgo, offs, ou
 
         def add_on_tensor(c, r, dx, bank, weighted=False, back=None, offset=None):
             back = bank if back is None else back
-            for b in range(CHUNK // P):
+            terms = [(src, b) for src in (res_sb[c, r], dx) for b in range(CHUNK // P)]
+            for i, (src, b) in enumerate(terms):
                 cols = slice(b * P, (b + 1) * P)
-                nc.tensor.matmul(bank[:, cols], lhsT=res_sb[c, r][:, cols], rhs=eye32[:], is_transpose=True, start=True, stop=False)
-                nc.tensor.matmul(bank[:, cols], lhsT=dx[:, cols], rhs=eye32[:], is_transpose=True, start=False, stop=True)
+                nc.tensor.matmul(
+                    bank[:, cols], lhsT=src[:, cols], rhs=eye32[:], is_transpose=True, start=(i == 0), stop=(i == len(terms) - 1)
+                )
             name = f"turned{c}{r}"
             turned = sb(name, [P, CHUNK], F32) if offset is None else sb_at(name, [P, CHUNK], F32, offset)
             if weighted:
@@ -275,7 +277,7 @@ def tile_list_embg_tgq8_res_kernel(tc, dy, w_words, w_scales, res, wgo, offs, ou
         quantise(r_a[1], lo_a1[0], E4M3, 0, HALF)
         quantise(r_a[1], lo_a1[1], E4M3, HALF, CHUNK)
 
-        def product_a(r, early):
+        def product_a(rows, early):
             passes = [
                 (0, qa, E5M2, 0, CHUNK, HALF),
                 (1, qa, E5M2, 0, CHUNK, 3 * HALF),
@@ -286,10 +288,10 @@ def tile_list_embg_tgq8_res_kernel(tc, dy, w_words, w_scales, res, wgo, offs, ou
             if not early:
                 passes.reverse()
             for i, (a, q, fmt, j0, j1, base) in enumerate(passes):
-                product(banks[4 + r], r, a, q, fmt, start=(i == 0), stop=(i == len(passes) - 1), j0=j0, j1=j1, base=base)
+                for r in rows:
+                    product(banks[4 + r], r, a, q, fmt, start=(i == 0), stop=(i == len(passes) - 1), j0=j0, j1=j1, base=base)
 
-        product_a(0, True)
-        product_a(1, True)
+        product_a((0, 1), True)
         q_b = [operand("q_b0", tag="lo_a11")]
         quantise(q_b[0], hi_b0, E5M2)
         clear_page(offset=0)
@@ -319,22 +321,22 @@ def tile_list_embg_tgq8_res_kernel(tc, dy, w_words, w_scales, res, wgo, offs, ou
         q_b.append((sb_at("q_b1_codes", [P, CHUNK], U32, 8192), sb("q_b1_sc", [P, CHUNK], U8)))
         quantise(q_b[1], hi_b1, E5M2)
         clear_page(offset=18432)
-        add_on_tensor(0, 1, dx, banks[6], True, banks[7], 10240)
+        add_on_tensor(0, 1, dx, banks[6], True, banks[7], 26624)
         total = fetch(0, 1, banks[7])
-        decoded = sb_at("dec_b0", [P, PACK, CHUNK], F32, 10240)
+        decoded = sb_at("dec_b0", [P, PACK, CHUNK], F32, 26624)
         take_decoded(0, decoded, CHUNK)
         lo_b = [sb("lo_b0", [P, CHUNK * PACK], BF16)]
         leftover_on_gpsimd(0, decoded, CHUNK)
-        product_a(2, False)
-        product_a(3, False)
+        product_a((2,), False)
+        product_a((3,), False)
         scatter_copy(0, 1, total)
         planes = sb("pl_b1", [P, PACK, CHUNK], BF16, tag="total01")
         for t in range(PACK):
             decode(banks[t], t, q_b[1])
             nc.vector.tensor_tensor(planes[:, t, :], raw_b[1][:, t, :], banks[t][:], ALU.subtract)
-        add_on_tensor(0, 2, take_dx(0, 2, banks[6]), banks[6], True, banks[0])
+        add_on_tensor(0, 2, take_dx(0, 2, banks[6]), banks[5], True, banks[0])
         total = fetch(0, 2, banks[0])
-        add_on_tensor(0, 3, take_dx(0, 3, banks[7]), banks[7], True)
+        add_on_tensor(0, 3, take_dx(0, 3, banks[7]), banks[4], True, banks[7])
         lo_b.append(sb("lo_b1", [P, CHUNK * PACK], BF16, tag="turned03"))
         weave("scalar", lo_b[1][:], planes[:])
         scatter_copy(0, 2, total)
@@ -345,13 +347,13 @@ def tile_list_embg_tgq8_res_kernel(tc, dy, w_words, w_scales, res, wgo, offs, ou
         scatter_copy(0, 3, total)
         ops_b = [(a, q_b[a], E5M2) for a in range(PASSES)] + [(a, r_b[a], E4M3) for a in range(PASSES)]
         for r in range(ROW_TILES):
-            bank = banks[(4, 5, 6, 1)[r]]
+            bank = banks[(1, 2, 3, 6)[r]]
             for i, (a, q, fmt) in enumerate(ops_b):
                 product(bank, r, a, q, fmt, start=(i == 0), stop=(i == len(ops_b) - 1))
             if r == 0:
                 total = add_on_vector(1, r, bank)
             else:
-                add_on_tensor(1, r, take_dx(1, r, bank), bank)
+                add_on_tensor(1, r, take_dx(1, r, bank), banks[(None, 5, 4, 0)[r]], back=bank)
                 total = fetch(1, r, bank)
             scatter(1, r, total)
             nc.sync.dma_start(out=out[r * P : (r + 1) * P, :], in_=pages[r][:])

@@ -22,8 +22,18 @@ K_PASS = P * PACK
 PASSES = K // K_PASS
 CHUNK = 512
 HALF = CHUNK // 2
+BLOCKS = CHUNK // P
 ROW_TILES = N // P
 RUN = 4
+LIST_ROWS = 16
+
+KIB = 1024
+AT_PAGE1 = 0
+AT_HI = 6 * KIB
+AT_TOTAL00 = 8 * KIB
+AT_HI_B1 = 16 * KIB
+AT_PAGE3 = 18 * KIB
+AT_DECODED = 26 * KIB
 
 
 def tile_list_embg_tgq8_res_kernel(tc, dy, w_words, w_scales, res, wgo, offs, out):
@@ -35,10 +45,9 @@ def tile_list_embg_tgq8_res_kernel(tc, dy, w_words, w_scales, res, wgo, offs, ou
         psum = ctx.enter_context(tc.psum_pool(name="psum", bufs=1))
         banks = [psum.tile([P, CHUNK], F32, name=f"bank{b}") for b in range(8)]
 
-        def sb(name, shape, dtype, tag=None):
-            return keep.tile(shape, dtype, name=name, tag=tag or name, align_bytes=64)
-
-        def sb_at(name, shape, dtype, offset):
+        def sb(name, shape, dtype, tag=None, offset=None):
+            if offset is None:
+                return keep.tile(shape, dtype, name=name, tag=tag or name, align_bytes=64)
             return laid.tile(shape, dtype, name=name, tag=name, align_bytes=64, offset=offset)
 
         def load_dy(name, a, j0, width):
@@ -47,13 +56,14 @@ def tile_list_embg_tgq8_res_kernel(tc, dy, w_words, w_scales, res, wgo, offs, ou
             nc.sync.dma_start(out=raw[:], in_=rows.rearrange("(p t) j -> p t j", t=PACK))
             return raw
 
-        def weave(engine, dst, src):
-            d = dst.rearrange("p (c i t) -> p c t i", i=RUN, t=PACK)
-            s = src.rearrange("p t (c i) -> p c t i", i=RUN)
-            if engine == "scalar":
-                nc.scalar.copy(out=d, in_=s)
-            else:
-                nc.vector.tensor_copy(out=d, in_=s)
+        def woven(dst):
+            return dst.rearrange("p (c i t) -> p c t i", i=RUN, t=PACK)
+
+        def by_runs(planes):
+            return planes.rearrange("p t (c i) -> p c t i", i=RUN)
+
+        def halves(tile, h):
+            return tile[:, h * HALF * PACK : (h + 1) * HALF * PACK]
 
         ones = sb("ones", [P, P], F32)
         nc.vector.memset(ones[:], 1.0)
@@ -85,7 +95,7 @@ def tile_list_embg_tgq8_res_kernel(tc, dy, w_words, w_scales, res, wgo, offs, ou
         nc.gpsimd.memset(w_sc[:].rearrange("p a n -> p (a n)").bitcast(I32), 0)
         pieces = [load_dy("raw_a00", 0, 0, HALF)]
         wgo_rows = sb("wgo_rows", [P, P], F32)
-        nc.sync.dma_start(out=wgo_rows[:], in_=wgo[0:16, :].rearrange("r (c j) -> (r c) j", j=P))
+        nc.sync.dma_start(out=wgo_rows[:], in_=wgo[0 : P * P // J, :].rearrange("r (c j) -> (r c) j", j=P))
         pieces.extend(load_dy(f"raw_a{a}{h}", a, h * HALF, HALF) for a, h in ((0, 1), (1, 0), (1, 1)))
         raw_b = [load_dy("raw_b0", 0, CHUNK, CHUNK)]
         w_codes = sb("w_codes", [P, PASSES, N], U32)
@@ -109,23 +119,22 @@ def tile_list_embg_tgq8_res_kernel(tc, dy, w_words, w_scales, res, wgo, offs, ou
             wgo_sb.append(sb(f"wgo{c}", [P, CHUNK], F32))
             nc.sync.dma_start(out=wgo_sb[c][:], in_=wgo[:, c * CHUNK : (c + 1) * CHUNK])
 
-        offsets = keep.tile([P, J // 16], U16, name="offsets")
+        offsets = keep.tile([P, J // LIST_ROWS], U16, name="offsets")
         nc.sync.dma_start(offsets[:], offs)
         load_res(0, 0)
         load_wgo(0)
         raw_b.append(load_dy("raw_b1", 1, CHUNK, CHUNK))
-        load_res(0, 1)
-        load_res(0, 2)
-        load_res(0, 3)
+        for r in range(1, ROW_TILES):
+            load_res(0, r)
         load_wgo(1)
         for r in range(ROW_TILES):
             load_res(1, r)
 
-        def operand(name, tag=None):
-            return sb(name + "_codes", [P, CHUNK], U32, tag=tag), sb(name + "_sc", [P, CHUNK], U8)
+        def operand(name, tag=None, offset=None):
+            return sb(name + "_codes", [P, CHUNK], U32, tag, offset), sb(name + "_sc", [P, CHUNK], U8)
 
         def quantise(q, src, fmt, j0=0, j1=CHUNK):
-            nc.vector.quantize_mx(out=q[0][:, j0:j1].bitcast(fmt), scales=q[1][:, j0:j1], in_=src[:])
+            nc.vector.quantize_mx(out=q[0][:, j0:j1].bitcast(fmt), scales=q[1][:, j0:j1], in_=src)
 
         def decode(bank, t, q, j0=0):
             cols = slice(t * P, (t + 1) * P)
@@ -139,7 +148,7 @@ def tile_list_embg_tgq8_res_kernel(tc, dy, w_words, w_scales, res, wgo, offs, ou
                 stop=True,
             )
 
-        def product(bank, r, a, q, fmt, start=False, stop=False, j0=0, j1=CHUNK, base=0):
+        def product(bank, r, a, q, fmt, start, stop, j0=0, j1=CHUNK, base=0):
             cols = slice(r * P, (r + 1) * P)
             nc.tensor.matmul_mx(
                 out=bank[:, j0:j1],
@@ -154,110 +163,94 @@ def tile_list_embg_tgq8_res_kernel(tc, dy, w_words, w_scales, res, wgo, offs, ou
         pages = []
 
         def clear_page(tag=None, offset=None):
-            name = f"page{len(pages)}"
-            page = sb(name, [P, T], F32, tag=tag) if tag else sb_at(name, [P, T], F32, offset)
+            page = sb(f"page{len(pages)}", [P, T], F32, tag, offset)
             nc.gpsimd.memset(page[:], 0.0)
             pages.append(page)
 
-        def scatter(c, r, total):
-            nc.vector.tensor_tensor(
-                pages[r][:].indirect(offsets[:, c * CHUNK // 16 : (c + 1) * CHUNK // 16]),
-                total[:],
-                wgo_sb[c][:],
-                ALU.mult,
-            )
+        def places(c, r):
+            columns = CHUNK // LIST_ROWS
+            return pages[r][:].indirect(offsets[:, c * columns : (c + 1) * columns])
 
-        def scatter_copy(c, r, total):
-            nc.vector.tensor_copy(pages[r][:].indirect(offsets[:, c * CHUNK // 16 : (c + 1) * CHUNK // 16]), total[:])
+        def scatter_times_wgo(c, r, total):
+            nc.vector.tensor_tensor(places(c, r), total[:], wgo_sb[c][:], ALU.mult)
+
+        def scatter_weighted(c, r, total):
+            nc.vector.tensor_copy(places(c, r), total[:])
 
         def add_on_vector(c, r, bank, offset=None):
-            name = f"total{c}{r}"
-            total = sb(name, [P, CHUNK], F32) if offset is None else sb_at(name, [P, CHUNK], F32, offset)
+            total = sb(f"total{c}{r}", [P, CHUNK], F32, offset=offset)
             nc.vector.tensor_tensor(total[:], bank[:], res_sb[c, r][:], ALU.add)
             return total
 
-        def take_dx(c, r, bank):
-            dx = sb(f"dx{c}{r}", [P, CHUNK], F32)
-            nc.scalar.copy(out=dx[:], in_=bank[:])
-            return dx
+        def to_sbuf(name, bank, tag=None):
+            tile = sb(name, [P, CHUNK], F32, tag)
+            nc.scalar.copy(out=tile[:], in_=bank[:])
+            return tile
 
-        def add_on_tensor(c, r, dx, bank, weighted=False, back=None, offset=None):
-            back = bank if back is None else back
-            terms = [(src, b) for src in (res_sb[c, r], dx) for b in range(CHUNK // P)]
+        def add_on_tensor(c, r, dx, sum_bank, back_bank, offset=None):
+            terms = [(src, b) for src in (res_sb[c, r], dx) for b in range(BLOCKS)]
             for i, (src, b) in enumerate(terms):
                 cols = slice(b * P, (b + 1) * P)
                 nc.tensor.matmul(
-                    bank[:, cols], lhsT=src[:, cols], rhs=eye32[:], is_transpose=True, start=(i == 0), stop=(i == len(terms) - 1)
+                    sum_bank[:, cols],
+                    lhsT=src[:, cols],
+                    rhs=eye32[:],
+                    is_transpose=True,
+                    start=(i == 0),
+                    stop=(i == len(terms) - 1),
                 )
-            name = f"turned{c}{r}"
-            turned = sb(name, [P, CHUNK], F32) if offset is None else sb_at(name, [P, CHUNK], F32, offset)
-            if weighted:
-                for b in range(CHUNK // P):
+            turned = sb(f"turned{c}{r}", [P, CHUNK], F32, offset=offset)
+            if c == 0:
+                for b in range(BLOCKS):
                     cols = slice(b * P, (b + 1) * P)
-                    g = c * (CHUNK // P) + b
-                    nc.scalar.activation(turned[:, cols], bank[:, cols], COPY, scale=wgo_col[:, g : g + 1])
+                    nc.scalar.activation(turned[:, cols], sum_bank[:, cols], COPY, scale=wgo_col[:, b : b + 1])
             else:
-                nc.scalar.copy(out=turned[:], in_=bank[:])
-            for b in range(CHUNK // P):
+                nc.scalar.copy(out=turned[:], in_=sum_bank[:])
+            for b in range(BLOCKS):
                 cols = slice(b * P, (b + 1) * P)
-                nc.tensor.transpose(back[:, cols], turned[:, cols], eye32[:])
-
-        def fetch(c, r, bank, tag=None):
-            total = sb(f"total{c}{r}", [P, CHUNK], F32, tag=tag)
-            nc.scalar.copy(out=total[:], in_=bank[:])
-            return total
-
-        def halves(tile, h):
-            return tile[:, h * HALF * PACK : (h + 1) * HALF * PACK]
+                nc.tensor.transpose(back_bank[:, cols], turned[:, cols], eye32[:])
 
         nc.tensor.transpose(banks[7][:, 0:P], wgo_rows[:], eye32[:])
-        wgo_col = sb("wgo_col", [P, J // P], F32)
-        nc.scalar.copy(out=wgo_col[:], in_=banks[7][:, 0 : J // P])
-        qa = (sb("q_a_codes", [P, 5 * HALF], U32), sb("q_a_sc", [P, 5 * HALF], U8))
-        nc.gpsimd.memset(qa[0][:, 0:HALF], 0)
-        nc.gpsimd.memset(qa[1][:, 0:HALF].bitcast(I32), 0)
-        hi_0 = sb("hi_a0", [P, HALF * PACK], BF16, tag="eye_in")
+        wgo_col = sb("wgo_col", [P, BLOCKS], F32)
+        nc.scalar.copy(out=wgo_col[:], in_=banks[7][:, 0 : BLOCKS])
+        q_a = (sb("q_a_codes", [P, 5 * HALF], U32), sb("q_a_sc", [P, 5 * HALF], U8))
+        nc.gpsimd.memset(q_a[0][:, 0:HALF], 0)
+        nc.gpsimd.memset(q_a[1][:, 0:HALF].bitcast(I32), 0)
+        hi_a0 = sb("hi_a0", [P, HALF * PACK], BF16, tag="eye_in")
         shared = sb("shared", [P, CHUNK + CHUNK * PACK], BF16)
-        hi_12 = shared[:, CHUNK:]
-        hi_3 = sb_at("hi_a3", [P, HALF * PACK], BF16, 6144)
+        hi_a12 = shared[:, CHUNK:]
+        planes_a0 = shared[:, 0 : PACK * HALF].rearrange("p (t j) -> p t j", t=PACK)
+        hi_a3 = sb("hi_a3", [P, HALF * PACK], BF16, offset=AT_HI)
         lo_a0 = sb("lo_a0", [P, CHUNK * PACK], BF16)
         lo_a1 = [sb(f"lo_a1{h}", [P, HALF * PACK], BF16) for h in range(2)]
         lo_pieces = [halves(lo_a0, 0), halves(lo_a0, 1), lo_a1[0][:], lo_a1[1][:]]
-        weave("vector", hi_0[:], pieces[0][:])
-        weave("scalar", halves(hi_12, 0), pieces[1][:])
-        weave("scalar", halves(hi_12, 1), pieces[2][:])
-        weave("scalar", hi_3[:], pieces[3][:])
+        nc.vector.tensor_copy(out=woven(hi_a0[:]), in_=by_runs(pieces[0][:]))
+        nc.scalar.copy(out=woven(halves(hi_a12, 0)), in_=by_runs(pieces[1][:]))
+        nc.scalar.copy(out=woven(halves(hi_a12, 1)), in_=by_runs(pieces[2][:]))
+        nc.scalar.copy(out=woven(hi_a3[:]), in_=by_runs(pieces[3][:]))
 
-        def quantise_hi(src, first, count):
-            cols = slice((first + 1) * HALF, (first + 1 + count) * HALF)
-            nc.vector.quantize_mx(out=qa[0][:, cols].bitcast(E5M2), scales=qa[1][:, cols], in_=src)
-
-        def subtract_a(i, bank0, planes, ts):
-            side = (1, 0, 1, 1)[i]
+        def subtract_piece(i, bank0, side, planes, ts):
             for t in ts:
-                nc.vector.tensor_tensor(
-                    planes[:, t, :], pieces[i][:, t, :], banks[bank0 + t][:, side * HALF : (side + 1) * HALF], ALU.subtract
-                )
+                decoded = banks[bank0 + t][:, side * HALF : (side + 1) * HALF]
+                nc.vector.tensor_tensor(planes[:, t, :], pieces[i][:, t, :], decoded, ALU.subtract)
 
-        def leftover_a(i, bank0):
-            name = f"pl_a{i // 2}{i % 2}"
-            planes = sb(name, [P, PACK, HALF], BF16) if i < 3 else sb_at(name, [P, PACK, HALF], BF16, 16384)
-            subtract_a(i, bank0, planes, range(PACK))
-            weave("scalar", lo_pieces[i], planes[:])
+        def leftover_piece(i, bank0, side, offset=None):
+            planes = sb(f"pl_a{i // 2}{i % 2}", [P, PACK, HALF], BF16, offset=offset)
+            subtract_piece(i, bank0, side, planes, range(PACK))
+            nc.scalar.copy(out=woven(lo_pieces[i]), in_=by_runs(planes[:]))
 
-        quantise_hi(hi_0[:], 0, 1)
+        quantise(q_a, hi_a0[:], E5M2, HALF, 2 * HALF)
         clear_page("eye_in")
         for t in range(PACK):
-            decode(banks[t], t, qa, 0)
-        planes_0 = shared[:, 0 : PACK * HALF].rearrange("p (t j) -> p t j", t=PACK)
-        subtract_a(0, 0, planes_0, (0, 1))
-        quantise_hi(hi_12, 1, 2)
-        subtract_a(0, 0, planes_0, (2, 3))
-        weave("scalar", lo_pieces[0], planes_0)
+            decode(banks[t], t, q_a, 0)
+        subtract_piece(0, 0, 1, planes_a0, (0, 1))
+        quantise(q_a, hi_a12, E5M2, 2 * HALF, 4 * HALF)
+        subtract_piece(0, 0, 1, planes_a0, (2, 3))
+        nc.scalar.copy(out=woven(lo_pieces[0]), in_=by_runs(planes_a0))
         for t in range(PACK):
-            decode(banks[4 + t], t, qa, 2 * HALF)
-        quantise_hi(hi_3[:], 3, 1)
-        hi_b0 = sb_at("hi_b0", [P, CHUNK * PACK], BF16, 6144)
+            decode(banks[4 + t], t, q_a, 2 * HALF)
+        quantise(q_a, hi_a3[:], E5M2, 4 * HALF, 5 * HALF)
+        hi_b0 = sb("hi_b0", [P, CHUNK * PACK], BF16, offset=AT_HI)
         for h in range(2):
             nc.gpsimd.tensor_scalar(
                 halves(hi_b0, h).rearrange("p (j t) -> p j t", t=PACK),
@@ -268,92 +261,88 @@ def tile_list_embg_tgq8_res_kernel(tc, dy, w_words, w_scales, res, wgo, offs, ou
                 ALU.add,
             )
         for t in range(PACK):
-            decode(banks[t], t, qa, 3 * HALF)
-        leftover_a(1, 4)
-        leftover_a(2, 4)
-        leftover_a(3, 0)
+            decode(banks[t], t, q_a, 3 * HALF)
+        leftover_piece(1, 4, 0)
+        leftover_piece(2, 4, 1)
+        leftover_piece(3, 0, 1, AT_HI_B1)
         r_a = [operand(f"r_a{a}") for a in range(PASSES)]
-        quantise(r_a[0], lo_a0, E4M3)
-        quantise(r_a[1], lo_a1[0], E4M3, 0, HALF)
-        quantise(r_a[1], lo_a1[1], E4M3, HALF, CHUNK)
+        quantise(r_a[0], lo_a0[:], E4M3)
+        quantise(r_a[1], lo_a1[0][:], E4M3, 0, HALF)
+        quantise(r_a[1], lo_a1[1][:], E4M3, HALF, CHUNK)
 
-        def product_a(rows, early):
-            passes = [
-                (0, qa, E5M2, 0, CHUNK, HALF),
-                (1, qa, E5M2, 0, CHUNK, 3 * HALF),
-                (0, r_a[0], E4M3, 0, CHUNK, 0),
-                (1, r_a[1], E4M3, 0, HALF, 0),
-                (1, r_a[1], E4M3, HALF, CHUNK, 0),
-            ]
-            if not early:
-                passes.reverse()
+        passes_a = [
+            (0, q_a, E5M2, 0, CHUNK, HALF),
+            (1, q_a, E5M2, 0, CHUNK, 3 * HALF),
+            (0, r_a[0], E4M3, 0, CHUNK, 0),
+            (1, r_a[1], E4M3, 0, HALF, 0),
+            (1, r_a[1], E4M3, HALF, CHUNK, 0),
+        ]
+
+        def product_a(rows, passes):
             for i, (a, q, fmt, j0, j1, base) in enumerate(passes):
                 for r in rows:
-                    product(banks[4 + r], r, a, q, fmt, start=(i == 0), stop=(i == len(passes) - 1), j0=j0, j1=j1, base=base)
+                    product(banks[4 + r], r, a, q, fmt, i == 0, i == len(passes) - 1, j0, j1, base)
 
-        product_a((0, 1), True)
+        product_a((0, 1), passes_a)
         q_b = [operand("q_b0", tag="lo_a11")]
-        quantise(q_b[0], hi_b0, E5M2)
-        clear_page(offset=0)
-        total = add_on_vector(0, 0, banks[4], 8192)
+        quantise(q_b[0], hi_b0[:], E5M2)
+        clear_page(offset=AT_PAGE1)
+        total = add_on_vector(0, 0, banks[4], AT_TOTAL00)
         clear_page("res00")
-        scatter(0, 0, total)
+        scatter_times_wgo(0, 0, total)
 
-        def take_decoded(a, decoded, width):
-            for t in range(PACK):
-                decode(banks[t], t, q_b[a])
-                nc.scalar.copy(out=decoded[:, t, :], in_=banks[t][:, 0:width])
-
-        def leftover_on_gpsimd(a, decoded, width):
-            for h in range(width // P):
-                cols = slice(h * P, (h + 1) * P)
-                nc.gpsimd.tensor_tensor(
-                    lo_b[a][:, h * P * PACK : (h + 1) * P * PACK].rearrange("p (c i t) -> p c t i", i=RUN, t=PACK),
-                    raw_b[a][:, :, cols].rearrange("p t (c i) -> p c t i", i=RUN),
-                    decoded[:, :, cols].rearrange("p t (c i) -> p c t i", i=RUN),
-                    ALU.subtract,
-                )
-
-        dx = take_dx(0, 1, banks[5])
-        hi_b1 = sb_at("hi_b1", [P, CHUNK * PACK], BF16, 16384)
+        dx = to_sbuf("dx01", banks[5])
+        hi_b1 = sb("hi_b1", [P, CHUNK * PACK], BF16, offset=AT_HI_B1)
         for h in range(2):
-            weave("scalar", halves(hi_b1, h), raw_b[1][:, :, h * HALF : (h + 1) * HALF])
-        q_b.append((sb_at("q_b1_codes", [P, CHUNK], U32, 8192), sb("q_b1_sc", [P, CHUNK], U8)))
-        quantise(q_b[1], hi_b1, E5M2)
-        clear_page(offset=18432)
-        add_on_tensor(0, 1, dx, banks[6], True, banks[7], 26624)
-        total = fetch(0, 1, banks[7])
-        decoded = sb_at("dec_b0", [P, PACK, CHUNK], F32, 26624)
-        take_decoded(0, decoded, CHUNK)
-        lo_b = [sb("lo_b0", [P, CHUNK * PACK], BF16)]
-        leftover_on_gpsimd(0, decoded, CHUNK)
-        product_a((2,), False)
-        product_a((3,), False)
-        scatter_copy(0, 1, total)
-        planes = sb("pl_b1", [P, PACK, CHUNK], BF16, tag="total01")
+            nc.scalar.copy(out=woven(halves(hi_b1, h)), in_=by_runs(raw_b[1][:, :, h * HALF : (h + 1) * HALF]))
+        q_b.append(operand("q_b1", offset=AT_TOTAL00))
+        quantise(q_b[1], hi_b1[:], E5M2)
+        clear_page(offset=AT_PAGE3)
+        add_on_tensor(0, 1, dx, banks[6], banks[7], AT_DECODED)
+        total = to_sbuf("total01", banks[7])
+        decoded_b0 = sb("dec_b0", [P, PACK, CHUNK], F32, offset=AT_DECODED)
+        for t in range(PACK):
+            decode(banks[t], t, q_b[0])
+            nc.scalar.copy(out=decoded_b0[:, t, :], in_=banks[t][:, 0:CHUNK])
+        lo_b0 = sb("lo_b0", [P, CHUNK * PACK], BF16)
+        for b in range(BLOCKS):
+            cols = slice(b * P, (b + 1) * P)
+            nc.gpsimd.tensor_tensor(
+                woven(lo_b0[:, b * P * PACK : (b + 1) * P * PACK]),
+                by_runs(raw_b[0][:, :, cols]),
+                by_runs(decoded_b0[:, :, cols]),
+                ALU.subtract,
+            )
+        product_a((2,), passes_a[::-1])
+        product_a((3,), passes_a[::-1])
+        scatter_weighted(0, 1, total)
+        planes_b1 = sb("pl_b1", [P, PACK, CHUNK], BF16, tag="total01")
         for t in range(PACK):
             decode(banks[t], t, q_b[1])
-            nc.vector.tensor_tensor(planes[:, t, :], raw_b[1][:, t, :], banks[t][:], ALU.subtract)
-        add_on_tensor(0, 2, take_dx(0, 2, banks[6]), banks[5], True, banks[0])
-        total = fetch(0, 2, banks[0])
-        add_on_tensor(0, 3, take_dx(0, 3, banks[7]), banks[4], True, banks[7])
-        lo_b.append(sb("lo_b1", [P, CHUNK * PACK], BF16, tag="turned03"))
-        weave("scalar", lo_b[1][:], planes[:])
-        scatter_copy(0, 2, total)
+            nc.vector.tensor_tensor(planes_b1[:, t, :], raw_b[1][:, t, :], banks[t][:], ALU.subtract)
+        add_on_tensor(0, 2, to_sbuf("dx02", banks[6]), banks[5], banks[0])
+        total = to_sbuf("total02", banks[0])
+        add_on_tensor(0, 3, to_sbuf("dx03", banks[7]), banks[4], banks[7])
+        lo_b1 = sb("lo_b1", [P, CHUNK * PACK], BF16, tag="turned03")
+        nc.scalar.copy(out=woven(lo_b1[:]), in_=by_runs(planes_b1[:]))
+        scatter_weighted(0, 2, total)
         r_b = [operand("r_b0", tag="total02"), operand("r_b1")]
-        quantise(r_b[0], lo_b[0], E4M3)
-        total = fetch(0, 3, banks[7], "lo_b0")
-        quantise(r_b[1], lo_b[1], E4M3)
-        scatter_copy(0, 3, total)
-        ops_b = [(a, q_b[a], E5M2) for a in range(PASSES)] + [(a, r_b[a], E4M3) for a in range(PASSES)]
+        quantise(r_b[0], lo_b0[:], E4M3)
+        total = to_sbuf("total03", banks[7], tag="lo_b0")
+        quantise(r_b[1], lo_b1[:], E4M3)
+        scatter_weighted(0, 3, total)
+
+        passes_b = [(a, q_b[a], E5M2) for a in range(PASSES)] + [(a, r_b[a], E4M3) for a in range(PASSES)]
+        product_banks = (1, 2, 3, 6)
+        sum_banks = {1: 5, 2: 4, 3: 0}
         for r in range(ROW_TILES):
-            bank = banks[(1, 2, 3, 6)[r]]
-            for i, (a, q, fmt) in enumerate(ops_b):
-                product(bank, r, a, q, fmt, start=(i == 0), stop=(i == len(ops_b) - 1))
+            bank = banks[product_banks[r]]
+            for i, (a, q, fmt) in enumerate(passes_b):
+                product(bank, r, a, q, fmt, i == 0, i == len(passes_b) - 1)
             if r == 0:
                 total = add_on_vector(1, r, bank)
             else:
-                add_on_tensor(1, r, take_dx(1, r, bank), banks[(None, 5, 4, 0)[r]], back=bank)
-                total = fetch(1, r, bank)
-            scatter(1, r, total)
+                add_on_tensor(1, r, to_sbuf(f"dx1{r}", bank), banks[sum_banks[r]], bank)
+                total = to_sbuf(f"total1{r}", bank)
+            scatter_times_wgo(1, r, total)
             nc.sync.dma_start(out=out[r * P : (r + 1) * P, :], in_=pages[r][:])

@@ -28,11 +28,13 @@ RUN = 4
 LIST_ROWS = 16
 
 KIB = 1024
-AT_PAGE1 = 0
+AT_PAGE2 = 0
 AT_HI = 6 * KIB
 AT_TOTAL00 = 8 * KIB
 AT_HI_B1 = 16 * KIB
-AT_PAGE3 = 18 * KIB
+AT_TOTAL03 = AT_HI_B1
+AT_PLANES_B1 = AT_HI_B1 + 2 * KIB
+AT_LO_B1 = AT_HI_B1 + 3 * KIB
 AT_DECODED = 26 * KIB
 
 
@@ -65,39 +67,41 @@ def tile_list_embg_tgq8_res_kernel(tc, dy, w_words, w_scales, res, wgo, offs, ou
         def halves(tile, h):
             return tile[:, h * HALF * PACK : (h + 1) * HALF * PACK]
 
-        ones = sb("ones", [P, P], F32)
+        w_sc = sb("w_sc", [P, PASSES, N], U8)
+        nc.gpsimd.memset(w_sc[:].rearrange("p a n -> p (a n)").bitcast(I32), 0)
+        ones = sb("ones", [P, P + 1], F32)
         nc.vector.memset(ones[:], 1.0)
         column = sb("column", [P, P], F32)
-        nc.vector.tensor_tensor_scan(column[:], ones[:], ones[:], -1.0, ALU.mult, ALU.add)
+        nc.vector.tensor_tensor_scan(column[:], ones[:, 0:P], ones[:, 0:P], -1.0, ALU.mult, ALU.add)
         in_quadrant = sb("in_quadrant", [P, 32], F32)
         nc.vector.transpose(in_quadrant[:], column[:, 0:32])
         quadrant = sb("quadrant", [P, 1], F32)
         for q in range(4):
-            nc.vector.memset(quadrant[32 * q : 32 * q + 32, :], float(32 * q))
-        eye_in = sb("eye_in", [P, PACK * K_PASS], BF16)
-        nc.gpsimd.memset(eye_in[:].bitcast(I32), 0)
-        for t in range(PACK):
-            nc.vector.tensor_scalar(
-                eye_in[:, t * K_PASS + t : (t + 1) * K_PASS : PACK],
-                column[:],
-                quadrant[:],
-                in_quadrant[:, 0:1],
-                ALU.subtract,
-                ALU.is_equal,
-            )
-        eye32 = sb("eye32", [P, P], F32)
-        nc.vector.tensor_scalar(eye32[:], column[:], quadrant[:], in_quadrant[:, 0:1], ALU.subtract, ALU.is_equal)
+            nc.gpsimd.memset(quadrant[32 * q : 32 * q + 32, :], float(32 * q))
+        eye_rows = sb("eye_in", [P, PACK * (K_PASS + 1) + 2], BF16)
+        nc.vector.memset(eye_rows[:].bitcast(I32), 0)
+        diagonals = eye_rows[:, 0 : PACK * (K_PASS + 1)].rearrange("p (t x) -> p t x", t=PACK)[:, :, 0:K_PASS:PACK]
+        nc.vector.tensor_scalar(
+            diagonals,
+            column[:].unsqueeze(1).to_broadcast([P, PACK, P]),
+            quadrant[:],
+            in_quadrant[:, 0:1],
+            ALU.subtract,
+            ALU.is_equal,
+        )
         eye_codes = sb("eye_codes", [P, K_PASS], U32)
         eye_sc = sb("eye_sc", [P, K_PASS], U8)
-        nc.vector.quantize_mx(out=eye_codes[:].bitcast(E4M3), scales=eye_sc[:], in_=eye_in[:])
+        nc.vector.quantize_mx(
+            out=eye_codes[:].bitcast(E4M3), scales=eye_sc[:], in_=eye_rows[:, 0 : PACK * K_PASS]
+        )
+        eye32 = sb("eye32", [P, P], F32)
+        nc.scalar.copy(out=eye32[:], in_=diagonals[:, 0, :])
 
-        w_sc = sb("w_sc", [P, PASSES, N], U8)
-        nc.gpsimd.memset(w_sc[:].rearrange("p a n -> p (a n)").bitcast(I32), 0)
         pieces = [load_dy("raw_a00", 0, 0, HALF)]
         wgo_rows = sb("wgo_rows", [P, P], F32)
         nc.sync.dma_start(out=wgo_rows[:], in_=wgo[0 : P * P // J, :].rearrange("r (c j) -> (r c) j", j=P))
         pieces.extend(load_dy(f"raw_a{a}{h}", a, h * HALF, HALF) for a, h in ((0, 1), (1, 0), (1, 1)))
-        raw_b = [load_dy("raw_b0", 0, CHUNK, CHUNK)]
+        raw_b = [[load_dy(f"raw_b0{a}", a, CHUNK, HALF) for a in range(PASSES)]]
         w_codes = sb("w_codes", [P, PASSES, N], U32)
         nc.sync.dma_start(
             out=w_codes[:].bitcast(I32),
@@ -123,12 +127,15 @@ def tile_list_embg_tgq8_res_kernel(tc, dy, w_words, w_scales, res, wgo, offs, ou
         nc.sync.dma_start(offsets[:], offs)
         load_res(0, 0)
         load_wgo(0)
-        raw_b.append(load_dy("raw_b1", 1, CHUNK, CHUNK))
+        raw_b.append([load_dy(f"raw_b1{a}", a, CHUNK + HALF, HALF) for a in range(PASSES)])
         for r in range(1, ROW_TILES):
             load_res(0, r)
-        load_wgo(1)
-        for r in range(ROW_TILES):
-            load_res(1, r)
+        res_b = {}
+        for h in range(2):
+            for pair in range(2):
+                res_b[h, pair] = sb(f"res_b{h}{pair}", [P, 2, HALF], F32)
+                rows = res[2 * pair * P : 2 * (pair + 1) * P, CHUNK + h * HALF : CHUNK + (h + 1) * HALF]
+                nc.sync.dma_start(out=res_b[h, pair][:], in_=rows.rearrange("(i p) j -> p i j", p=P))
 
         def operand(name, tag=None, offset=None):
             return sb(name + "_codes", [P, CHUNK], U32, tag, offset), sb(name + "_sc", [P, CHUNK], U8)
@@ -182,8 +189,8 @@ def tile_list_embg_tgq8_res_kernel(tc, dy, w_words, w_scales, res, wgo, offs, ou
             nc.vector.tensor_tensor(total[:], bank[:], res_sb[c, r][:], ALU.add)
             return total
 
-        def to_sbuf(name, bank, tag=None):
-            tile = sb(name, [P, CHUNK], F32, tag)
+        def to_sbuf(name, bank, tag=None, offset=None):
+            tile = sb(name, [P, CHUNK], F32, tag, offset)
             nc.scalar.copy(out=tile[:], in_=bank[:])
             return tile
 
@@ -211,8 +218,9 @@ def tile_list_embg_tgq8_res_kernel(tc, dy, w_words, w_scales, res, wgo, offs, ou
                 nc.tensor.transpose(back_bank[:, cols], turned[:, cols], eye32[:])
 
         nc.tensor.transpose(banks[7][:, 0:P], wgo_rows[:], eye32[:])
-        wgo_col = sb("wgo_col", [P, BLOCKS], F32)
-        nc.scalar.copy(out=wgo_col[:], in_=banks[7][:, 0 : BLOCKS])
+        wgo_col = sb("wgo_col", [P, J // P], F32)
+        nc.scalar.copy(out=wgo_col[:], in_=banks[7][:, 0 : J // P])
+        clear_page()
         q_a = (sb("q_a_codes", [P, 5 * HALF], U32), sb("q_a_sc", [P, 5 * HALF], U8))
         nc.gpsimd.memset(q_a[0][:, 0:HALF], 0)
         nc.gpsimd.memset(q_a[1][:, 0:HALF].bitcast(I32), 0)
@@ -254,7 +262,7 @@ def tile_list_embg_tgq8_res_kernel(tc, dy, w_words, w_scales, res, wgo, offs, ou
         for h in range(2):
             nc.gpsimd.tensor_scalar(
                 halves(hi_b0, h).rearrange("p (j t) -> p j t", t=PACK),
-                raw_b[0][:, :, h * HALF : (h + 1) * HALF].rearrange("p t j -> p j t"),
+                raw_b[0][h][:].rearrange("p t j -> p j t"),
                 1.0,
                 0.0,
                 ALU.mult,
@@ -286,63 +294,155 @@ def tile_list_embg_tgq8_res_kernel(tc, dy, w_words, w_scales, res, wgo, offs, ou
         product_a((0, 1), passes_a)
         q_b = [operand("q_b0", tag="lo_a11")]
         quantise(q_b[0], hi_b0[:], E5M2)
-        clear_page(offset=AT_PAGE1)
+        clear_page(offset=AT_PAGE2)
         total = add_on_vector(0, 0, banks[4], AT_TOTAL00)
         clear_page("res00")
         scatter_times_wgo(0, 0, total)
 
+        def copy_decoded(tile, pieces_b):
+            for a, j0, j1 in pieces_b:
+                for t in range(PACK):
+                    nc.scalar.copy(out=tile[:, a, t, j0:j1], in_=banks[t][:, a * HALF + j0 : a * HALF + j1])
+
+        def woven_block(lo, a, b):
+            return woven(lo[:, (a * HALF + b * P) * PACK : (a * HALF + (b + 1) * P) * PACK])
+
+        def subtract_on_gpsimd(h, lo, decoded, blocks):
+            for a, b in blocks:
+                cols = slice(b * P, (b + 1) * P)
+                nc.gpsimd.tensor_tensor(
+                    woven_block(lo, a, b),
+                    by_runs(raw_b[h][a][:, :, cols]),
+                    by_runs(decoded[:, a, :, cols]),
+                    ALU.subtract,
+                )
+
+        def product_b(into, q, fmt, first):
+            for b in range(2):
+                for a in range(PASSES):
+                    cols = slice(a * HALF + b * P, a * HALF + (b + 1) * P)
+                    nc.tensor.matmul_mx(
+                        out=into[b][:],
+                        lhsT=q[0][:, cols].bitcast(fmt),
+                        lhsT_scale=q[1][:, cols],
+                        rhs=w_codes[:, a, :].bitcast(E4M3),
+                        rhs_scale=w_sc[:, a, :],
+                        start=first and a == 0,
+                        stop=not first and a == PASSES - 1,
+                    )
+
+        def weighted(name, h, b, src):
+            tile = sb(name, [P, 2 * P], F32)
+            at = BLOCKS + 2 * h + b
+            nc.scalar.activation(tile[:], src, COPY, scale=wgo_col[:, at : at + 1])
+            return tile
+
+        def turn_back(bank, terms, start, stop):
+            steps = [(i, b) for i in range(2) for b in range(2)]
+            for n, (i, b) in enumerate(steps):
+                at = i * HALF + b * P
+                nc.tensor.matmul(
+                    bank[:, at : at + P],
+                    lhsT=terms[b][:, i * P : (i + 1) * P],
+                    rhs=eye32[:],
+                    is_transpose=True,
+                    start=start and n == 0,
+                    stop=stop and n == len(steps) - 1,
+                )
+
+        def turn_res(h, pair, bank):
+            for b in range(2):
+                for i in range(2):
+                    at = (2 * b + i) * P
+                    nc.tensor.transpose(bank[:, at : at + P], res_b[h, pair][:, i, b * P : (b + 1) * P], eye32[:])
+            turned = [
+                weighted(f"turned_res{h}{pair}{b}", h, b, bank[:, 2 * b * P : 2 * (b + 1) * P]) for b in range(2)
+            ]
+            turn_back(bank, turned, True, False)
+
+        def turn_dx(h, pair, bank, sources):
+            cols = slice(2 * pair * P, 2 * (pair + 1) * P)
+            dx_turned = [weighted(f"dx_b{h}{pair}{b}", h, b, sources[b][:, cols]) for b in range(2)]
+            turn_back(bank, dx_turned, False, True)
+
+        totals = {}
+
+        def fetch(h, r, bank, tag=None, offset=None):
+            totals[h, r] = sb(f"total_b{h}{r}", [P, HALF], F32, tag, offset)
+            nc.scalar.copy(out=totals[h, r][:], in_=bank[:, (r % 2) * HALF : (r % 2 + 1) * HALF])
+
+        def scatter_b(h, r):
+            columns = HALF // LIST_ROWS
+            first = (CHUNK + h * HALF) // LIST_ROWS
+            nc.vector.tensor_copy(pages[r][:].indirect(offsets[:, first : first + columns]), totals[h, r][:])
+            if h == 1:
+                nc.sync.dma_start(out=out[r * P : (r + 1) * P, :], in_=pages[r][:])
+
         dx = to_sbuf("dx01", banks[5])
         hi_b1 = sb("hi_b1", [P, CHUNK * PACK], BF16, offset=AT_HI_B1)
-        for h in range(2):
-            nc.scalar.copy(out=woven(halves(hi_b1, h)), in_=by_runs(raw_b[1][:, :, h * HALF : (h + 1) * HALF]))
+        for a in range(PASSES):
+            nc.scalar.copy(out=woven(halves(hi_b1, a)), in_=by_runs(raw_b[1][a][:]))
         q_b.append(operand("q_b1", offset=AT_TOTAL00))
         quantise(q_b[1], hi_b1[:], E5M2)
-        clear_page(offset=AT_PAGE3)
         add_on_tensor(0, 1, dx, banks[6], banks[7], AT_DECODED)
         total = to_sbuf("total01", banks[7])
-        decoded_b0 = sb("dec_b0", [P, PACK, CHUNK], F32, offset=AT_DECODED)
+        product_a((2,), passes_a[::-1])
+        dx = to_sbuf("dx02", banks[6])
         for t in range(PACK):
             decode(banks[t], t, q_b[0])
-            nc.scalar.copy(out=decoded_b0[:, t, :], in_=banks[t][:, 0:CHUNK])
-        lo_b0 = sb("lo_b0", [P, CHUNK * PACK], BF16)
-        for b in range(BLOCKS):
-            cols = slice(b * P, (b + 1) * P)
-            nc.gpsimd.tensor_tensor(
-                woven(lo_b0[:, b * P * PACK : (b + 1) * P * PACK]),
-                by_runs(raw_b[0][:, :, cols]),
-                by_runs(decoded_b0[:, :, cols]),
-                ALU.subtract,
-            )
-        product_a((2,), passes_a[::-1])
-        product_a((3,), passes_a[::-1])
+        decoded_b0 = sb("dec_b0", [P, PASSES, PACK, HALF], F32, offset=AT_DECODED)
+        lo_b0 = sb("lo_b0", [P, CHUNK * PACK], BF16, offset=AT_HI_B1)
+        copy_decoded(decoded_b0, [(0, 0, HALF)])
         scatter_weighted(0, 1, total)
-        planes_b1 = sb("pl_b1", [P, PACK, CHUNK], BF16, tag="total01")
+        add_on_tensor(0, 2, dx, banks[5], banks[4])
+        total = to_sbuf("total02", banks[4])
+        copy_decoded(decoded_b0, [(1, 0, HALF)])
+        subtract_on_gpsimd(0, lo_b0, decoded_b0, [(a, b) for a in range(PASSES) for b in range(2)])
+        product_a((3,), passes_a[::-1])
+        scatter_weighted(0, 2, total)
+        add_on_tensor(0, 3, to_sbuf("dx03", banks[7]), banks[6], banks[7])
         for t in range(PACK):
             decode(banks[t], t, q_b[1])
-            nc.vector.tensor_tensor(planes_b1[:, t, :], raw_b[1][:, t, :], banks[t][:], ALU.subtract)
-        add_on_tensor(0, 2, to_sbuf("dx02", banks[6]), banks[5], banks[0])
-        total = to_sbuf("total02", banks[0])
-        add_on_tensor(0, 3, to_sbuf("dx03", banks[7]), banks[4], banks[7])
-        lo_b1 = sb("lo_b1", [P, CHUNK * PACK], BF16, tag="turned03")
-        nc.scalar.copy(out=woven(lo_b1[:]), in_=by_runs(planes_b1[:]))
-        scatter_weighted(0, 2, total)
-        r_b = [operand("r_b0", tag="total02"), operand("r_b1")]
+        decoded_b1 = sb("dec_b1", [P, PASSES, PACK, HALF], F32, tag="dx02")
+        copy_decoded(decoded_b1, [(0, 0, HALF), (1, 0, P)])
+        product_b(banks[4:6], q_b[0], E5M2, True)
+        r_b = [operand("r_b0", tag="total02")]
         quantise(r_b[0], lo_b0[:], E4M3)
-        total = to_sbuf("total03", banks[7], tag="lo_b0")
-        quantise(r_b[1], lo_b1[:], E4M3)
+        total = to_sbuf("total03", banks[7], offset=AT_TOTAL03)
+        product_b(banks[4:6], r_b[0], E4M3, False)
+        planes_b1 = sb("pl_b1", [P, PACK, P], BF16, offset=AT_PLANES_B1)
+        for t in range(PACK):
+            nc.vector.tensor_tensor(
+                planes_b1[:, t, :], raw_b[1][1][:, t, P:HALF], banks[t][:, HALF + P : CHUNK], ALU.subtract
+            )
+        lo_b1 = sb("lo_b1", [P, CHUNK * PACK], BF16, offset=AT_LO_B1)
+        subtract_on_gpsimd(1, lo_b1, decoded_b1, [(0, 0), (0, 1), (1, 0)])
         scatter_weighted(0, 3, total)
-
-        passes_b = [(a, q_b[a], E5M2) for a in range(PASSES)] + [(a, r_b[a], E4M3) for a in range(PASSES)]
-        product_banks = (1, 2, 3, 6)
-        sum_banks = {1: 5, 2: 4, 3: 0}
-        for r in range(ROW_TILES):
-            bank = banks[product_banks[r]]
-            for i, (a, q, fmt) in enumerate(passes_b):
-                product(bank, r, a, q, fmt, i == 0, i == len(passes_b) - 1)
-            if r == 0:
-                total = add_on_vector(1, r, bank)
-            else:
-                add_on_tensor(1, r, to_sbuf(f"dx1{r}", bank), banks[sum_banks[r]], bank)
-                total = to_sbuf(f"total1{r}", bank)
-            scatter_times_wgo(1, r, total)
-            nc.sync.dma_start(out=out[r * P : (r + 1) * P, :], in_=pages[r][:])
+        turn_res(0, 0, banks[6])
+        turn_dx(0, 0, banks[6], banks[4:6])
+        fetch(0, 0, banks[6])
+        nc.scalar.copy(out=woven_block(lo_b1, 1, 1), in_=by_runs(planes_b1[:]))
+        turn_res(0, 1, banks[7])
+        turn_dx(0, 1, banks[7], banks[4:6])
+        product_b(banks[0:2], q_b[1], E5M2, True)
+        turn_res(1, 0, banks[2])
+        scatter_b(0, 0)
+        r_b.append(operand("r_b1", tag="total_b00"))
+        quantise(r_b[1], lo_b1[:], E4M3)
+        fetch(0, 1, banks[6], offset=AT_LO_B1)
+        fetch(0, 2, banks[7])
+        product_b(banks[0:2], r_b[1], E4M3, False)
+        scatter_b(0, 1)
+        scatter_b(0, 2)
+        turn_dx(1, 0, banks[2], banks[0:2])
+        fetch(1, 0, banks[2])
+        fetch(1, 1, banks[2])
+        turn_res(1, 1, banks[3])
+        turn_dx(1, 1, banks[3], banks[0:2])
+        scatter_b(1, 0)
+        scatter_b(1, 1)
+        fetch(0, 3, banks[7], tag="total_b10")
+        scatter_b(0, 3)
+        for r in (2, 3):
+            fetch(1, r, banks[3])
+            scatter_b(1, r)

@@ -31,11 +31,20 @@ KIB = 1024
 AT_PAGE2 = 0
 AT_HI = 6 * KIB
 AT_TOTAL00 = 8 * KIB
-AT_HI_B1 = 16 * KIB
-AT_TOTAL03 = AT_HI_B1
-AT_PLANES_B1 = AT_HI_B1 + 2 * KIB
+AT_HI_B1 = 10 * KIB
 AT_LO_B1 = AT_HI_B1 + 3 * KIB
-AT_DECODED = 26 * KIB
+AT_DECODED_B1 = 17 * KIB
+AT_TOTAL_B00 = 25 * KIB
+AT_TOTAL_B01 = AT_TOTAL_B00 - KIB // 2
+AT_R_B1 = AT_TOTAL_B00 + KIB // 2
+AT_DECODED = 28 * KIB
+AT_TURNED_RES001 = AT_DECODED + 8 * KIB
+AT_TOTAL02 = AT_TURNED_RES001 + KIB
+AT_TOTAL03 = AT_TOTAL02 - 3 * KIB // 2
+AT_R_B0_SC = AT_TOTAL02 + KIB // 2
+AT_TURNED_RES000 = AT_TOTAL02 + 2 * KIB
+AT_PLANES_B1 = AT_TURNED_RES000 - KIB // 2
+AT_R_B0 = AT_TURNED_RES000 + KIB // 2
 
 
 def tile_list_embg_tgq8_res_kernel(tc, dy, w_words, w_scales, res, wgo, offs, out):
@@ -137,8 +146,8 @@ def tile_list_embg_tgq8_res_kernel(tc, dy, w_words, w_scales, res, wgo, offs, ou
                 rows = res[2 * pair * P : 2 * (pair + 1) * P, CHUNK + h * HALF : CHUNK + (h + 1) * HALF]
                 nc.sync.dma_start(out=res_b[h, pair][:], in_=rows.rearrange("(i p) j -> p i j", p=P))
 
-        def operand(name, tag=None, offset=None):
-            return sb(name + "_codes", [P, CHUNK], U32, tag, offset), sb(name + "_sc", [P, CHUNK], U8)
+        def operand(name, tag=None, offset=None, scale_tag=None, scale_offset=None):
+            return sb(name + "_codes", [P, CHUNK], U32, tag, offset), sb(name + "_sc", [P, CHUNK], U8, scale_tag, scale_offset)
 
         def quantise(q, src, fmt, j0=0, j1=CHUNK):
             nc.vector.quantize_mx(out=q[0][:, j0:j1].bitcast(fmt), scales=q[1][:, j0:j1], in_=src)
@@ -331,8 +340,8 @@ def tile_list_embg_tgq8_res_kernel(tc, dy, w_words, w_scales, res, wgo, offs, ou
                         stop=not first and a == PASSES - 1,
                     )
 
-        def weighted(name, h, b, src):
-            tile = sb(name, [P, 2 * P], F32)
+        def weighted(name, h, b, src, offset=None):
+            tile = sb(name, [P, 2 * P], F32, offset=offset)
             at = BLOCKS + 2 * h + b
             nc.scalar.activation(tile[:], src, COPY, scale=wgo_col[:, at : at + 1])
             return tile
@@ -350,13 +359,14 @@ def tile_list_embg_tgq8_res_kernel(tc, dy, w_words, w_scales, res, wgo, offs, ou
                     stop=stop and n == len(steps) - 1,
                 )
 
-        def turn_res(h, pair, bank):
+        def turn_res(h, pair, through, bank, at_turned=(None, None)):
             for b in range(2):
                 for i in range(2):
                     at = (2 * b + i) * P
-                    nc.tensor.transpose(bank[:, at : at + P], res_b[h, pair][:, i, b * P : (b + 1) * P], eye32[:])
+                    nc.tensor.transpose(through[:, at : at + P], res_b[h, pair][:, i, b * P : (b + 1) * P], eye32[:])
             turned = [
-                weighted(f"turned_res{h}{pair}{b}", h, b, bank[:, 2 * b * P : 2 * (b + 1) * P]) for b in range(2)
+                weighted(f"turned_res{h}{pair}0", h, 0, through[:, 0 : 2 * P], at_turned[0]),
+                weighted(f"turned_res{h}{pair}1", h, 1, through[:, 2 * P : 4 * P], at_turned[1]),
             ]
             turn_back(bank, turned, True, False)
 
@@ -375,19 +385,19 @@ def tile_list_embg_tgq8_res_kernel(tc, dy, w_words, w_scales, res, wgo, offs, ou
             columns = HALF // LIST_ROWS
             first = (CHUNK + h * HALF) // LIST_ROWS
             nc.vector.tensor_copy(pages[r][:].indirect(offsets[:, first : first + columns]), totals[h, r][:])
-            if h == 1:
+            if (h == 1) != (r == ROW_TILES - 1):
                 nc.sync.dma_start(out=out[r * P : (r + 1) * P, :], in_=pages[r][:])
 
-        dx = to_sbuf("dx01", banks[5])
+        dx = to_sbuf("dx01", banks[5], offset=AT_DECODED)
         hi_b1 = sb("hi_b1", [P, CHUNK * PACK], BF16, offset=AT_HI_B1)
         for a in range(PASSES):
             nc.scalar.copy(out=woven(halves(hi_b1, a)), in_=by_runs(raw_b[1][a][:]))
         q_b.append(operand("q_b1", offset=AT_TOTAL00))
         quantise(q_b[1], hi_b1[:], E5M2)
-        add_on_tensor(0, 1, dx, banks[6], banks[7], AT_DECODED)
+        add_on_tensor(0, 1, dx, banks[4], banks[7])
         total = to_sbuf("total01", banks[7])
         product_a((2,), passes_a[::-1])
-        dx = to_sbuf("dx02", banks[6])
+        dx = to_sbuf("dx02", banks[6], offset=AT_DECODED_B1)
         for t in range(PACK):
             decode(banks[t], t, q_b[0])
         decoded_b0 = sb("dec_b0", [P, PASSES, PACK, HALF], F32, offset=AT_DECODED)
@@ -395,7 +405,7 @@ def tile_list_embg_tgq8_res_kernel(tc, dy, w_words, w_scales, res, wgo, offs, ou
         copy_decoded(decoded_b0, [(0, 0, HALF)])
         scatter_weighted(0, 1, total)
         add_on_tensor(0, 2, dx, banks[5], banks[4])
-        total = to_sbuf("total02", banks[4])
+        total = to_sbuf("total02", banks[4], offset=AT_TOTAL02)
         copy_decoded(decoded_b0, [(1, 0, HALF)])
         subtract_on_gpsimd(0, lo_b0, decoded_b0, [(a, b) for a in range(PASSES) for b in range(2)])
         product_a((3,), passes_a[::-1])
@@ -403,46 +413,47 @@ def tile_list_embg_tgq8_res_kernel(tc, dy, w_words, w_scales, res, wgo, offs, ou
         add_on_tensor(0, 3, to_sbuf("dx03", banks[7]), banks[6], banks[7])
         for t in range(PACK):
             decode(banks[t], t, q_b[1])
-        decoded_b1 = sb("dec_b1", [P, PASSES, PACK, HALF], F32, tag="dx02")
+        decoded_b1 = sb("dec_b1", [P, PASSES, PACK, HALF], F32, offset=AT_DECODED_B1)
         copy_decoded(decoded_b1, [(0, 0, HALF), (1, 0, P)])
-        product_b(banks[4:6], q_b[0], E5M2, True)
-        r_b = [operand("r_b0", tag="total02")]
-        quantise(r_b[0], lo_b0[:], E4M3)
-        total = to_sbuf("total03", banks[7], offset=AT_TOTAL03)
-        product_b(banks[4:6], r_b[0], E4M3, False)
+        turn_res(0, 0, banks[6], banks[6], (AT_TURNED_RES000, AT_TURNED_RES001))
         planes_b1 = sb("pl_b1", [P, PACK, P], BF16, offset=AT_PLANES_B1)
         for t in range(PACK):
             nc.vector.tensor_tensor(
                 planes_b1[:, t, :], raw_b[1][1][:, t, P:HALF], banks[t][:, HALF + P : CHUNK], ALU.subtract
             )
+        product_b(banks[4:6], q_b[0], E5M2, True)
+        r_b = [operand("r_b0", offset=AT_R_B0, scale_offset=AT_R_B0_SC)]
+        quantise(r_b[0], lo_b0[:], E4M3)
+        total = to_sbuf("total03", banks[7], offset=AT_TOTAL03)
+        product_b(banks[4:6], r_b[0], E4M3, False)
         lo_b1 = sb("lo_b1", [P, CHUNK * PACK], BF16, offset=AT_LO_B1)
         subtract_on_gpsimd(1, lo_b1, decoded_b1, [(0, 0), (0, 1), (1, 0)])
         scatter_weighted(0, 3, total)
-        turn_res(0, 0, banks[6])
         turn_dx(0, 0, banks[6], banks[4:6])
-        fetch(0, 0, banks[6])
+        fetch(0, 0, banks[6], offset=AT_TOTAL_B00)
         nc.scalar.copy(out=woven_block(lo_b1, 1, 1), in_=by_runs(planes_b1[:]))
-        turn_res(0, 1, banks[7])
+        turn_res(0, 1, banks[0], banks[7])
         turn_dx(0, 1, banks[7], banks[4:6])
+        turn_res(1, 0, banks[1], banks[2])
         product_b(banks[0:2], q_b[1], E5M2, True)
-        turn_res(1, 0, banks[2])
         scatter_b(0, 0)
-        r_b.append(operand("r_b1", tag="total_b00"))
+        r_b.append(operand("r_b1", offset=AT_R_B1, scale_tag="dx_b011"))
         quantise(r_b[1], lo_b1[:], E4M3)
-        fetch(0, 1, banks[6], offset=AT_LO_B1)
-        fetch(0, 2, banks[7])
+        fetch(0, 1, banks[6], offset=AT_TOTAL_B01)
+        fetch(0, 2, banks[7], offset=AT_LO_B1)
         product_b(banks[0:2], r_b[1], E4M3, False)
         scatter_b(0, 1)
         scatter_b(0, 2)
         turn_dx(1, 0, banks[2], banks[0:2])
         fetch(1, 0, banks[2])
         fetch(1, 1, banks[2])
-        turn_res(1, 1, banks[3])
+        turn_res(1, 1, banks[3], banks[3])
         turn_dx(1, 1, banks[3], banks[0:2])
         scatter_b(1, 0)
         scatter_b(1, 1)
-        fetch(0, 3, banks[7], tag="total_b10")
+        fetch(1, 2, banks[3])
+        fetch(1, 3, banks[3])
+        scatter_b(1, 2)
+        scatter_b(1, 3)
+        fetch(0, 3, banks[7], tag="total_b12")
         scatter_b(0, 3)
-        for r in (2, 3):
-            fetch(1, r, banks[3])
-            scatter_b(1, r)

@@ -39,12 +39,12 @@ AT_TOTAL_B01 = AT_TOTAL_B00 - KIB // 2
 AT_R_B1 = AT_TOTAL_B00 + KIB // 2
 AT_DECODED = 28 * KIB
 AT_TURNED_RES001 = AT_DECODED + 8 * KIB
-AT_TOTAL02 = AT_TURNED_RES001 + KIB
+AT_TOTAL02 = AT_TURNED_RES001 + KIB // 2
 AT_TOTAL03 = AT_TOTAL02 - 3 * KIB // 2
 AT_R_B0_SC = AT_TOTAL02 + KIB // 2
 AT_TURNED_RES000 = AT_TOTAL02 + 2 * KIB
-AT_PLANES_B1 = AT_TURNED_RES000 - KIB // 2
-AT_R_B0 = AT_TURNED_RES000 + KIB // 2
+AT_PLANES_B1 = AT_TURNED_RES000 - 3 * KIB // 4
+AT_R_B0 = AT_TURNED_RES000 + KIB // 4
 
 
 def tile_list_embg_tgq8_res_kernel(tc, dy, w_words, w_scales, res, wgo, offs, out):
@@ -111,6 +111,7 @@ def tile_list_embg_tgq8_res_kernel(tc, dy, w_words, w_scales, res, wgo, offs, ou
         nc.sync.dma_start(out=wgo_rows[:], in_=wgo[0 : P * P // J, :].rearrange("r (c j) -> (r c) j", j=P))
         pieces.extend(load_dy(f"raw_a{a}{h}", a, h * HALF, HALF) for a, h in ((0, 1), (1, 0), (1, 1)))
         raw_b = [[load_dy(f"raw_b0{a}", a, CHUNK, HALF) for a in range(PASSES)]]
+        raw_b.append([load_dy("raw_b10", 0, CHUNK + HALF, HALF)])
         w_codes = sb("w_codes", [P, PASSES, N], U32)
         nc.sync.dma_start(
             out=w_codes[:].bitcast(I32),
@@ -136,7 +137,7 @@ def tile_list_embg_tgq8_res_kernel(tc, dy, w_words, w_scales, res, wgo, offs, ou
         nc.sync.dma_start(offsets[:], offs)
         load_res(0, 0)
         load_wgo(0)
-        raw_b.append([load_dy(f"raw_b1{a}", a, CHUNK + HALF, HALF) for a in range(PASSES)])
+        raw_b[1].append(load_dy("raw_b11", 1, CHUNK + HALF, HALF))
         for r in range(1, ROW_TILES):
             load_res(0, r)
         res_b = {}
@@ -341,39 +342,45 @@ def tile_list_embg_tgq8_res_kernel(tc, dy, w_words, w_scales, res, wgo, offs, ou
                     )
 
         def weighted(name, h, b, src, offset=None):
-            tile = sb(name, [P, 2 * P], F32, offset=offset)
+            tile = sb(name, [P, src.shape[1]], F32, offset=offset)
             at = BLOCKS + 2 * h + b
             nc.scalar.activation(tile[:], src, COPY, scale=wgo_col[:, at : at + 1])
             return tile
 
         def turn_back(bank, terms, start, stop):
-            steps = [(i, b) for i in range(2) for b in range(2)]
-            for n, (i, b) in enumerate(steps):
-                at = i * HALF + b * P
+            for n, (tile, at_tile, at_bank) in enumerate(terms):
                 nc.tensor.matmul(
-                    bank[:, at : at + P],
-                    lhsT=terms[b][:, i * P : (i + 1) * P],
+                    bank[:, at_bank : at_bank + P],
+                    lhsT=tile[:, at_tile : at_tile + P],
                     rhs=eye32[:],
                     is_transpose=True,
                     start=start and n == 0,
-                    stop=stop and n == len(steps) - 1,
+                    stop=stop and n == len(terms) - 1,
                 )
 
-        def turn_res(h, pair, through, bank, at_turned=(None, None)):
+        turned_res = {}
+
+        def turn_res(h, pair, through):
             for b in range(2):
                 for i in range(2):
                     at = (2 * b + i) * P
                     nc.tensor.transpose(through[:, at : at + P], res_b[h, pair][:, i, b * P : (b + 1) * P], eye32[:])
-            turned = [
-                weighted(f"turned_res{h}{pair}0", h, 0, through[:, 0 : 2 * P], at_turned[0]),
-                weighted(f"turned_res{h}{pair}1", h, 1, through[:, 2 * P : 4 * P], at_turned[1]),
-            ]
-            turn_back(bank, turned, True, False)
 
-        def turn_dx(h, pair, bank, sources):
-            cols = slice(2 * pair * P, 2 * (pair + 1) * P)
-            dx_turned = [weighted(f"dx_b{h}{pair}{b}", h, b, sources[b][:, cols]) for b in range(2)]
-            turn_back(bank, dx_turned, False, True)
+        def weigh_res(h, rows, through, at_turned=(None, None)):
+            for b in range(2):
+                src = through[:, (2 * b + rows[0] % 2) * P : (2 * b + rows[-1] % 2 + 1) * P]
+                tile = weighted(f"turned_res{h}{rows[0]}{b}", h, b, src, at_turned[b])
+                for r in rows:
+                    turned_res[h, r, b] = (tile, (r - rows[0]) * P, r % 2 * HALF + b * P)
+
+        def open_rows(h, rows, bank):
+            turn_back(bank, [turned_res[h, r, b] for b in range(2) for r in rows], True, False)
+
+        def add_rows(h, rows, bank, sources):
+            cols = slice(rows[0] * P, (rows[-1] + 1) * P)
+            dx_turned = [weighted(f"dx_b{h}{rows[0]}{b}", h, b, sources[b][:, cols]) for b in range(2)]
+            dx_terms = [(dx_turned[b], (r - rows[0]) * P, r % 2 * HALF + b * P) for b in range(2) for r in rows]
+            turn_back(bank, dx_terms, False, True)
 
         totals = {}
 
@@ -415,7 +422,10 @@ def tile_list_embg_tgq8_res_kernel(tc, dy, w_words, w_scales, res, wgo, offs, ou
             decode(banks[t], t, q_b[1])
         decoded_b1 = sb("dec_b1", [P, PASSES, PACK, HALF], F32, offset=AT_DECODED_B1)
         copy_decoded(decoded_b1, [(0, 0, HALF), (1, 0, P)])
-        turn_res(0, 0, banks[6], banks[6], (AT_TURNED_RES000, AT_TURNED_RES001))
+        turn_res(0, 0, banks[6])
+        weigh_res(0, (1,), banks[6])
+        weigh_res(0, (0,), banks[6], (AT_TURNED_RES000, AT_TURNED_RES001))
+        open_rows(0, (0,), banks[6])
         planes_b1 = sb("pl_b1", [P, PACK, P], BF16, offset=AT_PLANES_B1)
         for t in range(PACK):
             nc.vector.tensor_tensor(
@@ -429,26 +439,36 @@ def tile_list_embg_tgq8_res_kernel(tc, dy, w_words, w_scales, res, wgo, offs, ou
         lo_b1 = sb("lo_b1", [P, CHUNK * PACK], BF16, offset=AT_LO_B1)
         subtract_on_gpsimd(1, lo_b1, decoded_b1, [(0, 0), (0, 1), (1, 0)])
         scatter_weighted(0, 3, total)
-        turn_dx(0, 0, banks[6], banks[4:6])
+        add_rows(0, (0,), banks[6], banks[4:6])
         fetch(0, 0, banks[6], offset=AT_TOTAL_B00)
+        open_rows(0, (1,), banks[6])
+        add_rows(0, (1,), banks[6], banks[4:6])
         nc.scalar.copy(out=woven_block(lo_b1, 1, 1), in_=by_runs(planes_b1[:]))
-        turn_res(0, 1, banks[0], banks[7])
-        turn_dx(0, 1, banks[7], banks[4:6])
-        turn_res(1, 0, banks[1], banks[2])
+        turn_res(0, 1, banks[0])
+        weigh_res(0, (2, 3), banks[0])
+        open_rows(0, (2, 3), banks[7])
+        add_rows(0, (2, 3), banks[7], banks[4:6])
+        turn_res(1, 0, banks[1])
+        weigh_res(1, (0, 1), banks[1])
+        open_rows(1, (0,), banks[2])
         product_b(banks[0:2], q_b[1], E5M2, True)
         scatter_b(0, 0)
-        r_b.append(operand("r_b1", offset=AT_R_B1, scale_tag="dx_b011"))
+        r_b.append(operand("r_b1", offset=AT_R_B1, scale_tag="dx_b021"))
         quantise(r_b[1], lo_b1[:], E4M3)
         fetch(0, 1, banks[6], offset=AT_TOTAL_B01)
         fetch(0, 2, banks[7], offset=AT_LO_B1)
         product_b(banks[0:2], r_b[1], E4M3, False)
         scatter_b(0, 1)
         scatter_b(0, 2)
-        turn_dx(1, 0, banks[2], banks[0:2])
+        add_rows(1, (0,), banks[2], banks[0:2])
         fetch(1, 0, banks[2])
+        open_rows(1, (1,), banks[2])
+        add_rows(1, (1,), banks[2], banks[0:2])
         fetch(1, 1, banks[2])
-        turn_res(1, 1, banks[3], banks[3])
-        turn_dx(1, 1, banks[3], banks[0:2])
+        turn_res(1, 1, banks[3])
+        weigh_res(1, (2, 3), banks[3])
+        open_rows(1, (2, 3), banks[3])
+        add_rows(1, (2, 3), banks[3], banks[0:2])
         scatter_b(1, 0)
         scatter_b(1, 1)
         fetch(1, 2, banks[3])

@@ -314,14 +314,14 @@ def tile_list_embg_tgq8_res_kernel(tc, dy, w_words, w_scales, res, wgo, offs, ou
                 for t in range(PACK):
                     nc.scalar.copy(out=tile[:, a, t, j0:j1], in_=banks[t][:, a * HALF + j0 : a * HALF + j1])
 
-        def woven_block(lo, a, b):
-            return woven(lo[:, (a * HALF + b * P) * PACK : (a * HALF + (b + 1) * P) * PACK])
+        def woven_part(lo, a, j0, j1):
+            return woven(lo[:, (a * HALF + j0) * PACK : (a * HALF + j1) * PACK])
 
-        def subtract_on_gpsimd(h, lo, decoded, blocks):
-            for a, b in blocks:
-                cols = slice(b * P, (b + 1) * P)
+        def subtract_on_gpsimd(h, lo, decoded, pieces_b):
+            for a, j0, j1 in pieces_b:
+                cols = slice(j0, j1)
                 nc.gpsimd.tensor_tensor(
-                    woven_block(lo, a, b),
+                    woven_part(lo, a, j0, j1),
                     by_runs(raw_b[h][a][:, :, cols]),
                     by_runs(decoded[:, a, :, cols]),
                     ALU.subtract,
@@ -392,7 +392,7 @@ def tile_list_embg_tgq8_res_kernel(tc, dy, w_words, w_scales, res, wgo, offs, ou
             columns = HALF // LIST_ROWS
             first = (CHUNK + h * HALF) // LIST_ROWS
             nc.vector.tensor_copy(pages[r][:].indirect(offsets[:, first : first + columns]), totals[h, r][:])
-            if (h == 1) != (r == ROW_TILES - 1):
+            if h == 1:
                 nc.sync.dma_start(out=out[r * P : (r + 1) * P, :], in_=pages[r][:])
 
         dx = to_sbuf("dx01", banks[5], offset=AT_DECODED)
@@ -414,7 +414,7 @@ def tile_list_embg_tgq8_res_kernel(tc, dy, w_words, w_scales, res, wgo, offs, ou
         add_on_tensor(0, 2, dx, banks[5], banks[4])
         total = to_sbuf("total02", banks[4], offset=AT_TOTAL02)
         copy_decoded(decoded_b0, [(1, 0, HALF)])
-        subtract_on_gpsimd(0, lo_b0, decoded_b0, [(a, b) for a in range(PASSES) for b in range(2)])
+        subtract_on_gpsimd(0, lo_b0, decoded_b0, [(a, 0, HALF) for a in range(PASSES)])
         product_a((3,), passes_a[::-1])
         scatter_weighted(0, 2, total)
         add_on_tensor(0, 3, to_sbuf("dx03", banks[7]), banks[6], banks[7])
@@ -437,13 +437,13 @@ def tile_list_embg_tgq8_res_kernel(tc, dy, w_words, w_scales, res, wgo, offs, ou
         total = to_sbuf("total03", banks[7], offset=AT_TOTAL03)
         product_b(banks[4:6], r_b[0], E4M3, False)
         lo_b1 = sb("lo_b1", [P, CHUNK * PACK], BF16, offset=AT_LO_B1)
-        subtract_on_gpsimd(1, lo_b1, decoded_b1, [(0, 0), (0, 1), (1, 0)])
+        subtract_on_gpsimd(1, lo_b1, decoded_b1, [(0, 0, HALF), (1, 0, P)])
         scatter_weighted(0, 3, total)
         add_rows(0, (0,), banks[6], banks[4:6])
         fetch(0, 0, banks[6], offset=AT_TOTAL_B00)
         open_rows(0, (1,), banks[6])
         add_rows(0, (1,), banks[6], banks[4:6])
-        nc.scalar.copy(out=woven_block(lo_b1, 1, 1), in_=by_runs(planes_b1[:]))
+        nc.scalar.copy(out=woven_part(lo_b1, 1, P, HALF), in_=by_runs(planes_b1[:]))
         turn_res(0, 1, banks[0])
         weigh_res(0, (2, 3), banks[0])
         open_rows(0, (2, 3), banks[7])
@@ -472,8 +472,9 @@ def tile_list_embg_tgq8_res_kernel(tc, dy, w_words, w_scales, res, wgo, offs, ou
         scatter_b(1, 0)
         scatter_b(1, 1)
         fetch(1, 2, banks[3])
-        fetch(1, 3, banks[3])
         scatter_b(1, 2)
-        scatter_b(1, 3)
-        fetch(0, 3, banks[7], tag="total_b12")
-        scatter_b(0, 3)
+        total = sb("total13", [P, CHUNK], F32)
+        for h, bank in enumerate((banks[7], banks[3])):
+            nc.scalar.copy(out=total[:, h * HALF : (h + 1) * HALF], in_=bank[:, HALF:CHUNK])
+        scatter_weighted(1, 3, total)
+        nc.sync.dma_start(out=out[3 * P : 4 * P, :], in_=pages[3][:])

@@ -33,7 +33,7 @@ AT_HI = 6 * KIB
 AT_TOTAL00 = 8 * KIB
 AT_HI_B1 = 10 * KIB
 AT_LO_B1 = AT_HI_B1 + 3 * KIB
-AT_DECODED_B1 = 17 * KIB
+AT_DECODED_B1 = 19 * KIB
 AT_TOTAL_B00 = 25 * KIB
 AT_TOTAL_B01 = AT_TOTAL_B00 - KIB // 2
 AT_R_B1 = AT_TOTAL_B00 + KIB // 2
@@ -86,7 +86,7 @@ def tile_list_embg_tgq8_res_kernel(tc, dy, w_words, w_scales, res, wgo, offs, ou
         nc.vector.transpose(in_quadrant[:], column[:, 0:32])
         quadrant = sb("quadrant", [P, 1], F32)
         for q in range(4):
-            nc.gpsimd.memset(quadrant[32 * q : 32 * q + 32, :], float(32 * q))
+            nc.vector.memset(quadrant[32 * q : 32 * q + 32, :], float(32 * q))
         eye_rows = sb("eye_in", [P, PACK * (K_PASS + 1) + 2], BF16)
         nc.vector.memset(eye_rows[:].bitcast(I32), 0)
         diagonals = eye_rows[:, 0 : PACK * (K_PASS + 1)].rearrange("p (t x) -> p t x", t=PACK)[:, :, 0:K_PASS:PACK]
@@ -104,7 +104,7 @@ def tile_list_embg_tgq8_res_kernel(tc, dy, w_words, w_scales, res, wgo, offs, ou
             out=eye_codes[:].bitcast(E4M3), scales=eye_sc[:], in_=eye_rows[:, 0 : PACK * K_PASS]
         )
         eye32 = sb("eye32", [P, P], F32)
-        nc.scalar.copy(out=eye32[:], in_=diagonals[:, 0, :])
+        nc.vector.tensor_scalar(eye32[:], column[:], quadrant[:], in_quadrant[:, 0:1], ALU.subtract, ALU.is_equal)
 
         pieces = [load_dy("raw_a00", 0, 0, HALF)]
         wgo_rows = sb("wgo_rows", [P, P], F32)
@@ -133,16 +133,16 @@ def tile_list_embg_tgq8_res_kernel(tc, dy, w_words, w_scales, res, wgo, offs, ou
             wgo_sb.append(sb(f"wgo{c}", [P, CHUNK], F32))
             nc.sync.dma_start(out=wgo_sb[c][:], in_=wgo[:, c * CHUNK : (c + 1) * CHUNK])
 
+        raw_b[1].append(load_dy("raw_b11", 1, CHUNK + HALF, HALF))
         offsets = keep.tile([P, J // LIST_ROWS], U16, name="offsets")
         nc.sync.dma_start(offsets[:], offs)
         load_res(0, 0)
         load_wgo(0)
-        raw_b[1].append(load_dy("raw_b11", 1, CHUNK + HALF, HALF))
         for r in range(1, ROW_TILES):
             load_res(0, r)
         res_b = {}
-        for h in range(2):
-            for pair in range(2):
+        for pair in range(2):
+            for h in range(2):
                 res_b[h, pair] = sb(f"res_b{h}{pair}", [P, 2, HALF], F32)
                 rows = res[2 * pair * P : 2 * (pair + 1) * P, CHUNK + h * HALF : CHUNK + (h + 1) * HALF]
                 nc.sync.dma_start(out=res_b[h, pair][:], in_=rows.rearrange("(i p) j -> p i j", p=P))
@@ -179,9 +179,11 @@ def tile_list_embg_tgq8_res_kernel(tc, dy, w_words, w_scales, res, wgo, offs, ou
 
         pages = []
 
-        def clear_page(tag=None, offset=None):
+        def clear_page(tag=None, offset=None, on_vector=0):
             page = sb(f"page{len(pages)}", [P, T], F32, tag, offset)
-            nc.gpsimd.memset(page[:], 0.0)
+            if on_vector:
+                nc.vector.memset(page[:, 0 : on_vector + 8], 0.0)
+            nc.gpsimd.memset(page[:, on_vector:], 0.0)
             pages.append(page)
 
         def places(c, r):
@@ -229,12 +231,12 @@ def tile_list_embg_tgq8_res_kernel(tc, dy, w_words, w_scales, res, wgo, offs, ou
 
         nc.tensor.transpose(banks[7][:, 0:P], wgo_rows[:], eye32[:])
         wgo_col = sb("wgo_col", [P, J // P], F32)
-        nc.scalar.copy(out=wgo_col[:], in_=banks[7][:, 0 : J // P])
+        nc.vector.tensor_copy(out=wgo_col[:], in_=banks[7][:, 0 : J // P])
         clear_page()
         q_a = (sb("q_a_codes", [P, 5 * HALF], U32), sb("q_a_sc", [P, 5 * HALF], U8))
         nc.gpsimd.memset(q_a[0][:, 0:HALF], 0)
         nc.gpsimd.memset(q_a[1][:, 0:HALF].bitcast(I32), 0)
-        hi_a0 = sb("hi_a0", [P, HALF * PACK], BF16, tag="eye_in")
+        hi_a0 = sb("hi_a0", [P, HALF * PACK], BF16)
         shared = sb("shared", [P, CHUNK + CHUNK * PACK], BF16)
         hi_a12 = shared[:, CHUNK:]
         planes_a0 = shared[:, 0 : PACK * HALF].rearrange("p (t j) -> p t j", t=PACK)
@@ -242,7 +244,7 @@ def tile_list_embg_tgq8_res_kernel(tc, dy, w_words, w_scales, res, wgo, offs, ou
         lo_a0 = sb("lo_a0", [P, CHUNK * PACK], BF16)
         lo_a1 = [sb(f"lo_a1{h}", [P, HALF * PACK], BF16) for h in range(2)]
         lo_pieces = [halves(lo_a0, 0), halves(lo_a0, 1), lo_a1[0][:], lo_a1[1][:]]
-        nc.vector.tensor_copy(out=woven(hi_a0[:]), in_=by_runs(pieces[0][:]))
+        nc.scalar.copy(out=woven(hi_a0[:]), in_=by_runs(pieces[0][:]))
         nc.scalar.copy(out=woven(halves(hi_a12, 0)), in_=by_runs(pieces[1][:]))
         nc.scalar.copy(out=woven(halves(hi_a12, 1)), in_=by_runs(pieces[2][:]))
         nc.scalar.copy(out=woven(hi_a3[:]), in_=by_runs(pieces[3][:]))
@@ -258,7 +260,7 @@ def tile_list_embg_tgq8_res_kernel(tc, dy, w_words, w_scales, res, wgo, offs, ou
             nc.scalar.copy(out=woven(lo_pieces[i]), in_=by_runs(planes[:]))
 
         quantise(q_a, hi_a0[:], E5M2, HALF, 2 * HALF)
-        clear_page("eye_in")
+        clear_page("hi_a0", on_vector=CHUNK)
         for t in range(PACK):
             decode(banks[t], t, q_a, 0)
         subtract_piece(0, 0, 1, planes_a0, (0, 1))
@@ -309,21 +311,22 @@ def tile_list_embg_tgq8_res_kernel(tc, dy, w_words, w_scales, res, wgo, offs, ou
         clear_page("res00")
         scatter_times_wgo(0, 0, total)
 
-        def copy_decoded(tile, pieces_b):
-            for a, j0, j1 in pieces_b:
-                for t in range(PACK):
-                    nc.scalar.copy(out=tile[:, a, t, j0:j1], in_=banks[t][:, a * HALF + j0 : a * HALF + j1])
+        def copy_decoded(name, j0, j1, offset):
+            tile = sb(name, [P, PACK, j1 - j0], F32, offset=offset)
+            for t in range(PACK):
+                nc.scalar.copy(out=tile[:, t, :], in_=banks[t][:, j0:j1])
+            return tile[:]
 
         def woven_part(lo, a, j0, j1):
             return woven(lo[:, (a * HALF + j0) * PACK : (a * HALF + j1) * PACK])
 
-        def subtract_on_gpsimd(h, lo, decoded, pieces_b):
-            for a, j0, j1 in pieces_b:
-                cols = slice(j0, j1)
+        def subtract_on_gpsimd(h, lo, decoded):
+            for a in range(PASSES):
+                width = decoded[a].shape[2]
                 nc.gpsimd.tensor_tensor(
-                    woven_part(lo, a, j0, j1),
-                    by_runs(raw_b[h][a][:, :, cols]),
-                    by_runs(decoded[:, a, :, cols]),
+                    woven_part(lo, a, 0, width),
+                    by_runs(raw_b[h][a][:, :, 0:width]),
+                    by_runs(decoded[a]),
                     ALU.subtract,
                 )
 
@@ -401,31 +404,32 @@ def tile_list_embg_tgq8_res_kernel(tc, dy, w_words, w_scales, res, wgo, offs, ou
             nc.scalar.copy(out=woven(halves(hi_b1, a)), in_=by_runs(raw_b[1][a][:]))
         q_b.append(operand("q_b1", offset=AT_TOTAL00))
         quantise(q_b[1], hi_b1[:], E5M2)
-        add_on_tensor(0, 1, dx, banks[4], banks[7])
+        add_on_tensor(0, 1, dx, banks[5], banks[7], AT_DECODED + 4 * KIB)
         total = to_sbuf("total01", banks[7])
         product_a((2,), passes_a[::-1])
         dx = to_sbuf("dx02", banks[6], offset=AT_DECODED_B1)
         for t in range(PACK):
             decode(banks[t], t, q_b[0])
-        decoded_b0 = sb("dec_b0", [P, PASSES, PACK, HALF], F32, offset=AT_DECODED)
         lo_b0 = sb("lo_b0", [P, CHUNK * PACK], BF16, offset=AT_HI_B1)
-        copy_decoded(decoded_b0, [(0, 0, HALF)])
+        decoded_b0 = [copy_decoded("dec_b00", 0, HALF, AT_DECODED)]
         scatter_weighted(0, 1, total)
-        add_on_tensor(0, 2, dx, banks[5], banks[4])
-        total = to_sbuf("total02", banks[4], offset=AT_TOTAL02)
-        copy_decoded(decoded_b0, [(1, 0, HALF)])
-        subtract_on_gpsimd(0, lo_b0, decoded_b0, [(a, 0, HALF) for a in range(PASSES)])
+        add_on_tensor(0, 2, dx, banks[4], banks[5])
+        total = to_sbuf("total02", banks[5], offset=AT_TOTAL02)
+        decoded_b0.append(copy_decoded("dec_b01", HALF, CHUNK, AT_DECODED + 4 * KIB))
+        subtract_on_gpsimd(0, lo_b0, decoded_b0)
         product_a((3,), passes_a[::-1])
         scatter_weighted(0, 2, total)
         add_on_tensor(0, 3, to_sbuf("dx03", banks[7]), banks[6], banks[7])
         for t in range(PACK):
             decode(banks[t], t, q_b[1])
-        decoded_b1 = sb("dec_b1", [P, PASSES, PACK, HALF], F32, offset=AT_DECODED_B1)
-        copy_decoded(decoded_b1, [(0, 0, HALF), (1, 0, P)])
-        turn_res(0, 0, banks[6])
-        weigh_res(0, (1,), banks[6])
-        weigh_res(0, (0,), banks[6], (AT_TURNED_RES000, AT_TURNED_RES001))
+        decoded = copy_decoded("dec_b1", 0, HALF + P, AT_DECODED_B1)
+        decoded_b1 = [decoded[:, :, 0:HALF], decoded[:, :, HALF:]]
+        turn_res(0, 0, banks[4])
+        weigh_res(0, (1,), banks[4])
+        weigh_res(0, (0,), banks[4], (AT_TURNED_RES000, AT_TURNED_RES001))
         open_rows(0, (0,), banks[6])
+        turn_res(1, 0, banks[4])
+        weigh_res(1, (0, 1), banks[4])
         planes_b1 = sb("pl_b1", [P, PACK, P], BF16, offset=AT_PLANES_B1)
         for t in range(PACK):
             nc.vector.tensor_tensor(
@@ -437,7 +441,7 @@ def tile_list_embg_tgq8_res_kernel(tc, dy, w_words, w_scales, res, wgo, offs, ou
         total = to_sbuf("total03", banks[7], offset=AT_TOTAL03)
         product_b(banks[4:6], r_b[0], E4M3, False)
         lo_b1 = sb("lo_b1", [P, CHUNK * PACK], BF16, offset=AT_LO_B1)
-        subtract_on_gpsimd(1, lo_b1, decoded_b1, [(0, 0, HALF), (1, 0, P)])
+        subtract_on_gpsimd(1, lo_b1, decoded_b1)
         scatter_weighted(0, 3, total)
         add_rows(0, (0,), banks[6], banks[4:6])
         fetch(0, 0, banks[6], offset=AT_TOTAL_B00)
@@ -448,27 +452,25 @@ def tile_list_embg_tgq8_res_kernel(tc, dy, w_words, w_scales, res, wgo, offs, ou
         weigh_res(0, (2, 3), banks[0])
         open_rows(0, (2, 3), banks[7])
         add_rows(0, (2, 3), banks[7], banks[4:6])
-        turn_res(1, 0, banks[1])
-        weigh_res(1, (0, 1), banks[1])
         open_rows(1, (0,), banks[2])
-        product_b(banks[0:2], q_b[1], E5M2, True)
+        product_b(banks[4:6], q_b[1], E5M2, True)
         scatter_b(0, 0)
         r_b.append(operand("r_b1", offset=AT_R_B1, scale_tag="dx_b021"))
         quantise(r_b[1], lo_b1[:], E4M3)
         fetch(0, 1, banks[6], offset=AT_TOTAL_B01)
         fetch(0, 2, banks[7], offset=AT_LO_B1)
-        product_b(banks[0:2], r_b[1], E4M3, False)
+        product_b(banks[4:6], r_b[1], E4M3, False)
         scatter_b(0, 1)
         scatter_b(0, 2)
-        add_rows(1, (0,), banks[2], banks[0:2])
+        add_rows(1, (0,), banks[2], banks[4:6])
         fetch(1, 0, banks[2])
         open_rows(1, (1,), banks[2])
-        add_rows(1, (1,), banks[2], banks[0:2])
+        add_rows(1, (1,), banks[2], banks[4:6])
         fetch(1, 1, banks[2])
         turn_res(1, 1, banks[3])
         weigh_res(1, (2, 3), banks[3])
         open_rows(1, (2, 3), banks[3])
-        add_rows(1, (2, 3), banks[3], banks[0:2])
+        add_rows(1, (2, 3), banks[3], banks[4:6])
         scatter_b(1, 0)
         scatter_b(1, 1)
         fetch(1, 2, banks[3])

@@ -141,11 +141,13 @@ def tile_list_embg_tgq8_res_kernel(tc, dy, w_words, w_scales, res, wgo, offs, ou
         for r in range(1, ROW_TILES):
             load_res(0, r)
         res_b = {}
-        for pair in range(2):
+        for rows in ((0,), (1, 2, 3)):
             for h in range(2):
-                res_b[h, pair] = sb(f"res_b{h}{pair}", [P, 2, HALF], F32)
-                rows = res[2 * pair * P : 2 * (pair + 1) * P, CHUNK + h * HALF : CHUNK + (h + 1) * HALF]
-                nc.sync.dma_start(out=res_b[h, pair][:], in_=rows.rearrange("(i p) j -> p i j", p=P))
+                tile = sb(f"res_b{h}{rows[0]}", [P, len(rows), HALF], F32)
+                src = res[rows[0] * P : (rows[-1] + 1) * P, CHUNK + h * HALF : CHUNK + (h + 1) * HALF]
+                nc.sync.dma_start(out=tile[:], in_=src.rearrange("(i p) j -> p i j", p=P))
+                for i, r in enumerate(rows):
+                    res_b[h, r] = tile[:, i, :]
 
         def operand(name, tag=None, offset=None, scale_tag=None, scale_offset=None):
             return sb(name + "_codes", [P, CHUNK], U32, tag, offset), sb(name + "_sc", [P, CHUNK], U8, scale_tag, scale_offset)
@@ -363,18 +365,15 @@ def tile_list_embg_tgq8_res_kernel(tc, dy, w_words, w_scales, res, wgo, offs, ou
 
         turned_res = {}
 
-        def turn_res(h, pair, through):
-            for b in range(2):
-                for i in range(2):
-                    at = (2 * b + i) * P
-                    nc.tensor.transpose(through[:, at : at + P], res_b[h, pair][:, i, b * P : (b + 1) * P], eye32[:])
+        def turn_res(h, b, rows, through, offset=None):
+            for i, r in enumerate(rows):
+                nc.tensor.transpose(through[:, i * P : (i + 1) * P], res_b[h, r][:, b * P : (b + 1) * P], eye32[:])
+            return lambda: weigh_res(h, b, rows, through, offset)
 
-        def weigh_res(h, rows, through, at_turned=(None, None)):
-            for b in range(2):
-                src = through[:, (2 * b + rows[0] % 2) * P : (2 * b + rows[-1] % 2 + 1) * P]
-                tile = weighted(f"turned_res{h}{rows[0]}{b}", h, b, src, at_turned[b])
-                for r in rows:
-                    turned_res[h, r, b] = (tile, (r - rows[0]) * P, r % 2 * HALF + b * P)
+        def weigh_res(h, b, rows, through, offset):
+            tile = weighted(f"turned_res{h}{rows[0]}{b}", h, b, through[:, 0 : len(rows) * P], offset)
+            for i, r in enumerate(rows):
+                turned_res[h, r, b] = (tile, i * P, r % 2 * HALF + b * P)
 
         def open_rows(h, rows, bank):
             turn_back(bank, [turned_res[h, r, b] for b in range(2) for r in rows], True, False)
@@ -424,12 +423,12 @@ def tile_list_embg_tgq8_res_kernel(tc, dy, w_words, w_scales, res, wgo, offs, ou
             decode(banks[t], t, q_b[1])
         decoded = copy_decoded("dec_b1", 0, HALF + P, AT_DECODED_B1)
         decoded_b1 = [decoded[:, :, 0:HALF], decoded[:, :, HALF:]]
-        turn_res(0, 0, banks[4])
-        weigh_res(0, (1,), banks[4])
-        weigh_res(0, (0,), banks[4], (AT_TURNED_RES000, AT_TURNED_RES001))
+        firsts = [(1, 0, None), (1, 1, None), (0, 0, AT_TURNED_RES000), (0, 1, AT_TURNED_RES001)]
+        for weigh in [
+            turn_res(h, b, (0,), banks[4][:, i * P : (i + 1) * P], at) for i, (h, b, at) in enumerate(firsts)
+        ]:
+            weigh()
         open_rows(0, (0,), banks[6])
-        turn_res(1, 0, banks[4])
-        weigh_res(1, (0, 1), banks[4])
         planes_b1 = sb("pl_b1", [P, PACK, P], BF16, offset=AT_PLANES_B1)
         for t in range(PACK):
             nc.vector.tensor_tensor(
@@ -445,13 +444,13 @@ def tile_list_embg_tgq8_res_kernel(tc, dy, w_words, w_scales, res, wgo, offs, ou
         scatter_weighted(0, 3, total)
         add_rows(0, (0,), banks[6], banks[4:6])
         fetch(0, 0, banks[6], offset=AT_TOTAL_B00)
-        open_rows(0, (1,), banks[6])
-        add_rows(0, (1,), banks[6], banks[4:6])
         nc.scalar.copy(out=woven_part(lo_b1, 1, P, HALF), in_=by_runs(planes_b1[:]))
-        turn_res(0, 1, banks[0])
-        weigh_res(0, (2, 3), banks[0])
+        for b in range(2):
+            turn_res(0, b, (1, 2, 3), banks[b])()
         open_rows(0, (2, 3), banks[7])
         add_rows(0, (2, 3), banks[7], banks[4:6])
+        open_rows(0, (1,), banks[6])
+        add_rows(0, (1,), banks[6], banks[4:6])
         open_rows(1, (0,), banks[2])
         product_b(banks[4:6], q_b[1], E5M2, True)
         scatter_b(0, 0)
@@ -464,11 +463,11 @@ def tile_list_embg_tgq8_res_kernel(tc, dy, w_words, w_scales, res, wgo, offs, ou
         scatter_b(0, 2)
         add_rows(1, (0,), banks[2], banks[4:6])
         fetch(1, 0, banks[2])
+        for b in range(2):
+            turn_res(1, b, (1, 2, 3), banks[b])()
         open_rows(1, (1,), banks[2])
         add_rows(1, (1,), banks[2], banks[4:6])
         fetch(1, 1, banks[2])
-        turn_res(1, 1, banks[3])
-        weigh_res(1, (2, 3), banks[3])
         open_rows(1, (2, 3), banks[3])
         add_rows(1, (2, 3), banks[3], banks[4:6])
         scatter_b(1, 0)

@@ -78,18 +78,18 @@ def tile_list_embg_tgq8_res_kernel(tc, dy, w_words, w_scales, res, wgo, offs, ou
 
         w_sc = sb("w_sc", [P, PASSES, N], U8)
         nc.gpsimd.memset(w_sc[:].rearrange("p a n -> p (a n)").bitcast(I32), 0)
-        ones = sb("ones", [P, P + 1], F32)
+        ones = sb("ones", [P, P], F32)
         nc.vector.memset(ones[:], 1.0)
         column = sb("column", [P, P], F32)
-        nc.vector.tensor_tensor_scan(column[:], ones[:, 0:P], ones[:, 0:P], -1.0, ALU.mult, ALU.add)
+        nc.vector.tensor_tensor_scan(column[:], ones[:], ones[:], -1.0, ALU.mult, ALU.add)
         in_quadrant = sb("in_quadrant", [P, 32], F32)
         nc.vector.transpose(in_quadrant[:], column[:, 0:32])
         quadrant = sb("quadrant", [P, 1], F32)
         for q in range(4):
-            nc.vector.memset(quadrant[32 * q : 32 * q + 32, :], float(32 * q))
-        eye_rows = sb("eye_in", [P, PACK * (K_PASS + 1) + 2], BF16)
+            nc.gpsimd.memset(quadrant[32 * q : 32 * q + 32, :], float(32 * q))
+        eye_rows = sb("eye_in", [P, PACK * (K_PASS + 1)], BF16)
         nc.vector.memset(eye_rows[:].bitcast(I32), 0)
-        diagonals = eye_rows[:, 0 : PACK * (K_PASS + 1)].rearrange("p (t x) -> p t x", t=PACK)[:, :, 0:K_PASS:PACK]
+        diagonals = eye_rows[:].rearrange("p (t x) -> p t x", t=PACK)[:, :, 0:K_PASS:PACK]
         nc.vector.tensor_scalar(
             diagonals,
             column[:].unsqueeze(1).to_broadcast([P, PACK, P]),
@@ -181,11 +181,9 @@ def tile_list_embg_tgq8_res_kernel(tc, dy, w_words, w_scales, res, wgo, offs, ou
 
         pages = []
 
-        def clear_page(tag=None, offset=None, on_vector=0):
+        def clear_page(tag=None, offset=None, engine=nc.gpsimd):
             page = sb(f"page{len(pages)}", [P, T], F32, tag, offset)
-            if on_vector:
-                nc.vector.memset(page[:, 0 : on_vector + 8], 0.0)
-            nc.gpsimd.memset(page[:, on_vector:], 0.0)
+            engine.memset(page[:], 0.0)
             pages.append(page)
 
         def places(c, r):
@@ -234,7 +232,7 @@ def tile_list_embg_tgq8_res_kernel(tc, dy, w_words, w_scales, res, wgo, offs, ou
         nc.tensor.transpose(banks[7][:, 0:P], wgo_rows[:], eye32[:])
         wgo_col = sb("wgo_col", [P, J // P], F32)
         nc.vector.tensor_copy(out=wgo_col[:], in_=banks[7][:, 0 : J // P])
-        clear_page()
+        clear_page(engine=nc.vector)
         q_a = (sb("q_a_codes", [P, 5 * HALF], U32), sb("q_a_sc", [P, 5 * HALF], U8))
         nc.gpsimd.memset(q_a[0][:, 0:HALF], 0)
         nc.gpsimd.memset(q_a[1][:, 0:HALF].bitcast(I32), 0)
@@ -262,7 +260,7 @@ def tile_list_embg_tgq8_res_kernel(tc, dy, w_words, w_scales, res, wgo, offs, ou
             nc.scalar.copy(out=woven(lo_pieces[i]), in_=by_runs(planes[:]))
 
         quantise(q_a, hi_a0[:], E5M2, HALF, 2 * HALF)
-        clear_page("hi_a0", on_vector=CHUNK)
+        clear_page("hi_a0")
         for t in range(PACK):
             decode(banks[t], t, q_a, 0)
         subtract_piece(0, 0, 1, planes_a0, (0, 1))

@@ -20,31 +20,28 @@ P = 128
 PACK = 4
 K_PASS = P * PACK
 PASSES = K // K_PASS
-CHUNK = 512
-HALF = CHUNK // 2
+BANK = 512
+CHUNK = 256
+CHUNKS = J // CHUNK
 BLOCKS = CHUNK // P
+WOVEN = CHUNK * PACK
 ROW_TILES = N // P
 RUN = 4
 LIST_ROWS = 16
 
+BOTH = 2
 KIB = 1024
-AT_PAGE2 = 0
-AT_HI = 6 * KIB
-AT_TOTAL00 = 8 * KIB
-AT_HI_B1 = 10 * KIB
-AT_LO_B1 = AT_HI_B1 + 3 * KIB
-AT_DECODED_B1 = 19 * KIB
-AT_TOTAL_B00 = 25 * KIB
-AT_TOTAL_B01 = AT_TOTAL_B00 - KIB // 2
-AT_R_B1 = AT_TOTAL_B00 + KIB // 2
-AT_DECODED = 28 * KIB
-AT_TURNED_RES001 = AT_DECODED + 8 * KIB
-AT_TOTAL02 = AT_TURNED_RES001 + KIB // 2
-AT_TOTAL03 = AT_TOTAL02 - 3 * KIB // 2
-AT_R_B0_SC = AT_TOTAL02 + KIB // 2
-AT_TURNED_RES000 = AT_TOTAL02 + 2 * KIB
-AT_PLANES_B1 = AT_TURNED_RES000 - 3 * KIB // 4
-AT_R_B0 = AT_TURNED_RES000 + KIB // 4
+AT_DECODED21 = 0
+AT_DECODED31 = 4 * KIB
+AT_LO0 = 8 * KIB
+AT_HI1 = AT_LO0 + 4 * KIB
+AT_LO1 = 16 * KIB
+AT_ONES = AT_LO1 + 4 * KIB
+AT_TOTAL01 = AT_ONES + 64 - KIB
+AT_TURNED_DX0 = AT_ONES + 64
+AT_HI2 = 22 * KIB
+AT_ONE = AT_HI2 + 4 * KIB
+AT_TOTAL02 = AT_ONE + 64 - KIB
 
 
 def tile_list_embg_tgq8_res_kernel(tc, dy, w_words, w_scales, res, wgo, offs, out):
@@ -54,18 +51,12 @@ def tile_list_embg_tgq8_res_kernel(tc, dy, w_words, w_scales, res, wgo, offs, ou
         keep = ctx.enter_context(tc.tile_pool(name="keep", bufs=1))
         laid = ctx.enter_context(tc.tile_pool(name="laid", bufs=1))
         psum = ctx.enter_context(tc.psum_pool(name="psum", bufs=1))
-        banks = [psum.tile([P, CHUNK], F32, name=f"bank{b}") for b in range(8)]
+        banks = [psum.tile([P, BANK], F32, name=f"bank{b}") for b in range(8)]
 
-        def sb(name, shape, dtype, tag=None, offset=None):
-            if offset is None:
-                return keep.tile(shape, dtype, name=name, tag=tag or name, align_bytes=64)
-            return laid.tile(shape, dtype, name=name, tag=name, align_bytes=64, offset=offset)
-
-        def load_dy(name, a, j0, width):
-            raw = sb(name, [P, PACK, width], F32)
-            rows = dy[a * K_PASS : (a + 1) * K_PASS, j0 : j0 + width]
-            nc.sync.dma_start(out=raw[:], in_=rows.rearrange("(p t) j -> p t j", t=PACK))
-            return raw
+        def sb(name, shape, dtype, at=None):
+            if isinstance(at, int):
+                return laid.tile(shape, dtype, name=name, tag=name, align_bytes=64, offset=at)
+            return keep.tile(shape, dtype, name=name, tag=at or name, align_bytes=64)
 
         def woven(dst):
             return dst.rearrange("p (c i t) -> p c t i", i=RUN, t=PACK)
@@ -73,45 +64,46 @@ def tile_list_embg_tgq8_res_kernel(tc, dy, w_words, w_scales, res, wgo, offs, ou
         def by_runs(planes):
             return planes.rearrange("p t (c i) -> p c t i", i=RUN)
 
-        def halves(tile, h):
-            return tile[:, h * HALF * PACK : (h + 1) * HALF * PACK]
-
         w_sc = sb("w_sc", [P, PASSES, N], U8)
         nc.gpsimd.memset(w_sc[:].rearrange("p a n -> p (a n)").bitcast(I32), 0)
-        ones = sb("ones", [P, P], F32)
+        quadrant = sb("quadrant", [P, 1], F32)
+        for q in range(4):
+            nc.gpsimd.memset(quadrant[32 * q : 32 * q + 32, :], float(32 * q))
+        one_b = sb("one_b", [P, 1], F32, AT_ONE)
+        nc.gpsimd.memset(one_b[:], 1.0)
+        ones = sb("ones", [P, P], F32, AT_ONES)
         nc.vector.memset(ones[:], 1.0)
         column = sb("column", [P, P], F32)
         nc.vector.tensor_tensor_scan(column[:], ones[:], ones[:], -1.0, ALU.mult, ALU.add)
         in_quadrant = sb("in_quadrant", [P, 32], F32)
         nc.vector.transpose(in_quadrant[:], column[:, 0:32])
-        quadrant = sb("quadrant", [P, 1], F32)
-        for q in range(4):
-            nc.gpsimd.memset(quadrant[32 * q : 32 * q + 32, :], float(32 * q))
+        eye32 = sb("eye32", [P, P], F32)
+        nc.vector.tensor_scalar(eye32[:], column[:], quadrant[:], in_quadrant[:, 0:1], ALU.subtract, ALU.is_equal)
         eye_rows = sb("eye_in", [P, PACK * (K_PASS + 1)], BF16)
         nc.vector.memset(eye_rows[:].bitcast(I32), 0)
         diagonals = eye_rows[:].rearrange("p (t x) -> p t x", t=PACK)[:, :, 0:K_PASS:PACK]
-        nc.vector.tensor_scalar(
-            diagonals,
-            column[:].unsqueeze(1).to_broadcast([P, PACK, P]),
-            quadrant[:],
-            in_quadrant[:, 0:1],
-            ALU.subtract,
-            ALU.is_equal,
-        )
+        nc.scalar.copy(out=diagonals, in_=eye32[:].unsqueeze(1).to_broadcast([P, PACK, P]))
         eye_codes = sb("eye_codes", [P, K_PASS], U32)
         eye_sc = sb("eye_sc", [P, K_PASS], U8)
-        nc.vector.quantize_mx(
-            out=eye_codes[:].bitcast(E4M3), scales=eye_sc[:], in_=eye_rows[:, 0 : PACK * K_PASS]
-        )
-        eye32 = sb("eye32", [P, P], F32)
-        nc.vector.tensor_scalar(eye32[:], column[:], quadrant[:], in_quadrant[:, 0:1], ALU.subtract, ALU.is_equal)
 
-        pieces = [load_dy("raw_a00", 0, 0, HALF)]
-        wgo_rows = sb("wgo_rows", [P, P], F32)
-        nc.sync.dma_start(out=wgo_rows[:], in_=wgo[0 : P * P // J, :].rearrange("r (c j) -> (r c) j", j=P))
-        pieces.extend(load_dy(f"raw_a{a}{h}", a, h * HALF, HALF) for a, h in ((0, 1), (1, 0), (1, 1)))
-        raw_b = [[load_dy(f"raw_b0{a}", a, CHUNK, HALF) for a in range(PASSES)]]
-        raw_b.append([load_dy("raw_b10", 0, CHUNK + HALF, HALF)])
+        raw, res_sb = {}, {}
+
+        def load_dy(c, a):
+            raw[c, a] = sb(f"raw{c}{a}", [P, PACK, CHUNK], F32)
+            rows = dy[a * K_PASS : (a + 1) * K_PASS, c * CHUNK : (c + 1) * CHUNK]
+            nc.sync.dma_start(out=raw[c, a][:], in_=rows.rearrange("(p t) j -> p t j", t=PACK))
+
+        def load_res(c0, c1, r0, r1):
+            tile = sb(f"res{c0}{r0}", [P, r1 - r0, (c1 - c0) * CHUNK], F32)
+            src = res[r0 * P : r1 * P, c0 * CHUNK : c1 * CHUNK]
+            nc.sync.dma_start(out=tile[:], in_=src.rearrange("(i p) j -> p i j", p=P))
+            for c in range(c0, c1):
+                for r in range(r0, r1):
+                    res_sb[c, r] = tile[:, r - r0, (c - c0) * CHUNK : (c - c0 + 1) * CHUNK]
+
+        for c in range(2):
+            for a in range(PASSES):
+                load_dy(c, a)
         w_codes = sb("w_codes", [P, PASSES, N], U32)
         nc.sync.dma_start(
             out=w_codes[:].bitcast(I32),
@@ -122,358 +114,356 @@ def tile_list_embg_tgq8_res_kernel(tc, dy, w_words, w_scales, res, wgo, offs, ou
                 out=w_sc[32 * q : 32 * q + 4, :, :].bitcast(I32),
                 in_=w_scales[:, 4 * q : 4 * q + 4, :].rearrange("a r n -> r a n").bitcast(I32),
             )
-        res_sb = {}
-        wgo_sb = []
-
-        def load_res(c, r):
-            res_sb[c, r] = sb(f"res{c}{r}", [P, CHUNK], F32)
-            nc.sync.dma_start(out=res_sb[c, r][:], in_=res[r * P : (r + 1) * P, c * CHUNK : (c + 1) * CHUNK])
-
-        def load_wgo(c):
-            wgo_sb.append(sb(f"wgo{c}", [P, CHUNK], F32))
-            nc.sync.dma_start(out=wgo_sb[c][:], in_=wgo[:, c * CHUNK : (c + 1) * CHUNK])
-
-        raw_b[1].append(load_dy("raw_b11", 1, CHUNK + HALF, HALF))
+        load_res(0, 1, 0, 2)
+        wgo_rows = sb("wgo_rows", [P, P], F32)
+        nc.sync.dma_start(out=wgo_rows[:], in_=wgo[0 : P * P // J, :].rearrange("r (c j) -> (r c) j", j=P))
+        wgo0 = sb("wgo0", [P, CHUNK], F32)
+        nc.sync.dma_start(out=wgo0[:], in_=wgo[:, 0:CHUNK])
         offsets = keep.tile([P, J // LIST_ROWS], U16, name="offsets")
         nc.sync.dma_start(offsets[:], offs)
-        load_res(0, 0)
-        load_wgo(0)
-        for r in range(1, ROW_TILES):
-            load_res(0, r)
-        res_b = {}
-        for rows in ((0,), (1, 2, 3)):
-            for h in range(2):
-                tile = sb(f"res_b{h}{rows[0]}", [P, len(rows), HALF], F32)
-                src = res[rows[0] * P : (rows[-1] + 1) * P, CHUNK + h * HALF : CHUNK + (h + 1) * HALF]
-                nc.sync.dma_start(out=tile[:], in_=src.rearrange("(i p) j -> p i j", p=P))
-                for i, r in enumerate(rows):
-                    res_b[h, r] = tile[:, i, :]
+        load_dy(2, 0)
+        load_dy(2, 1)
+        load_res(0, 1, 2, ROW_TILES)
+        load_dy(3, 0)
+        load_res(1, 2, 0, ROW_TILES)
+        load_dy(3, 1)
+        load_res(2, CHUNKS, 0, ROW_TILES)
 
-        def operand(name, tag=None, offset=None, scale_tag=None, scale_offset=None):
-            return sb(name + "_codes", [P, CHUNK], U32, tag, offset), sb(name + "_sc", [P, CHUNK], U8, scale_tag, scale_offset)
+        hi, lo, first, second, decoded, turned_res, turned_dx, totals, pages = {}, {}, {}, {}, {}, {}, {}, {}, []
 
-        def quantise(q, src, fmt, j0=0, j1=CHUNK):
-            nc.vector.quantize_mx(out=q[0][:, j0:j1].bitcast(fmt), scales=q[1][:, j0:j1], in_=src)
+        def part(pieces, a, j0=0, j1=CHUNK):
+            return pieces[a][:, j0 * PACK : j1 * PACK]
 
-        def decode(bank, t, q, j0=0):
+        def woven_pair(name, at=None):
+            tile = sb(name, [P, PASSES * WOVEN], BF16, at)
+            return tile[:, 0:WOVEN], tile[:, WOVEN:], tile[:]
+
+        def operand(name, columns, at=None, scale_at=None):
+            return sb(name + "_codes", [P, columns], U32, at)[:], sb(name + "_sc", [P, columns], U8, scale_at)[:]
+
+        def operand_pair(name, at=None, scale_at=None):
+            codes, scales = operand(name, PASSES * CHUNK, at, scale_at)
+            return (codes[:, 0:CHUNK], scales[:, 0:CHUNK]), (codes[:, CHUNK:], scales[:, CHUNK:]), (codes, scales)
+
+        def cast(engine, c, a, j0=0, j1=CHUNK, one=1.0):
+            dst, src = woven(part(hi[c], a, j0, j1)), by_runs(raw[c, a][:, :, j0:j1])
+            if engine == "scalar":
+                nc.scalar.activation(dst, src, COPY, scale=one)
+            elif engine == "vector":
+                nc.vector.tensor_copy(out=dst, in_=src)
+            else:
+                nc.gpsimd.tensor_scalar(
+                    part(hi[c], a, j0, j1).rearrange("p (j t) -> p j t", t=PACK),
+                    raw[c, a][:, :, j0:j1].rearrange("p t j -> p j t"),
+                    one,
+                    0.0,
+                    ALU.mult,
+                    ALU.add,
+                )
+
+        def quantise(q, src, fmt, a):
+            nc.vector.quantize_mx(out=q[a][0].bitcast(fmt), scales=q[a][1], in_=src[a])
+
+        def decode(into, t, q, j0, j1):
             cols = slice(t * P, (t + 1) * P)
             nc.tensor.matmul_mx(
-                out=bank[:],
+                out=into,
                 lhsT=eye_codes[:, cols].bitcast(E4M3),
                 lhsT_scale=eye_sc[:, cols],
-                rhs=q[0][:, j0 : j0 + CHUNK].bitcast(E5M2),
-                rhs_scale=q[1][:, j0 : j0 + CHUNK],
+                rhs=q[0][:, j0:j1].bitcast(E5M2),
+                rhs_scale=q[1][:, j0:j1],
                 start=True,
                 stop=True,
             )
 
-        def product(bank, r, a, q, fmt, start, stop, j0=0, j1=CHUNK, base=0):
-            cols = slice(r * P, (r + 1) * P)
-            nc.tensor.matmul_mx(
-                out=bank[:, j0:j1],
-                lhsT=w_codes[:, a, cols].bitcast(E4M3),
-                lhsT_scale=w_sc[:, a, cols],
-                rhs=q[0][:, base + j0 : base + j1].bitcast(fmt),
-                rhs_scale=q[1][:, base + j0 : base + j1],
-                start=start,
-                stop=stop,
+        def decode_block(bank, c, a, b):
+            for t in range(PACK):
+                decode(bank[:, t * P : (t + 1) * P], t, first[c][a], b * P, (b + 1) * P)
+
+        def subtract_block(bank, c, a, b):
+            nc.vector.tensor_tensor(
+                woven(part(lo[c], a, b * P, (b + 1) * P)),
+                by_runs(raw[c, a][:, :, b * P : (b + 1) * P]),
+                by_runs(bank[:].rearrange("p (t j) -> p t j", t=PACK)),
+                ALU.subtract,
             )
 
-        pages = []
+        def copy_decoded(bank, c, a, b, at=None):
+            if b == 0:
+                decoded[c, a] = sb(f"decoded{c}{a}", [P, BLOCKS, BANK], F32, at)
+            nc.scalar.copy(out=decoded[c, a][:, b, :], in_=bank[:])
 
-        def clear_page(tag=None, offset=None, engine=nc.gpsimd):
-            page = sb(f"page{len(pages)}", [P, T], F32, tag, offset)
-            engine.memset(page[:], 0.0)
+        def subtract_on_gpsimd(c, a, b):
+            nc.gpsimd.tensor_tensor(
+                woven(part(lo[c], a, b * P, (b + 1) * P)),
+                by_runs(raw[c, a][:, :, b * P : (b + 1) * P]),
+                by_runs(decoded[c, a][:, b, :].rearrange("p (t j) -> p t j", t=PACK)),
+                ALU.subtract,
+            )
+
+        def add_on_vector(r, bank, at=None):
+            totals[0, r] = sb(f"total0{r}", [P, CHUNK], F32, at)[:]
+            nc.vector.tensor_tensor(totals[0, r], bank[:, 0:CHUNK], res_sb[0, r], ALU.add)
+
+        def scatter_times_wgo(r):
+            places = pages[r][:].indirect(offsets[:, 0 : CHUNK // LIST_ROWS])
+            nc.vector.tensor_tensor(places, totals[0, r], wgo0[:], ALU.mult)
+
+        def product(pair, q, fmt, terms, start=(), stop=()):
+            for a, b in terms:
+                cols = slice(b * P, (b + 1) * P)
+                nc.tensor.matmul_mx(
+                    out=pair[b][:],
+                    lhsT=q[a][0][:, cols].bitcast(fmt),
+                    lhsT_scale=q[a][1][:, cols],
+                    rhs=w_codes[:, a, :].bitcast(E4M3),
+                    rhs_scale=w_sc[:, a, :],
+                    start=a in start,
+                    stop=a in stop,
+                )
+
+        def product_last_row(bank):
+            terms = [(q, fmt, a, b) for q, fmt in ((first[0], E5M2), (second[0], E4M3)) for a, b in in_order]
+            for n, (q, fmt, a, b) in enumerate(terms):
+                cols = slice(b * P, (b + 1) * P)
+                nc.tensor.matmul_mx(
+                    out=bank[:, cols],
+                    lhsT=q[a][0][:, cols].bitcast(fmt),
+                    lhsT_scale=q[a][1][:, cols],
+                    rhs=w_codes[:, a, N - P : N].bitcast(E4M3),
+                    rhs_scale=w_sc[:, a, N - P : N],
+                    start=n == 0,
+                    stop=n == len(terms) - 1,
+                )
+
+        def product_row(bank, r, q, fmt, start, stop):
+            for a in range(PASSES):
+                nc.tensor.matmul_mx(
+                    out=bank[:, 0:CHUNK],
+                    lhsT=w_codes[:, a, r * P : (r + 1) * P].bitcast(E4M3),
+                    lhsT_scale=w_sc[:, a, r * P : (r + 1) * P],
+                    rhs=q[a][0].bitcast(fmt),
+                    rhs_scale=q[a][1],
+                    start=start and a == 0,
+                    stop=stop and a == PASSES - 1,
+                )
+
+        def weighted(name, c, b, src, r0, r1, into, place=None):
+            tile = sb(name, [P, (r1 - r0) * P], F32)[:] if place is None else place
+            column = c * BLOCKS + b
+            nc.scalar.activation(tile, src, COPY, scale=wgo_col[:, column : column + 1])
+            for r in range(r0, r1):
+                into[c, b, r] = tile[:, (r - r0) * P : (r - r0 + 1) * P]
+
+        def turn_res(c, b, bank, r0=0, r1=ROW_TILES):
+            for r in range(r0, r1):
+                nc.tensor.transpose(bank[:, r * P : (r + 1) * P], res_sb[c, r][:, b * P : (b + 1) * P], eye32[:])
+
+        def take_res(c, b, bank, r0=0, r1=ROW_TILES, place=None):
+            weighted(f"turned_res{c}{b}{r0}", c, b, bank[:, r0 * P : r1 * P], r0, r1, turned_res, place)
+
+        def take_dx(c, b, bank, r0=0, r1=ROW_TILES, place=None):
+            weighted(f"turned_dx{c}{b}{r0}", c, b, bank[:, r0 * P : r1 * P], r0, r1, turned_dx, place)
+
+        def turn_back(c, r, bank):
+            terms = [(src[c, b, r], b) for src in (turned_res, turned_dx) for b in range(BLOCKS)]
+            for n, (tile, b) in enumerate(terms):
+                nc.tensor.matmul(
+                    bank[:, b * P : (b + 1) * P],
+                    lhsT=tile,
+                    rhs=eye32[:],
+                    is_transpose=True,
+                    start=n == 0,
+                    stop=n == len(terms) - 1,
+                )
+
+        def fetch(c, r, bank, at=None, into=None):
+            totals[c, r] = sb(f"total{c}{r}", [P, CHUNK], F32, at)[:] if into is None else into
+            nc.scalar.copy(out=totals[c, r], in_=bank[:, 0:CHUNK])
+
+        def clear_page(engine, pieces, at=None):
+            page = sb(f"page{len(pages)}", [P, T], F32, at)
+            for n in range(pieces):
+                engine.memset(page[:, n * T // pieces : (n + 1) * T // pieces], 0.0)
             pages.append(page)
 
-        def places(c, r):
+        def scatter(c, r, values=None, chunks=1):
             columns = CHUNK // LIST_ROWS
-            return pages[r][:].indirect(offsets[:, c * columns : (c + 1) * columns])
-
-        def scatter_times_wgo(c, r, total):
-            nc.vector.tensor_tensor(places(c, r), total[:], wgo_sb[c][:], ALU.mult)
-
-        def scatter_weighted(c, r, total):
-            nc.vector.tensor_copy(places(c, r), total[:])
-
-        def add_on_vector(c, r, bank, offset=None):
-            total = sb(f"total{c}{r}", [P, CHUNK], F32, offset=offset)
-            nc.vector.tensor_tensor(total[:], bank[:], res_sb[c, r][:], ALU.add)
-            return total
-
-        def to_sbuf(name, bank, tag=None, offset=None):
-            tile = sb(name, [P, CHUNK], F32, tag, offset)
-            nc.scalar.copy(out=tile[:], in_=bank[:])
-            return tile
-
-        def add_on_tensor(c, r, dx, sum_bank, back_bank, offset=None):
-            terms = [(src, b) for src in (res_sb[c, r], dx) for b in range(BLOCKS)]
-            for i, (src, b) in enumerate(terms):
-                cols = slice(b * P, (b + 1) * P)
-                nc.tensor.matmul(
-                    sum_bank[:, cols],
-                    lhsT=src[:, cols],
-                    rhs=eye32[:],
-                    is_transpose=True,
-                    start=(i == 0),
-                    stop=(i == len(terms) - 1),
-                )
-            turned = sb(f"turned{c}{r}", [P, CHUNK], F32, offset=offset)
-            if c == 0:
-                for b in range(BLOCKS):
-                    cols = slice(b * P, (b + 1) * P)
-                    nc.scalar.activation(turned[:, cols], sum_bank[:, cols], COPY, scale=wgo_col[:, b : b + 1])
-            else:
-                nc.scalar.copy(out=turned[:], in_=sum_bank[:])
-            for b in range(BLOCKS):
-                cols = slice(b * P, (b + 1) * P)
-                nc.tensor.transpose(back_bank[:, cols], turned[:, cols], eye32[:])
-
-        nc.tensor.transpose(banks[7][:, 0:P], wgo_rows[:], eye32[:])
-        wgo_col = sb("wgo_col", [P, J // P], F32)
-        nc.vector.tensor_copy(out=wgo_col[:], in_=banks[7][:, 0 : J // P])
-        clear_page(engine=nc.vector)
-        q_a = (sb("q_a_codes", [P, 5 * HALF], U32), sb("q_a_sc", [P, 5 * HALF], U8))
-        nc.gpsimd.memset(q_a[0][:, 0:HALF], 0)
-        nc.gpsimd.memset(q_a[1][:, 0:HALF].bitcast(I32), 0)
-        hi_a0 = sb("hi_a0", [P, HALF * PACK], BF16)
-        shared = sb("shared", [P, CHUNK + CHUNK * PACK], BF16)
-        hi_a12 = shared[:, CHUNK:]
-        planes_a0 = shared[:, 0 : PACK * HALF].rearrange("p (t j) -> p t j", t=PACK)
-        hi_a3 = sb("hi_a3", [P, HALF * PACK], BF16, offset=AT_HI)
-        lo_a0 = sb("lo_a0", [P, CHUNK * PACK], BF16)
-        lo_a1 = [sb(f"lo_a1{h}", [P, HALF * PACK], BF16) for h in range(2)]
-        lo_pieces = [halves(lo_a0, 0), halves(lo_a0, 1), lo_a1[0][:], lo_a1[1][:]]
-        nc.scalar.copy(out=woven(hi_a0[:]), in_=by_runs(pieces[0][:]))
-        nc.scalar.copy(out=woven(halves(hi_a12, 0)), in_=by_runs(pieces[1][:]))
-        nc.scalar.copy(out=woven(halves(hi_a12, 1)), in_=by_runs(pieces[2][:]))
-        nc.scalar.copy(out=woven(hi_a3[:]), in_=by_runs(pieces[3][:]))
-
-        def subtract_piece(i, bank0, side, planes, ts):
-            for t in ts:
-                decoded = banks[bank0 + t][:, side * HALF : (side + 1) * HALF]
-                nc.vector.tensor_tensor(planes[:, t, :], pieces[i][:, t, :], decoded, ALU.subtract)
-
-        def leftover_piece(i, bank0, side, offset=None):
-            planes = sb(f"pl_a{i // 2}{i % 2}", [P, PACK, HALF], BF16, offset=offset)
-            subtract_piece(i, bank0, side, planes, range(PACK))
-            nc.scalar.copy(out=woven(lo_pieces[i]), in_=by_runs(planes[:]))
-
-        quantise(q_a, hi_a0[:], E5M2, HALF, 2 * HALF)
-        clear_page("hi_a0")
-        for t in range(PACK):
-            decode(banks[t], t, q_a, 0)
-        subtract_piece(0, 0, 1, planes_a0, (0, 1))
-        quantise(q_a, hi_a12, E5M2, 2 * HALF, 4 * HALF)
-        subtract_piece(0, 0, 1, planes_a0, (2, 3))
-        nc.scalar.copy(out=woven(lo_pieces[0]), in_=by_runs(planes_a0))
-        for t in range(PACK):
-            decode(banks[4 + t], t, q_a, 2 * HALF)
-        quantise(q_a, hi_a3[:], E5M2, 4 * HALF, 5 * HALF)
-        hi_b0 = sb("hi_b0", [P, CHUNK * PACK], BF16, offset=AT_HI)
-        for h in range(2):
-            nc.gpsimd.tensor_scalar(
-                halves(hi_b0, h).rearrange("p (j t) -> p j t", t=PACK),
-                raw_b[0][h][:].rearrange("p t j -> p j t"),
-                1.0,
-                0.0,
-                ALU.mult,
-                ALU.add,
-            )
-        for t in range(PACK):
-            decode(banks[t], t, q_a, 3 * HALF)
-        leftover_piece(1, 4, 0)
-        leftover_piece(2, 4, 1)
-        leftover_piece(3, 0, 1, AT_HI_B1)
-        r_a = [operand(f"r_a{a}") for a in range(PASSES)]
-        quantise(r_a[0], lo_a0[:], E4M3)
-        quantise(r_a[1], lo_a1[0][:], E4M3, 0, HALF)
-        quantise(r_a[1], lo_a1[1][:], E4M3, HALF, CHUNK)
-
-        passes_a = [
-            (0, q_a, E5M2, 0, CHUNK, HALF),
-            (1, q_a, E5M2, 0, CHUNK, 3 * HALF),
-            (0, r_a[0], E4M3, 0, CHUNK, 0),
-            (1, r_a[1], E4M3, 0, HALF, 0),
-            (1, r_a[1], E4M3, HALF, CHUNK, 0),
-        ]
-
-        def product_a(rows, passes):
-            for i, (a, q, fmt, j0, j1, base) in enumerate(passes):
-                for r in rows:
-                    product(banks[4 + r], r, a, q, fmt, i == 0, i == len(passes) - 1, j0, j1, base)
-
-        product_a((0, 1), passes_a)
-        q_b = [operand("q_b0", tag="lo_a11")]
-        quantise(q_b[0], hi_b0[:], E5M2)
-        clear_page(offset=AT_PAGE2)
-        total = add_on_vector(0, 0, banks[4], AT_TOTAL00)
-        clear_page("res00")
-        scatter_times_wgo(0, 0, total)
-
-        def copy_decoded(name, j0, j1, offset):
-            tile = sb(name, [P, PACK, j1 - j0], F32, offset=offset)
-            for t in range(PACK):
-                nc.scalar.copy(out=tile[:, t, :], in_=banks[t][:, j0:j1])
-            return tile[:]
-
-        def woven_part(lo, a, j0, j1):
-            return woven(lo[:, (a * HALF + j0) * PACK : (a * HALF + j1) * PACK])
-
-        def subtract_on_gpsimd(h, lo, decoded):
-            for a in range(PASSES):
-                width = decoded[a].shape[2]
-                nc.gpsimd.tensor_tensor(
-                    woven_part(lo, a, 0, width),
-                    by_runs(raw_b[h][a][:, :, 0:width]),
-                    by_runs(decoded[a]),
-                    ALU.subtract,
-                )
-
-        def product_b(into, q, fmt, first):
-            for b in range(2):
-                for a in range(PASSES):
-                    cols = slice(a * HALF + b * P, a * HALF + (b + 1) * P)
-                    nc.tensor.matmul_mx(
-                        out=into[b][:],
-                        lhsT=q[0][:, cols].bitcast(fmt),
-                        lhsT_scale=q[1][:, cols],
-                        rhs=w_codes[:, a, :].bitcast(E4M3),
-                        rhs_scale=w_sc[:, a, :],
-                        start=first and a == 0,
-                        stop=not first and a == PASSES - 1,
-                    )
-
-        def weighted(name, h, b, src, offset=None):
-            tile = sb(name, [P, src.shape[1]], F32, offset=offset)
-            at = BLOCKS + 2 * h + b
-            nc.scalar.activation(tile[:], src, COPY, scale=wgo_col[:, at : at + 1])
-            return tile
-
-        def turn_back(bank, terms, start, stop):
-            for n, (tile, at_tile, at_bank) in enumerate(terms):
-                nc.tensor.matmul(
-                    bank[:, at_bank : at_bank + P],
-                    lhsT=tile[:, at_tile : at_tile + P],
-                    rhs=eye32[:],
-                    is_transpose=True,
-                    start=start and n == 0,
-                    stop=stop and n == len(terms) - 1,
-                )
-
-        turned_res = {}
-
-        def turn_res(h, b, rows, through, offset=None):
-            for i, r in enumerate(rows):
-                nc.tensor.transpose(through[:, i * P : (i + 1) * P], res_b[h, r][:, b * P : (b + 1) * P], eye32[:])
-            return lambda: weigh_res(h, b, rows, through, offset)
-
-        def weigh_res(h, b, rows, through, offset):
-            tile = weighted(f"turned_res{h}{rows[0]}{b}", h, b, through[:, 0 : len(rows) * P], offset)
-            for i, r in enumerate(rows):
-                turned_res[h, r, b] = (tile, i * P, r % 2 * HALF + b * P)
-
-        def open_rows(h, rows, bank):
-            turn_back(bank, [turned_res[h, r, b] for b in range(2) for r in rows], True, False)
-
-        def add_rows(h, rows, bank, sources):
-            cols = slice(rows[0] * P, (rows[-1] + 1) * P)
-            dx_turned = [weighted(f"dx_b{h}{rows[0]}{b}", h, b, sources[b][:, cols]) for b in range(2)]
-            dx_terms = [(dx_turned[b], (r - rows[0]) * P, r % 2 * HALF + b * P) for b in range(2) for r in rows]
-            turn_back(bank, dx_terms, False, True)
-
-        totals = {}
-
-        def fetch(h, r, bank, tag=None, offset=None):
-            totals[h, r] = sb(f"total_b{h}{r}", [P, HALF], F32, tag, offset)
-            nc.scalar.copy(out=totals[h, r][:], in_=bank[:, (r % 2) * HALF : (r % 2 + 1) * HALF])
-
-        def scatter_b(h, r):
-            columns = HALF // LIST_ROWS
-            first = (CHUNK + h * HALF) // LIST_ROWS
-            nc.vector.tensor_copy(pages[r][:].indirect(offsets[:, first : first + columns]), totals[h, r][:])
-            if h == 1:
+            places = pages[r][:].indirect(offsets[:, c * columns : (c + chunks) * columns])
+            nc.vector.tensor_copy(places, totals[c, r] if values is None else values)
+            if c + chunks == CHUNKS:
                 nc.sync.dma_start(out=out[r * P : (r + 1) * P, :], in_=pages[r][:])
 
-        dx = to_sbuf("dx01", banks[5], offset=AT_DECODED)
-        hi_b1 = sb("hi_b1", [P, CHUNK * PACK], BF16, offset=AT_HI_B1)
-        for a in range(PASSES):
-            nc.scalar.copy(out=woven(halves(hi_b1, a)), in_=by_runs(raw_b[1][a][:]))
-        q_b.append(operand("q_b1", offset=AT_TOTAL00))
-        quantise(q_b[1], hi_b1[:], E5M2)
-        add_on_tensor(0, 1, dx, banks[5], banks[7], AT_DECODED + 4 * KIB)
-        total = to_sbuf("total01", banks[7])
-        product_a((2,), passes_a[::-1])
-        dx = to_sbuf("dx02", banks[6], offset=AT_DECODED_B1)
-        for t in range(PACK):
-            decode(banks[t], t, q_b[0])
-        lo_b0 = sb("lo_b0", [P, CHUNK * PACK], BF16, offset=AT_HI_B1)
-        decoded_b0 = [copy_decoded("dec_b00", 0, HALF, AT_DECODED)]
-        scatter_weighted(0, 1, total)
-        add_on_tensor(0, 2, dx, banks[4], banks[5])
-        total = to_sbuf("total02", banks[5], offset=AT_TOTAL02)
-        decoded_b0.append(copy_decoded("dec_b01", HALF, CHUNK, AT_DECODED + 4 * KIB))
-        subtract_on_gpsimd(0, lo_b0, decoded_b0)
-        product_a((3,), passes_a[::-1])
-        scatter_weighted(0, 2, total)
-        add_on_tensor(0, 3, to_sbuf("dx03", banks[7]), banks[6], banks[7])
-        for t in range(PACK):
-            decode(banks[t], t, q_b[1])
-        decoded = copy_decoded("dec_b1", 0, HALF + P, AT_DECODED_B1)
-        decoded_b1 = [decoded[:, :, 0:HALF], decoded[:, :, HALF:]]
-        firsts = [(1, 0, None), (1, 1, None), (0, 0, AT_TURNED_RES000), (0, 1, AT_TURNED_RES001)]
-        for weigh in [
-            turn_res(h, b, (0,), banks[4][:, i * P : (i + 1) * P], at) for i, (h, b, at) in enumerate(firsts)
-        ]:
-            weigh()
-        open_rows(0, (0,), banks[6])
-        planes_b1 = sb("pl_b1", [P, PACK, P], BF16, offset=AT_PLANES_B1)
-        for t in range(PACK):
-            nc.vector.tensor_tensor(
-                planes_b1[:, t, :], raw_b[1][1][:, t, P:HALF], banks[t][:, HALF + P : CHUNK], ALU.subtract
-            )
-        product_b(banks[4:6], q_b[0], E5M2, True)
-        r_b = [operand("r_b0", offset=AT_R_B0, scale_offset=AT_R_B0_SC)]
-        quantise(r_b[0], lo_b0[:], E4M3)
-        total = to_sbuf("total03", banks[7], offset=AT_TOTAL03)
-        product_b(banks[4:6], r_b[0], E4M3, False)
-        lo_b1 = sb("lo_b1", [P, CHUNK * PACK], BF16, offset=AT_LO_B1)
-        subtract_on_gpsimd(1, lo_b1, decoded_b1)
-        scatter_weighted(0, 3, total)
-        add_rows(0, (0,), banks[6], banks[4:6])
-        fetch(0, 0, banks[6], offset=AT_TOTAL_B00)
-        nc.scalar.copy(out=woven_part(lo_b1, 1, P, HALF), in_=by_runs(planes_b1[:]))
-        for b in range(2):
-            turn_res(0, b, (1, 2, 3), banks[b])()
-        open_rows(0, (2, 3), banks[7])
-        add_rows(0, (2, 3), banks[7], banks[4:6])
-        open_rows(0, (1,), banks[6])
-        add_rows(0, (1,), banks[6], banks[4:6])
-        open_rows(1, (0,), banks[2])
-        product_b(banks[4:6], q_b[1], E5M2, True)
-        scatter_b(0, 0)
-        r_b.append(operand("r_b1", offset=AT_R_B1, scale_tag="dx_b021"))
-        quantise(r_b[1], lo_b1[:], E4M3)
-        fetch(0, 1, banks[6], offset=AT_TOTAL_B01)
-        fetch(0, 2, banks[7], offset=AT_LO_B1)
-        product_b(banks[4:6], r_b[1], E4M3, False)
-        scatter_b(0, 1)
-        scatter_b(0, 2)
-        add_rows(1, (0,), banks[2], banks[4:6])
-        fetch(1, 0, banks[2])
-        for b in range(2):
-            turn_res(1, b, (1, 2, 3), banks[b])()
-        open_rows(1, (1,), banks[2])
-        add_rows(1, (1,), banks[2], banks[4:6])
-        fetch(1, 1, banks[2])
-        open_rows(1, (2, 3), banks[3])
-        add_rows(1, (2, 3), banks[3], banks[4:6])
-        scatter_b(1, 0)
-        scatter_b(1, 1)
-        fetch(1, 2, banks[3])
-        scatter_b(1, 2)
-        total = sb("total13", [P, CHUNK], F32)
-        for h, bank in enumerate((banks[7], banks[3])):
-            nc.scalar.copy(out=total[:, h * HALF : (h + 1) * HALF], in_=bank[:, HALF:CHUNK])
-        scatter_weighted(1, 3, total)
-        nc.sync.dma_start(out=out[3 * P : 4 * P, :], in_=pages[3][:])
+        both = [(a, b) for b in range(BLOCKS) for a in range(PASSES)]
+        blocks = range(BLOCKS)
+        in_order = [(a, b) for a in range(PASSES) for b in blocks]
+        hi[0], hi[1] = woven_pair("hi0"), woven_pair("hi1", AT_HI1)
+        lo[0], lo[1] = woven_pair("lo0", AT_LO0), woven_pair("lo1", AT_LO1)
+        first[0] = operand_pair("first0")
+        for c in range(CHUNKS):
+            second[c] = operand_pair(f"second{c}")
+
+        clear_page(nc.vector, 1, "column")
+        clear_page(nc.vector, 1, "in_quadrant")
+        cast("scalar", 0, 0, 0, P)
+        cast("vector", 0, 0, P, CHUNK)
+        nc.vector.quantize_mx(
+            out=eye_codes[:].bitcast(E4M3), scales=eye_sc[:], in_=eye_rows[:, 0 : PACK * K_PASS]
+        )
+        quantise(first[0], hi[0], E5M2, 0)
+        for b in blocks:
+            decode_block(banks[b], 0, 0, b)
+        cast("scalar", 0, 1, 0, P)
+        cast("vector", 0, 1, P, CHUNK)
+        quantise(first[0], hi[0], E5M2, 1)
+        for b in blocks:
+            decode_block(banks[2 + b], 0, 1, b)
+        cast("scalar", 1, 0)
+        cast("scalar", 1, 1)
+        clear_page(nc.gpsimd, 1, "hi0")
+        for a, b in in_order:
+            subtract_block(banks[2 * a + b], 0, a, b)
+        first[1] = operand_pair("first1", "raw00")
+        quantise(first[1], hi[1], E5M2, 0)
+        quantise(second[0], lo[0], E4M3, BOTH)
+        quantise(first[1], hi[1], E5M2, 1)
+        clear_page(nc.gpsimd, 1, AT_LO0)
+        for a, b in in_order:
+            decode_block(banks[4 + 2 * a + b], 1, a, b)
+        product(banks[2:4], first[1], E5M2, both, start=(0,))
+        for a, b in in_order:
+            subtract_block(banks[4 + 2 * a + b], 1, a, b)
+        for r in range(3):
+            product_row(banks[4 + r], r, first[0], E5M2, True, False)
+            product_row(banks[4 + r], r, second[0], E4M3, False, True)
+        add_on_vector(0, banks[4])
+        quantise(second[1], lo[1], E4M3, BOTH)
+        scatter_times_wgo(0)
+        hi[2] = woven_pair("hi2", AT_HI2)
+        cast("scalar", 2, 0)
+        nc.tensor.transpose(banks[7][:, 0:P], wgo_rows[:], eye32[:])
+        wgo_col = sb("wgo_col", [P, J // P], F32)
+        nc.scalar.copy(out=wgo_col[:], in_=banks[7][:, 0 : J // P])
+        cast("scalar", 2, 1, one=ones[:, 0:1])
+        product_last_row(banks[7])
+        product(banks[2:4], second[1], E4M3, both, stop=(1,))
+        for b in blocks:
+            turn_res(0, b, banks[b], 3, ROW_TILES)
+        add_on_vector(1, banks[5], AT_TOTAL01)
+        first[2] = operand_pair("first2", AT_LO1)
+        quantise(first[2], hi[2], E5M2, BOTH)
+        scatter_times_wgo(1)
+        turned_dx0 = sb("turned_dx0", [P, BLOCKS, P], F32, AT_TURNED_DX0)
+        for b in blocks:
+            weighted("turned_dx0", 0, b, banks[7][:, b * P : (b + 1) * P], 3, ROW_TILES, turned_dx, turned_dx0[:, b, :])
+        for b in blocks:
+            take_res(0, b, banks[b], 3, ROW_TILES)
+        turn_back(0, 3, banks[5])
+        decode_block(banks[7], 2, 0, 0)
+        decode_block(banks[4], 2, 0, 1)
+        for b in blocks:
+            turn_res(1, b, banks[b])
+        hi[3] = [sb("hi30", [P, WOVEN], BF16)[:]]
+        cast("scalar", 3, 0, one=one_b[:])
+        add_on_vector(2, banks[6], AT_TOTAL02)
+        first[3] = (operand("first30", CHUNK, AT_HI2), operand("first31", CHUNK, AT_DECODED21 + 2 * KIB, AT_DECODED21 + 3 * KIB))
+        quantise(first[3], hi[3], E5M2, 0)
+        scatter_times_wgo(2)
+        lo[2] = woven_pair("lo2", "hi30")
+        fetch(0, 3, banks[5])
+        scatter(0, 3)
+        copy_decoded(banks[7], 2, 0, 0)
+        subtract_on_gpsimd(2, 0, 0)
+        copy_decoded(banks[4], 2, 0, 1)
+        subtract_on_gpsimd(2, 0, 1)
+        for b in blocks:
+            decode_block(banks[6 + b], 2, 1, b)
+        for b in blocks:
+            take_dx(1, b, banks[2 + b], 0, 1)
+            take_res(1, b, banks[b], 0, 1)
+        turn_back(1, 0, banks[4])
+        take_dx(1, 0, banks[2], 1, ROW_TILES)
+        product(banks[2:4], first[2], E5M2, [(0, 0), (1, 0)], start=(0,))
+        fetch(1, 0, banks[4])
+        scatter(1, 0)
+        copy_decoded(banks[6], 2, 1, 0, AT_DECODED21)
+        subtract_on_gpsimd(2, 1, 0)
+        take_dx(1, 1, banks[3], 1, 2)
+        for b in blocks:
+            take_res(1, b, banks[b], 1, 2)
+        turn_back(1, 1, banks[5])
+        decode_block(banks[6], 3, 0, 0)
+        copy_decoded(banks[7], 2, 1, 1)
+        subtract_on_gpsimd(2, 1, 1)
+        fetch(1, 1, banks[5])
+        scatter(1, 1)
+        take_dx(1, 1, banks[3], 2, ROW_TILES)
+        for b in blocks:
+            take_res(1, b, banks[b], 2, ROW_TILES)
+        decode_block(banks[7], 3, 0, 1)
+        turn_back(1, 2, banks[4])
+        turn_back(1, 3, banks[5])
+        product(banks[2:4], first[2], E5M2, [(0, 1), (1, 1)], start=(0,))
+        for b in blocks:
+            turn_res(2, b, banks[b])
+        hi[3].append(sb("hi31", [P, WOVEN], BF16, "decoded20")[:])
+        cast("scalar", 3, 1)
+        quantise(second[2], lo[2], E4M3, BOTH)
+        quantise(first[3], hi[3], E5M2, 1)
+        fetch(1, 2, banks[4], AT_DECODED21)
+        scatter(1, 2)
+        product(banks[2:4], second[2], E4M3, both, stop=(1,))
+        lo[3] = woven_pair("lo3", "decoded20")
+        for b in blocks:
+            copy_decoded(banks[6 + b], 3, 0, b)
+            subtract_on_gpsimd(3, 0, b)
+        fetch(1, 3, banks[5], AT_DECODED21 + KIB)
+        for b in blocks:
+            decode_block(banks[6 + b], 3, 1, b)
+        scatter(1, 3)
+        subtract_block(banks[7], 3, 1, 1)
+        for b in blocks:
+            take_res(2, b, banks[b], 0, 1)
+        for b in blocks:
+            take_dx(2, b, banks[2 + b], 0, 1)
+        turn_back(2, 0, banks[4])
+        copy_decoded(banks[6], 3, 1, 0, AT_DECODED31)
+        subtract_on_gpsimd(3, 1, 0)
+        fetch(2, 0, banks[4])
+        scatter(2, 0)
+        for b in blocks:
+            take_dx(2, b, banks[2 + b], 1, ROW_TILES)
+        product(banks[2:4], first[3], E5M2, both, start=(0,))
+        for b in blocks:
+            take_res(2, b, banks[b], 1, ROW_TILES)
+        turn_back(2, 1, banks[4])
+        turn_back(2, 2, banks[5])
+        for b in blocks:
+            turn_res(3, b, banks[b])
+        quantise(second[3], lo[3], E4M3, BOTH)
+        fetch(2, 1, banks[4], AT_DECODED31)
+        scatter(2, 1)
+        product(banks[2:4], second[3], E4M3, both, stop=(1,))
+        turn_back(2, 3, banks[6])
+        fetch(2, 2, banks[5], AT_DECODED31 + KIB)
+        scatter(2, 2)
+        for b in blocks:
+            take_res(3, b, banks[b])
+        for b in blocks:
+            take_dx(3, b, banks[2 + b], 0, 1)
+        turn_back(3, 0, banks[4])
+        for b in blocks:
+            take_dx(3, b, banks[2 + b], 1, ROW_TILES)
+        fetch(3, 0, banks[4])
+        scatter(3, 0)
+        last = sb("last", [P, 2 * CHUNK], F32)
+        turn_back(3, 1, banks[5])
+        turn_back(3, 2, banks[4])
+        fetch(3, 1, banks[5])
+        scatter(3, 1)
+        fetch(3, 2, banks[4])
+        turn_back(3, 3, banks[4])
+        scatter(3, 2)
+        fetch(2, 3, banks[6], into=last[:, 0:CHUNK])
+        fetch(3, 3, banks[4], into=last[:, CHUNK:])
+        scatter(2, 3, last[:], 2)

@@ -28,20 +28,17 @@ WOVEN = CHUNK * PACK
 ROW_TILES = N // P
 RUN = 4
 LIST_ROWS = 16
-
+CLEAR_PIECES = 4
 BOTH = 2
+
 KIB = 1024
-AT_DECODED21 = 0
-AT_DECODED31 = 4 * KIB
-AT_LO0 = 8 * KIB
-AT_HI1 = AT_LO0 + 4 * KIB
-AT_LO1 = 16 * KIB
-AT_ONES = AT_LO1 + 4 * KIB
-AT_TOTAL01 = AT_ONES + 64 - KIB
-AT_TURNED_DX0 = AT_ONES + 64
-AT_HI2 = 22 * KIB
-AT_ONE = AT_HI2 + 4 * KIB
-AT_TOTAL02 = AT_ONE + 64 - KIB
+AT_LO1 = 0
+AT_HI21 = 4 * KIB
+AT_LO2 = 2 * KIB
+AT_HI31 = 6 * KIB
+AT_LO3 = 4 * KIB
+AT_DECODED21 = 8 * KIB
+AT_TURNED_RES1 = 12 * KIB
 
 
 def tile_list_embg_tgq8_res_kernel(tc, dy, w_words, w_scales, res, wgo, offs, out):
@@ -53,10 +50,10 @@ def tile_list_embg_tgq8_res_kernel(tc, dy, w_words, w_scales, res, wgo, offs, ou
         psum = ctx.enter_context(tc.psum_pool(name="psum", bufs=1))
         banks = [psum.tile([P, BANK], F32, name=f"bank{b}") for b in range(8)]
 
-        def sb(name, shape, dtype, at=None):
-            if isinstance(at, int):
-                return laid.tile(shape, dtype, name=name, tag=name, align_bytes=64, offset=at)
-            return keep.tile(shape, dtype, name=name, tag=at or name, align_bytes=64)
+        def sb(name, shape, dtype, after=None):
+            if isinstance(after, int):
+                return laid.tile(shape, dtype, name=name, tag=name, align_bytes=64, offset=after)
+            return keep.tile(shape, dtype, name=name, tag=after or name, align_bytes=64)
 
         def woven(dst):
             return dst.rearrange("p (c i t) -> p c t i", i=RUN, t=PACK)
@@ -64,14 +61,13 @@ def tile_list_embg_tgq8_res_kernel(tc, dy, w_words, w_scales, res, wgo, offs, ou
         def by_runs(planes):
             return planes.rearrange("p t (c i) -> p c t i", i=RUN)
 
-        w_sc = sb("w_sc", [P, PASSES, N], U8)
-        nc.gpsimd.memset(w_sc[:].rearrange("p a n -> p (a n)").bitcast(I32), 0)
+        def planes_of(bank):
+            return bank[:].rearrange("p (t j) -> p t j", t=PACK)
+
         quadrant = sb("quadrant", [P, 1], F32)
         for q in range(4):
             nc.gpsimd.memset(quadrant[32 * q : 32 * q + 32, :], float(32 * q))
-        one_b = sb("one_b", [P, 1], F32, AT_ONE)
-        nc.gpsimd.memset(one_b[:], 1.0)
-        ones = sb("ones", [P, P], F32, AT_ONES)
+        ones = sb("ones", [P, P], F32)
         nc.vector.memset(ones[:], 1.0)
         column = sb("column", [P, P], F32)
         nc.vector.tensor_tensor_scan(column[:], ones[:], ones[:], -1.0, ALU.mult, ALU.add)
@@ -83,6 +79,8 @@ def tile_list_embg_tgq8_res_kernel(tc, dy, w_words, w_scales, res, wgo, offs, ou
         nc.vector.memset(eye_rows[:].bitcast(I32), 0)
         diagonals = eye_rows[:].rearrange("p (t x) -> p t x", t=PACK)[:, :, 0:K_PASS:PACK]
         nc.scalar.copy(out=diagonals, in_=eye32[:].unsqueeze(1).to_broadcast([P, PACK, P]))
+        w_sc = sb("w_sc", [P, PASSES, N], U8, "in_quadrant")
+        nc.vector.memset(w_sc[:].rearrange("p a n -> p (a n)").bitcast(I32), 0)
         eye_codes = sb("eye_codes", [P, K_PASS], U32)
         eye_sc = sb("eye_sc", [P, K_PASS], U8)
 
@@ -101,369 +99,345 @@ def tile_list_embg_tgq8_res_kernel(tc, dy, w_words, w_scales, res, wgo, offs, ou
                 for r in range(r0, r1):
                     res_sb[c, r] = tile[:, r - r0, (c - c0) * CHUNK : (c - c0 + 1) * CHUNK]
 
-        for c in range(2):
-            for a in range(PASSES):
-                load_dy(c, a)
+        load_dy(0, 0)
+        load_dy(0, 1)
+        for q in range(4):
+            nc.scalar.dma_start(
+                out=w_sc[32 * q : 32 * q + 4, :, :].bitcast(I32),
+                in_=w_scales[:, 4 * q : 4 * q + 4, :].rearrange("a r n -> r a n").bitcast(I32),
+            )
+        load_dy(1, 0)
         w_codes = sb("w_codes", [P, PASSES, N], U32)
         nc.sync.dma_start(
             out=w_codes[:].bitcast(I32),
             in_=w_words.rearrange("a p n i -> p a (n i)").bitcast(I32),
         )
-        for q in range(4):
-            nc.sync.dma_start(
-                out=w_sc[32 * q : 32 * q + 4, :, :].bitcast(I32),
-                in_=w_scales[:, 4 * q : 4 * q + 4, :].rearrange("a r n -> r a n").bitcast(I32),
-            )
-        load_res(0, 1, 0, 2)
         wgo_rows = sb("wgo_rows", [P, P], F32)
         nc.sync.dma_start(out=wgo_rows[:], in_=wgo[0 : P * P // J, :].rearrange("r (c j) -> (r c) j", j=P))
+        load_dy(1, 1)
+        load_res(0, 1, 0, 1)
         wgo0 = sb("wgo0", [P, CHUNK], F32)
         nc.sync.dma_start(out=wgo0[:], in_=wgo[:, 0:CHUNK])
         offsets = keep.tile([P, J // LIST_ROWS], U16, name="offsets")
         nc.sync.dma_start(offsets[:], offs)
+        load_res(0, 1, 1, ROW_TILES)
         load_dy(2, 0)
         load_dy(2, 1)
-        load_res(0, 1, 2, ROW_TILES)
         load_dy(3, 0)
         load_res(1, 2, 0, ROW_TILES)
         load_dy(3, 1)
         load_res(2, CHUNKS, 0, ROW_TILES)
 
         hi, lo, first, second, decoded, turned_res, turned_dx, totals, pages = {}, {}, {}, {}, {}, {}, {}, {}, []
+        blocks = range(BLOCKS)
+        product_banks, decode_banks, res_banks = banks[0:2], banks[2:4], (banks[7], banks[4])
+        early_bank, late_bank = banks[6], banks[5]
 
         def part(pieces, a, j0=0, j1=CHUNK):
             return pieces[a][:, j0 * PACK : j1 * PACK]
 
-        def woven_pair(name, at=None):
-            tile = sb(name, [P, PASSES * WOVEN], BF16, at)
+        def woven_pair(name, after=None):
+            tile = sb(name, [P, PASSES * WOVEN], BF16, after)
             return tile[:, 0:WOVEN], tile[:, WOVEN:], tile[:]
 
-        def operand(name, columns, at=None, scale_at=None):
-            return sb(name + "_codes", [P, columns], U32, at)[:], sb(name + "_sc", [P, columns], U8, scale_at)[:]
-
-        def operand_pair(name, at=None, scale_at=None):
-            codes, scales = operand(name, PASSES * CHUNK, at, scale_at)
+        def operand_pair(name, after=None):
+            codes = sb(name + "_codes", [P, PASSES * CHUNK], U32)[:]
+            scales = sb(name + "_sc", [P, PASSES * CHUNK], U8, after)[:]
             return (codes[:, 0:CHUNK], scales[:, 0:CHUNK]), (codes[:, CHUNK:], scales[:, CHUNK:]), (codes, scales)
 
-        def cast(engine, c, a, j0=0, j1=CHUNK, one=1.0):
+        def operand(name, codes_after=None, scales_after=None):
+            return sb(name + "_codes", [P, CHUNK], U32, codes_after)[:], sb(name + "_sc", [P, CHUNK], U8, scales_after)[:]
+
+        def cast(c, a, j0=0, j1=CHUNK, on_vector=False):
             dst, src = woven(part(hi[c], a, j0, j1)), by_runs(raw[c, a][:, :, j0:j1])
-            if engine == "scalar":
-                nc.scalar.activation(dst, src, COPY, scale=one)
-            elif engine == "vector":
+            if on_vector:
                 nc.vector.tensor_copy(out=dst, in_=src)
             else:
-                nc.gpsimd.tensor_scalar(
-                    part(hi[c], a, j0, j1).rearrange("p (j t) -> p j t", t=PACK),
-                    raw[c, a][:, :, j0:j1].rearrange("p t j -> p j t"),
-                    one,
-                    0.0,
-                    ALU.mult,
-                    ALU.add,
-                )
+                nc.scalar.copy(out=dst, in_=src)
 
         def quantise(q, src, fmt, a):
             nc.vector.quantize_mx(out=q[a][0].bitcast(fmt), scales=q[a][1], in_=src[a])
 
-        def decode(into, t, q, j0, j1):
-            cols = slice(t * P, (t + 1) * P)
-            nc.tensor.matmul_mx(
-                out=into,
-                lhsT=eye_codes[:, cols].bitcast(E4M3),
-                lhsT_scale=eye_sc[:, cols],
-                rhs=q[0][:, j0:j1].bitcast(E5M2),
-                rhs_scale=q[1][:, j0:j1],
-                start=True,
-                stop=True,
-            )
-
-        def decode_block(bank, c, a, b):
+        def decode(bank, c, a, b):
+            codes, scales = first[c][a]
             for t in range(PACK):
-                decode(bank[:, t * P : (t + 1) * P], t, first[c][a], b * P, (b + 1) * P)
+                cols = slice(t * P, (t + 1) * P)
+                nc.tensor.matmul_mx(
+                    out=bank[:, cols],
+                    lhsT=eye_codes[:, cols].bitcast(E4M3),
+                    lhsT_scale=eye_sc[:, cols],
+                    rhs=codes[:, b * P : (b + 1) * P].bitcast(E5M2),
+                    rhs_scale=scales[:, b * P : (b + 1) * P],
+                    start=True,
+                    stop=True,
+                )
 
-        def subtract_block(bank, c, a, b):
+        def subtract_on_vector(bank, c, a, b):
             nc.vector.tensor_tensor(
                 woven(part(lo[c], a, b * P, (b + 1) * P)),
                 by_runs(raw[c, a][:, :, b * P : (b + 1) * P]),
-                by_runs(bank[:].rearrange("p (t j) -> p t j", t=PACK)),
+                by_runs(planes_of(bank)),
                 ALU.subtract,
             )
 
-        def copy_decoded(bank, c, a, b, at=None):
+        def subtract_on_gpsimd(bank, c, a, b, after=None):
             if b == 0:
-                decoded[c, a] = sb(f"decoded{c}{a}", [P, BLOCKS, BANK], F32, at)
-            nc.scalar.copy(out=decoded[c, a][:, b, :], in_=bank[:])
-
-        def subtract_on_gpsimd(c, a, b):
+                decoded[c, a] = sb(f"decoded{c}{a}", [P, BLOCKS, BANK], F32, after)
+            walked = decoded[c, a][:, b, :].rearrange("p (c t i) -> p c t i", t=PACK, i=RUN)
+            nc.scalar.copy(out=walked, in_=by_runs(planes_of(bank)))
             nc.gpsimd.tensor_tensor(
                 woven(part(lo[c], a, b * P, (b + 1) * P)),
                 by_runs(raw[c, a][:, :, b * P : (b + 1) * P]),
-                by_runs(decoded[c, a][:, b, :].rearrange("p (t j) -> p t j", t=PACK)),
+                walked,
                 ALU.subtract,
             )
 
-        def add_on_vector(r, bank, at=None):
-            totals[0, r] = sb(f"total0{r}", [P, CHUNK], F32, at)[:]
-            nc.vector.tensor_tensor(totals[0, r], bank[:, 0:CHUNK], res_sb[0, r], ALU.add)
-
-        def scatter_times_wgo(r):
-            places = pages[r][:].indirect(offsets[:, 0 : CHUNK // LIST_ROWS])
-            nc.vector.tensor_tensor(places, totals[0, r], wgo0[:], ALU.mult)
-
-        def product(pair, q, fmt, terms, start=(), stop=()):
-            for a, b in terms:
+        def product(c, q, fmt, passes, spans=((0, N),), start=False, stop=False):
+            for b in blocks:
                 cols = slice(b * P, (b + 1) * P)
-                nc.tensor.matmul_mx(
-                    out=pair[b][:],
-                    lhsT=q[a][0][:, cols].bitcast(fmt),
-                    lhsT_scale=q[a][1][:, cols],
-                    rhs=w_codes[:, a, :].bitcast(E4M3),
-                    rhs_scale=w_sc[:, a, :],
-                    start=a in start,
-                    stop=a in stop,
-                )
+                terms = [(a, n0, n1) for a in passes for n0, n1 in spans]
+                for n, (a, n0, n1) in enumerate(terms):
+                    nc.tensor.matmul_mx(
+                        out=product_banks[b][:, n0:n1],
+                        lhsT=q[a][0][:, cols].bitcast(fmt),
+                        lhsT_scale=q[a][1][:, cols],
+                        rhs=w_codes[:, a, n0:n1].bitcast(E4M3),
+                        rhs_scale=w_sc[:, a, n0:n1],
+                        start=start and n == 0,
+                        stop=stop and n == len(terms) - 1,
+                    )
 
-        def product_last_row(bank):
-            terms = [(q, fmt, a, b) for q, fmt in ((first[0], E5M2), (second[0], E4M3)) for a, b in in_order]
-            for n, (q, fmt, a, b) in enumerate(terms):
-                cols = slice(b * P, (b + 1) * P)
-                nc.tensor.matmul_mx(
-                    out=bank[:, cols],
-                    lhsT=q[a][0][:, cols].bitcast(fmt),
-                    lhsT_scale=q[a][1][:, cols],
-                    rhs=w_codes[:, a, N - P : N].bitcast(E4M3),
-                    rhs_scale=w_sc[:, a, N - P : N],
-                    start=n == 0,
-                    stop=n == len(terms) - 1,
-                )
-
-        def product_row(bank, r, q, fmt, start, stop):
+        def product_first_row(q, fmt, start, stop):
             for a in range(PASSES):
                 nc.tensor.matmul_mx(
-                    out=bank[:, 0:CHUNK],
-                    lhsT=w_codes[:, a, r * P : (r + 1) * P].bitcast(E4M3),
-                    lhsT_scale=w_sc[:, a, r * P : (r + 1) * P],
+                    out=early_bank[:, 0:CHUNK],
+                    lhsT=w_codes[:, a, 0:P].bitcast(E4M3),
+                    lhsT_scale=w_sc[:, a, 0:P],
                     rhs=q[a][0].bitcast(fmt),
                     rhs_scale=q[a][1],
                     start=start and a == 0,
                     stop=stop and a == PASSES - 1,
                 )
 
-        def weighted(name, c, b, src, r0, r1, into, place=None):
-            tile = sb(name, [P, (r1 - r0) * P], F32)[:] if place is None else place
-            column = c * BLOCKS + b
-            nc.scalar.activation(tile, src, COPY, scale=wgo_col[:, column : column + 1])
-            for r in range(r0, r1):
-                into[c, b, r] = tile[:, (r - r0) * P : (r - r0 + 1) * P]
+        def turn_res(c, r0, r1, into):
+            for b in blocks:
+                for r in range(r0, r1):
+                    at = (r - r0) * P
+                    nc.tensor.transpose(into(b)[:, at : at + P], res_sb[c, r][:, b * P : (b + 1) * P], eye32[:])
 
-        def turn_res(c, b, bank, r0=0, r1=ROW_TILES):
-            for r in range(r0, r1):
-                nc.tensor.transpose(bank[:, r * P : (r + 1) * P], res_sb[c, r][:, b * P : (b + 1) * P], eye32[:])
+        def turned_tile(name, r0, r1, after=None):
+            return sb(name, [P, BLOCKS, (r1 - r0) * P], F32, after), r0
 
-        def take_res(c, b, bank, r0=0, r1=ROW_TILES, place=None):
-            weighted(f"turned_res{c}{b}{r0}", c, b, bank[:, r0 * P : r1 * P], r0, r1, turned_res, place)
+        def take(turned, place, source, c, r0, r1):
+            tile, base = place
+            for b in blocks:
+                at = c * BLOCKS + b
+                dst = tile[:, b, (r0 - base) * P : (r1 - base) * P]
+                nc.scalar.activation(dst, source(b), COPY, scale=wgo_col[:, at : at + 1])
+                for r in range(r0, r1):
+                    turned[c, b, r] = dst[:, (r - r0) * P : (r - r0 + 1) * P]
 
-        def take_dx(c, b, bank, r0=0, r1=ROW_TILES, place=None):
-            weighted(f"turned_dx{c}{b}{r0}", c, b, bank[:, r0 * P : r1 * P], r0, r1, turned_dx, place)
+        def take_res(place, c, r0, r1):
+            take(turned_res, place, lambda b: res_banks[b][:, r0 * P : r1 * P], c, r0, r1)
 
-        def turn_back(c, r, bank):
-            terms = [(src[c, b, r], b) for src in (turned_res, turned_dx) for b in range(BLOCKS)]
-            for n, (tile, b) in enumerate(terms):
+        def take_dx(place, c, r0, r1):
+            take(turned_dx, place, lambda b: product_banks[b][:, r0 * P : r1 * P], c, r0, r1)
+
+        def turn_back(bank, c, r0, r1):
+            terms = [(src, r, b) for r in range(r0, r1) for src in (turned_res, turned_dx) for b in blocks]
+            for n, (src, r, b) in enumerate(terms):
+                at = (r - r0) * CHUNK + b * P
                 nc.tensor.matmul(
-                    bank[:, b * P : (b + 1) * P],
-                    lhsT=tile,
+                    bank[:, at : at + P],
+                    lhsT=src[c, b, r],
                     rhs=eye32[:],
                     is_transpose=True,
                     start=n == 0,
                     stop=n == len(terms) - 1,
                 )
 
-        def fetch(c, r, bank, at=None, into=None):
-            totals[c, r] = sb(f"total{c}{r}", [P, CHUNK], F32, at)[:] if into is None else into
-            nc.scalar.copy(out=totals[c, r], in_=bank[:, 0:CHUNK])
+        def fetch(bank, c, r0, r1, after=None, into=None):
+            width = (r1 - r0) * CHUNK
+            tile = sb(f"total{c}{r0}", [P, width], F32, after)[:] if into is None else into
+            nc.scalar.copy(out=tile, in_=bank[:, 0:width])
+            for r in range(r0, r1):
+                totals[c, r] = tile[:, (r - r0) * CHUNK : (r - r0 + 1) * CHUNK]
 
-        def clear_page(engine, pieces, at=None):
-            page = sb(f"page{len(pages)}", [P, T], F32, at)
+        def clear_page(engine, pieces, after):
+            page = sb(f"page{len(pages)}", [P, T], F32, after)
             for n in range(pieces):
                 engine.memset(page[:, n * T // pieces : (n + 1) * T // pieces], 0.0)
             pages.append(page)
 
-        def scatter(c, r, values=None, chunks=1):
+        def places(c, r, chunks=1):
             columns = CHUNK // LIST_ROWS
-            places = pages[r][:].indirect(offsets[:, c * columns : (c + chunks) * columns])
-            nc.vector.tensor_copy(places, totals[c, r] if values is None else values)
+            return pages[r][:].indirect(offsets[:, c * columns : (c + chunks) * columns])
+
+        def scatter(c, r, values=None, chunks=1):
+            nc.vector.tensor_copy(places(c, r, chunks), totals[c, r] if values is None else values)
             if c + chunks == CHUNKS:
                 nc.sync.dma_start(out=out[r * P : (r + 1) * P, :], in_=pages[r][:])
 
-        both = [(a, b) for b in range(BLOCKS) for a in range(PASSES)]
-        blocks = range(BLOCKS)
-        in_order = [(a, b) for a in range(PASSES) for b in blocks]
-        hi[0], hi[1] = woven_pair("hi0"), woven_pair("hi1", AT_HI1)
-        lo[0], lo[1] = woven_pair("lo0", AT_LO0), woven_pair("lo1", AT_LO1)
-        first[0] = operand_pair("first0")
-        for c in range(CHUNKS):
-            second[c] = operand_pair(f"second{c}")
+        both = range(PASSES)
+        hi[0] = [sb(f"hi0{a}", [P, WOVEN], BF16)[:] for a in both]
+        hi[1] = [sb(f"hi1{a}", [P, WOVEN], BF16)[:] for a in both]
+        hi[2] = [sb("hi20", [P, WOVEN], BF16)[:], sb("hi21", [P, WOVEN], BF16, AT_HI21)[:]]
+        hi[3] = [sb("hi30", [P, WOVEN], BF16)[:], sb("hi31", [P, WOVEN], BF16, AT_HI31)[:]]
+        lo[0], lo[1] = woven_pair("lo0"), woven_pair("lo1", AT_LO1)
+        for c in range(3):
+            first[c] = [operand(f"first{c}{a}") for a in both]
+
+        def whole_banks(b):
+            return res_banks[b][:]
 
         clear_page(nc.vector, 1, "column")
-        clear_page(nc.vector, 1, "in_quadrant")
-        cast("scalar", 0, 0, 0, P)
-        cast("vector", 0, 0, P, CHUNK)
-        nc.vector.quantize_mx(
-            out=eye_codes[:].bitcast(E4M3), scales=eye_sc[:], in_=eye_rows[:, 0 : PACK * K_PASS]
-        )
-        quantise(first[0], hi[0], E5M2, 0)
-        for b in blocks:
-            decode_block(banks[b], 0, 0, b)
-        cast("scalar", 0, 1, 0, P)
-        cast("vector", 0, 1, P, CHUNK)
-        quantise(first[0], hi[0], E5M2, 1)
-        for b in blocks:
-            decode_block(banks[2 + b], 0, 1, b)
-        cast("scalar", 1, 0)
-        cast("scalar", 1, 1)
-        clear_page(nc.gpsimd, 1, "hi0")
-        for a, b in in_order:
-            subtract_block(banks[2 * a + b], 0, a, b)
-        first[1] = operand_pair("first1", "raw00")
+        nc.vector.quantize_mx(out=eye_codes[:].bitcast(E4M3), scales=eye_sc[:], in_=eye_rows[:, 0 : PACK * K_PASS])
+        for a in both:
+            cast(0, a, 0, P)
+            cast(0, a, P, CHUNK, on_vector=True)
+            quantise(first[0], hi[0], E5M2, a)
+            for b in blocks:
+                decode(banks[2 * a + b], 0, a, b)
+        cast(1, 0)
+        clear_page(nc.gpsimd, CLEAR_PIECES, "hi01")
+        for a in both:
+            for b in blocks:
+                subtract_on_vector(banks[2 * a + b], 0, a, b)
         quantise(first[1], hi[1], E5M2, 0)
+        second[0] = operand_pair("second0")
         quantise(second[0], lo[0], E4M3, BOTH)
-        quantise(first[1], hi[1], E5M2, 1)
-        clear_page(nc.gpsimd, 1, AT_LO0)
-        for a, b in in_order:
-            decode_block(banks[4 + 2 * a + b], 1, a, b)
-        product(banks[2:4], first[1], E5M2, both, start=(0,))
-        for a, b in in_order:
-            subtract_block(banks[4 + 2 * a + b], 1, a, b)
-        for r in range(3):
-            product_row(banks[4 + r], r, first[0], E5M2, True, False)
-            product_row(banks[4 + r], r, second[0], E4M3, False, True)
-        add_on_vector(0, banks[4])
-        quantise(second[1], lo[1], E4M3, BOTH)
-        scatter_times_wgo(0)
-        hi[2] = woven_pair("hi2", AT_HI2)
-        cast("scalar", 2, 0)
+        clear_page(nc.gpsimd, CLEAR_PIECES, "lo0")
+        for b in blocks:
+            decode(banks[4 + b], 1, 0, b)
+        later_rows = ((P, 2 * P), (2 * P, N))
+        product_first_row(first[0], E5M2, True, False)
+        product(0, first[0], E5M2, both, later_rows, start=True)
+        product_first_row(second[0], E4M3, False, True)
+        product(0, second[0], E4M3, both, later_rows, stop=True)
         nc.tensor.transpose(banks[7][:, 0:P], wgo_rows[:], eye32[:])
         wgo_col = sb("wgo_col", [P, J // P], F32)
+        cast(1, 1)
         nc.scalar.copy(out=wgo_col[:], in_=banks[7][:, 0 : J // P])
-        cast("scalar", 2, 1, one=ones[:, 0:1])
-        product_last_row(banks[7])
-        product(banks[2:4], second[1], E4M3, both, stop=(1,))
+        subtract_on_vector(banks[4], 1, 0, 0)
+        total00 = sb("total00", [P, CHUNK], F32)
+        nc.vector.tensor_tensor(total00[:], early_bank[:, 0:CHUNK], res_sb[0, 0], ALU.add)
+        subtract_on_vector(banks[5], 1, 0, 1)
+        quantise(first[1], hi[1], E5M2, 1)
+        clear_page(nc.gpsimd, CLEAR_PIECES, "hi11")
+        nc.vector.tensor_tensor(places(0, 0), total00[:], wgo0[:], ALU.mult)
         for b in blocks:
-            turn_res(0, b, banks[b], 3, ROW_TILES)
-        add_on_vector(1, banks[5], AT_TOTAL01)
-        first[2] = operand_pair("first2", AT_LO1)
-        quantise(first[2], hi[2], E5M2, BOTH)
-        scatter_times_wgo(1)
-        turned_dx0 = sb("turned_dx0", [P, BLOCKS, P], F32, AT_TURNED_DX0)
+            decode(decode_banks[b], 1, 1, b)
+
+        def row1(b):
+            return res_banks[0][:, b * P : (b + 1) * P]
+
+        def rows23(b):
+            return res_banks[1][:, b * CHUNK : (b + 1) * CHUNK]
+
+        dx_place = turned_tile("turned_dx0", 0, ROW_TILES, "turned_dx")
+        turn_res(0, 1, 2, row1)
+        take_dx(dx_place, 0, 1, 2)
+        take(turned_res, turned_tile("turned_res01", 1, 2), row1, 0, 1, 2)
+        turn_back(late_bank, 0, 1, 2)
+        turn_res(0, 2, ROW_TILES, rows23)
+        cast(2, 0)
+        fetch(late_bank, 0, 1, 2)
         for b in blocks:
-            weighted("turned_dx0", 0, b, banks[7][:, b * P : (b + 1) * P], 3, ROW_TILES, turned_dx, turned_dx0[:, b, :])
+            subtract_on_vector(decode_banks[b], 1, 1, b)
+        quantise(first[2], hi[2], E5M2, 0)
+        scatter(0, 1)
+        take_dx(dx_place, 0, 2, ROW_TILES)
+        take(turned_res, turned_tile("turned_res02", 2, ROW_TILES), rows23, 0, 2, ROW_TILES)
+        turn_back(late_bank, 0, 2, ROW_TILES)
         for b in blocks:
-            take_res(0, b, banks[b], 3, ROW_TILES)
-        turn_back(0, 3, banks[5])
-        decode_block(banks[7], 2, 0, 0)
-        decode_block(banks[4], 2, 0, 1)
-        for b in blocks:
-            turn_res(1, b, banks[b])
-        hi[3] = [sb("hi30", [P, WOVEN], BF16)[:]]
-        cast("scalar", 3, 0, one=one_b[:])
-        add_on_vector(2, banks[6], AT_TOTAL02)
-        first[3] = (operand("first30", CHUNK, AT_HI2), operand("first31", CHUNK, AT_DECODED21 + 2 * KIB, AT_DECODED21 + 3 * KIB))
-        quantise(first[3], hi[3], E5M2, 0)
-        scatter_times_wgo(2)
-        lo[2] = woven_pair("lo2", "hi30")
-        fetch(0, 3, banks[5])
+            decode(decode_banks[b], 2, 0, b)
+        product(1, first[1], E5M2, both, start=True)
+        cast(2, 1)
+        second[1] = operand_pair("second1", "turned_res02")
+        quantise(second[1], lo[1], E4M3, BOTH)
+        quantise(first[2], hi[2], E5M2, 1)
+        product(1, second[1], E4M3, both, stop=True)
+        lo[2] = woven_pair("lo2", AT_LO2)
+        subtract_on_gpsimd(decode_banks[0], 2, 0, 0, "turned_res01")
+        fetch(late_bank, 0, 2, ROW_TILES)
+        subtract_on_gpsimd(decode_banks[1], 2, 0, 1)
+        scatter(0, 2)
         scatter(0, 3)
-        copy_decoded(banks[7], 2, 0, 0)
-        subtract_on_gpsimd(2, 0, 0)
-        copy_decoded(banks[4], 2, 0, 1)
-        subtract_on_gpsimd(2, 0, 1)
         for b in blocks:
-            decode_block(banks[6 + b], 2, 1, b)
-        for b in blocks:
-            take_dx(1, b, banks[2 + b], 0, 1)
-            take_res(1, b, banks[b], 0, 1)
-        turn_back(1, 0, banks[4])
-        take_dx(1, 0, banks[2], 1, ROW_TILES)
-        product(banks[2:4], first[2], E5M2, [(0, 0), (1, 0)], start=(0,))
-        fetch(1, 0, banks[4])
+            decode(decode_banks[b], 2, 1, b)
+
+        dx_place = turned_tile("turned_dx1", 0, ROW_TILES, "turned_dx")
+        res_place = turned_tile("turned_res1", 0, ROW_TILES, AT_TURNED_RES1)
+        turn_res(1, 0, ROW_TILES, whole_banks)
+        take_res(res_place, 1, 0, 2)
+        take_dx(dx_place, 1, 0, 2)
+        turn_back(early_bank, 1, 0, 1)
+        turn_back(late_bank, 1, 1, 2)
+        subtract_on_gpsimd(decode_banks[0], 2, 1, 0, AT_DECODED21)
+        fetch(early_bank, 1, 0, 1)
         scatter(1, 0)
-        copy_decoded(banks[6], 2, 1, 0, AT_DECODED21)
-        subtract_on_gpsimd(2, 1, 0)
-        take_dx(1, 1, banks[3], 1, 2)
-        for b in blocks:
-            take_res(1, b, banks[b], 1, 2)
-        turn_back(1, 1, banks[5])
-        decode_block(banks[6], 3, 0, 0)
-        copy_decoded(banks[7], 2, 1, 1)
-        subtract_on_gpsimd(2, 1, 1)
-        fetch(1, 1, banks[5])
+        subtract_on_gpsimd(decode_banks[1], 2, 1, 1)
+        fetch(late_bank, 1, 1, 2)
         scatter(1, 1)
-        take_dx(1, 1, banks[3], 2, ROW_TILES)
-        for b in blocks:
-            take_res(1, b, banks[b], 2, ROW_TILES)
-        decode_block(banks[7], 3, 0, 1)
-        turn_back(1, 2, banks[4])
-        turn_back(1, 3, banks[5])
-        product(banks[2:4], first[2], E5M2, [(0, 1), (1, 1)], start=(0,))
-        for b in blocks:
-            turn_res(2, b, banks[b])
-        hi[3].append(sb("hi31", [P, WOVEN], BF16, "decoded20")[:])
-        cast("scalar", 3, 1)
+        take_res(res_place, 1, 2, ROW_TILES)
+        take_dx(dx_place, 1, 2, ROW_TILES)
+        turn_back(late_bank, 1, 2, ROW_TILES)
+        product(2, first[2], E5M2, both, start=True)
+        cast(3, 0)
+        cast(3, 1)
+        first[3] = [operand(f"first3{a}", AT_DECODED21 + a * KIB, AT_TURNED_RES1 + a * CHUNK) for a in both]
+        second[2] = operand_pair("second2", AT_TURNED_RES1 + PASSES * CHUNK)
+        quantise(first[3], hi[3], E5M2, 0)
         quantise(second[2], lo[2], E4M3, BOTH)
         quantise(first[3], hi[3], E5M2, 1)
-        fetch(1, 2, banks[4], AT_DECODED21)
+        for b in blocks:
+            decode(decode_banks[b], 3, 0, b)
+        product(2, second[2], E4M3, both, stop=True)
+        fetch(late_bank, 1, 2, ROW_TILES, AT_DECODED21 + 2 * KIB)
+        lo[3] = woven_pair("lo3", AT_LO3)
+        for b in blocks:
+            subtract_on_gpsimd(decode_banks[b], 3, 0, b)
         scatter(1, 2)
-        product(banks[2:4], second[2], E4M3, both, stop=(1,))
-        lo[3] = woven_pair("lo3", "decoded20")
-        for b in blocks:
-            copy_decoded(banks[6 + b], 3, 0, b)
-            subtract_on_gpsimd(3, 0, b)
-        fetch(1, 3, banks[5], AT_DECODED21 + KIB)
-        for b in blocks:
-            decode_block(banks[6 + b], 3, 1, b)
         scatter(1, 3)
-        subtract_block(banks[7], 3, 1, 1)
+
+        dx_place = turned_tile("turned_dx2", 0, ROW_TILES, "turned_dx")
+        res_place = turned_tile("turned_res2", 0, ROW_TILES)
+        turn_res(2, 0, ROW_TILES, whole_banks)
         for b in blocks:
-            take_res(2, b, banks[b], 0, 1)
-        for b in blocks:
-            take_dx(2, b, banks[2 + b], 0, 1)
-        turn_back(2, 0, banks[4])
-        copy_decoded(banks[6], 3, 1, 0, AT_DECODED31)
-        subtract_on_gpsimd(3, 1, 0)
-        fetch(2, 0, banks[4])
+            decode(decode_banks[b], 3, 1, b)
+        take_res(res_place, 2, 0, ROW_TILES)
+        take_dx(dx_place, 2, 0, 1)
+        turn_back(early_bank, 2, 0, 1)
+        subtract_on_gpsimd(decode_banks[0], 3, 1, 0)
+        subtract_on_vector(decode_banks[1], 3, 1, 1)
+        fetch(early_bank, 2, 0, 1)
         scatter(2, 0)
-        for b in blocks:
-            take_dx(2, b, banks[2 + b], 1, ROW_TILES)
-        product(banks[2:4], first[3], E5M2, both, start=(0,))
-        for b in blocks:
-            take_res(2, b, banks[b], 1, ROW_TILES)
-        turn_back(2, 1, banks[4])
-        turn_back(2, 2, banks[5])
-        for b in blocks:
-            turn_res(3, b, banks[b])
-        quantise(second[3], lo[3], E4M3, BOTH)
-        fetch(2, 1, banks[4], AT_DECODED31)
-        scatter(2, 1)
-        product(banks[2:4], second[3], E4M3, both, stop=(1,))
-        turn_back(2, 3, banks[6])
-        fetch(2, 2, banks[5], AT_DECODED31 + KIB)
-        scatter(2, 2)
-        for b in blocks:
-            take_res(3, b, banks[b])
-        for b in blocks:
-            take_dx(3, b, banks[2 + b], 0, 1)
-        turn_back(3, 0, banks[4])
-        for b in blocks:
-            take_dx(3, b, banks[2 + b], 1, ROW_TILES)
-        fetch(3, 0, banks[4])
-        scatter(3, 0)
+        take_dx(dx_place, 2, 1, ROW_TILES)
+        turn_back(late_bank, 2, 3, ROW_TILES)
+        turn_back(early_bank, 2, 1, 3)
+        product(3, first[3], E5M2, both, start=True)
+        turn_res(3, 0, ROW_TILES, whole_banks)
         last = sb("last", [P, 2 * CHUNK], F32)
-        turn_back(3, 1, banks[5])
-        turn_back(3, 2, banks[4])
-        fetch(3, 1, banks[5])
+        fetch(late_bank, 2, 3, ROW_TILES, into=last[:, 0:CHUNK])
+        res_place = turned_tile("turned_res3", 0, ROW_TILES)
+        take_res(res_place, 3, 0, ROW_TILES)
+        second[3] = operand_pair("second3", "turned_res2")
+        quantise(second[3], lo[3], E4M3, BOTH)
+        product(3, second[3], E4M3, both, stop=True)
+        fetch(early_bank, 2, 1, 3, "raw31")
+        scatter(2, 1)
+        scatter(2, 2)
+
+        dx_place = turned_tile("turned_dx3", 0, ROW_TILES, "turned_dx")
+        take_dx(dx_place, 3, 0, 1)
+        turn_back(late_bank, 3, 0, 1)
+        take_dx(dx_place, 3, 1, ROW_TILES)
+        fetch(late_bank, 3, 0, 1)
+        scatter(3, 0)
+        turn_back(early_bank, 3, 1, 3)
+        fetch(early_bank, 3, 1, 3)
+        turn_back(late_bank, 3, 3, ROW_TILES)
         scatter(3, 1)
-        fetch(3, 2, banks[4])
-        turn_back(3, 3, banks[4])
         scatter(3, 2)
-        fetch(2, 3, banks[6], into=last[:, 0:CHUNK])
-        fetch(3, 3, banks[4], into=last[:, CHUNK:])
+        fetch(late_bank, 3, 3, ROW_TILES, into=last[:, CHUNK:])
         scatter(2, 3, last[:], 2)

@@ -28,17 +28,18 @@ WOVEN = CHUNK * PACK
 ROW_TILES = N // P
 RUN = 4
 LIST_ROWS = 16
-CLEAR_PIECES = 4
 BOTH = 2
 
 KIB = 1024
-AT_LO1 = 0
 AT_HI21 = 4 * KIB
 AT_LO2 = 2 * KIB
 AT_HI31 = 6 * KIB
 AT_LO3 = 4 * KIB
 AT_DECODED21 = 8 * KIB
 AT_TURNED_RES1 = 12 * KIB
+AT_TURNED_RES10 = 17 * KIB
+AT_HI01 = 28 * KIB
+SCALAR_SHARE = 96
 
 
 def tile_list_embg_tgq8_res_kernel(tc, dy, w_words, w_scales, res, wgo, offs, out):
@@ -64,6 +65,14 @@ def tile_list_embg_tgq8_res_kernel(tc, dy, w_words, w_scales, res, wgo, offs, ou
         def planes_of(bank):
             return bank[:].rearrange("p (t j) -> p t j", t=PACK)
 
+        w_sc = sb("w_sc", [P, PASSES, N], U8)
+        nc.gpsimd.memset(w_sc[:].rearrange("p a n -> p (a n)").bitcast(I32), 0)
+        for q in range(4):
+            nc.scalar.dma_start(
+                out=w_sc[32 * q : 32 * q + 4, :, :].bitcast(I32),
+                in_=w_scales[:, 4 * q : 4 * q + 4, :].rearrange("a r n -> r a n").bitcast(I32),
+            )
+
         quadrant = sb("quadrant", [P, 1], F32)
         for q in range(4):
             nc.gpsimd.memset(quadrant[32 * q : 32 * q + 32, :], float(32 * q))
@@ -75,14 +84,17 @@ def tile_list_embg_tgq8_res_kernel(tc, dy, w_words, w_scales, res, wgo, offs, ou
         nc.vector.transpose(in_quadrant[:], column[:, 0:32])
         eye32 = sb("eye32", [P, P], F32)
         nc.vector.tensor_scalar(eye32[:], column[:], quadrant[:], in_quadrant[:, 0:1], ALU.subtract, ALU.is_equal)
-        eye_rows = sb("eye_in", [P, PACK * (K_PASS + 1)], BF16)
-        nc.vector.memset(eye_rows[:].bitcast(I32), 0)
-        diagonals = eye_rows[:].rearrange("p (t x) -> p t x", t=PACK)[:, :, 0:K_PASS:PACK]
-        nc.scalar.copy(out=diagonals, in_=eye32[:].unsqueeze(1).to_broadcast([P, PACK, P]))
-        w_sc = sb("w_sc", [P, PASSES, N], U8, "in_quadrant")
-        nc.vector.memset(w_sc[:].rearrange("p a n -> p (a n)").bitcast(I32), 0)
-        eye_codes = sb("eye_codes", [P, K_PASS], U32)
-        eye_sc = sb("eye_sc", [P, K_PASS], U8)
+        fours = sb("fours", [P, P, PACK], BF16)
+        nc.scalar.copy(out=fours[:], in_=eye32[:].unsqueeze(2).to_broadcast([P, P, PACK]))
+        fours_codes = sb("fours_codes", [P, P], U32)
+        eye_sc = sb("eye_sc", [P, P], U8)
+        nc.vector.quantize_mx(out=fours_codes[:].bitcast(E4M3), scales=eye_sc[:], in_=fours[:].rearrange("p m t -> p (m t)"))
+        eye_codes = sb("eye_codes", [P, K_PASS + 1], U32)
+        nc.vector.memset(eye_codes[:], 0)
+        nc.vector.tensor_copy(
+            out=eye_codes[:].bitcast(U8).rearrange("p (t x) -> p t x", t=PACK)[:, :, 0:K_PASS:PACK],
+            in_=fours_codes[:].bitcast(U8).rearrange("p (m t) -> p t m", t=PACK),
+        )
 
         raw, res_sb = {}, {}
 
@@ -98,40 +110,36 @@ def tile_list_embg_tgq8_res_kernel(tc, dy, w_words, w_scales, res, wgo, offs, ou
             for c in range(c0, c1):
                 for r in range(r0, r1):
                     res_sb[c, r] = tile[:, r - r0, (c - c0) * CHUNK : (c - c0 + 1) * CHUNK]
+            return tile
 
         load_dy(0, 0)
         load_dy(0, 1)
-        for q in range(4):
-            nc.scalar.dma_start(
-                out=w_sc[32 * q : 32 * q + 4, :, :].bitcast(I32),
-                in_=w_scales[:, 4 * q : 4 * q + 4, :].rearrange("a r n -> r a n").bitcast(I32),
-            )
+        wgo_rows = sb("wgo_rows", [P, P], F32)
+        nc.sync.dma_start(out=wgo_rows[:], in_=wgo[0 : P * P // J, :].rearrange("r (c j) -> (r c) j", j=P))
         load_dy(1, 0)
+        load_dy(1, 1)
         w_codes = sb("w_codes", [P, PASSES, N], U32)
         nc.sync.dma_start(
             out=w_codes[:].bitcast(I32),
             in_=w_words.rearrange("a p n i -> p a (n i)").bitcast(I32),
         )
-        wgo_rows = sb("wgo_rows", [P, P], F32)
-        nc.sync.dma_start(out=wgo_rows[:], in_=wgo[0 : P * P // J, :].rearrange("r (c j) -> (r c) j", j=P))
-        load_dy(1, 1)
-        load_res(0, 1, 0, 1)
+        res_first = load_res(0, 1, 0, 2)
+        load_dy(2, 0)
+        load_res(0, 1, 2, ROW_TILES)
         wgo0 = sb("wgo0", [P, CHUNK], F32)
         nc.sync.dma_start(out=wgo0[:], in_=wgo[:, 0:CHUNK])
         offsets = keep.tile([P, J // LIST_ROWS], U16, name="offsets")
         nc.sync.dma_start(offsets[:], offs)
-        load_res(0, 1, 1, ROW_TILES)
-        load_dy(2, 0)
         load_dy(2, 1)
-        load_dy(3, 0)
         load_res(1, 2, 0, ROW_TILES)
+        load_dy(3, 0)
         load_dy(3, 1)
         load_res(2, CHUNKS, 0, ROW_TILES)
 
         hi, lo, first, second, decoded, turned_res, turned_dx, totals, pages = {}, {}, {}, {}, {}, {}, {}, {}, []
         blocks = range(BLOCKS)
-        product_banks, decode_banks, res_banks = banks[0:2], banks[2:4], (banks[7], banks[4])
-        early_bank, late_bank = banks[6], banks[5]
+        product_banks, res_banks, decode_banks = banks[2:4], banks[4:6], banks[6:8]
+        early_bank, late_bank = banks[1], banks[0]
 
         def part(pieces, a, j0=0, j1=CHUNK):
             return pieces[a][:, j0 * PACK : j1 * PACK]
@@ -165,7 +173,7 @@ def tile_list_embg_tgq8_res_kernel(tc, dy, w_words, w_scales, res, wgo, offs, ou
                 nc.tensor.matmul_mx(
                     out=bank[:, cols],
                     lhsT=eye_codes[:, cols].bitcast(E4M3),
-                    lhsT_scale=eye_sc[:, cols],
+                    lhsT_scale=eye_sc[:],
                     rhs=codes[:, b * P : (b + 1) * P].bitcast(E5M2),
                     rhs_scale=scales[:, b * P : (b + 1) * P],
                     start=True,
@@ -192,32 +200,42 @@ def tile_list_embg_tgq8_res_kernel(tc, dy, w_words, w_scales, res, wgo, offs, ou
                 ALU.subtract,
             )
 
-        def product(c, q, fmt, passes, spans=((0, N),), start=False, stop=False):
-            for b in blocks:
-                cols = slice(b * P, (b + 1) * P)
-                terms = [(a, n0, n1) for a in passes for n0, n1 in spans]
-                for n, (a, n0, n1) in enumerate(terms):
-                    nc.tensor.matmul_mx(
-                        out=product_banks[b][:, n0:n1],
-                        lhsT=q[a][0][:, cols].bitcast(fmt),
-                        lhsT_scale=q[a][1][:, cols],
-                        rhs=w_codes[:, a, n0:n1].bitcast(E4M3),
-                        rhs_scale=w_sc[:, a, n0:n1],
-                        start=start and n == 0,
-                        stop=stop and n == len(terms) - 1,
-                    )
+        def mx(into, stationary, moving, start, stop):
+            (lhs, lhs_sc, lhs_fmt), (rhs, rhs_sc, rhs_fmt) = stationary, moving
+            nc.tensor.matmul_mx(
+                out=into,
+                lhsT=lhs.bitcast(lhs_fmt),
+                lhsT_scale=lhs_sc,
+                rhs=rhs.bitcast(rhs_fmt),
+                rhs_scale=rhs_sc,
+                start=start,
+                stop=stop,
+            )
 
-        def product_first_row(q, fmt, start, stop):
-            for a in range(PASSES):
-                nc.tensor.matmul_mx(
-                    out=early_bank[:, 0:CHUNK],
-                    lhsT=w_codes[:, a, 0:P].bitcast(E4M3),
-                    lhsT_scale=w_sc[:, a, 0:P],
-                    rhs=q[a][0].bitcast(fmt),
-                    rhs_scale=q[a][1],
-                    start=start and a == 0,
-                    stop=stop and a == PASSES - 1,
-                )
+        def w_columns(a, n0, n1):
+            return w_codes[:, a, n0:n1], w_sc[:, a, n0:n1], E4M3
+
+        def dy_block(q, fmt, a, b):
+            return q[a][0][:, b * P : (b + 1) * P], q[a][1][:, b * P : (b + 1) * P], fmt
+
+        def product(q, fmt, start=False, stop=False):
+            for b in blocks:
+                for a in both:
+                    mx(product_banks[b][:], dy_block(q, fmt, a, b), w_columns(a, 0, N), start and a == 0, stop and a == 1)
+
+        def product_first_rows(q, fmt, start=False, stop=False):
+            for r in range(2):
+                for a in both:
+                    into = banks[0][:, r * CHUNK : (r + 1) * CHUNK]
+                    n = PASSES * r + a
+                    mx(into, w_columns(a, r * P, (r + 1) * P), (*q[a], fmt), start and n == 0, stop and n == 3)
+
+        def product_last_rows(q, fmt, start=False, stop=False):
+            for b in blocks:
+                for a in both:
+                    into = banks[1][:, b * CHUNK : (b + 1) * CHUNK]
+                    n = PASSES * b + a
+                    mx(into, dy_block(q, fmt, a, b), w_columns(a, 2 * P, N), start and n == 0, stop and n == 3)
 
         def turn_res(c, r0, r1, into):
             for b in blocks:
@@ -263,7 +281,7 @@ def tile_list_embg_tgq8_res_kernel(tc, dy, w_words, w_scales, res, wgo, offs, ou
             for r in range(r0, r1):
                 totals[c, r] = tile[:, (r - r0) * CHUNK : (r - r0 + 1) * CHUNK]
 
-        def clear_page(engine, pieces, after):
+        def clear_page(engine, after=None, pieces=1):
             page = sb(f"page{len(pages)}", [P, T], F32, after)
             for n in range(pieces):
                 engine.memset(page[:, n * T // pieces : (n + 1) * T // pieces], 0.0)
@@ -279,110 +297,96 @@ def tile_list_embg_tgq8_res_kernel(tc, dy, w_words, w_scales, res, wgo, offs, ou
                 nc.sync.dma_start(out=out[r * P : (r + 1) * P, :], in_=pages[r][:])
 
         both = range(PASSES)
-        hi[0] = [sb(f"hi0{a}", [P, WOVEN], BF16)[:] for a in both]
+        hi[0] = [sb("hi00", [P, WOVEN], BF16)[:], sb("hi01", [P, WOVEN], BF16, AT_HI01)[:]]
         hi[1] = [sb(f"hi1{a}", [P, WOVEN], BF16)[:] for a in both]
         hi[2] = [sb("hi20", [P, WOVEN], BF16)[:], sb("hi21", [P, WOVEN], BF16, AT_HI21)[:]]
-        hi[3] = [sb("hi30", [P, WOVEN], BF16)[:], sb("hi31", [P, WOVEN], BF16, AT_HI31)[:]]
-        lo[0], lo[1] = woven_pair("lo0"), woven_pair("lo1", AT_LO1)
+        lo[0], lo[1] = woven_pair("lo0", AT_HI01 - 3 * KIB), woven_pair("lo1")
         for c in range(3):
             first[c] = [operand(f"first{c}{a}") for a in both]
 
         def whole_banks(b):
             return res_banks[b][:]
 
-        clear_page(nc.vector, 1, "column")
-        nc.vector.quantize_mx(out=eye_codes[:].bitcast(E4M3), scales=eye_sc[:], in_=eye_rows[:, 0 : PACK * K_PASS])
+        clear_page(nc.vector, None, 4)
         for a in both:
-            cast(0, a, 0, P)
-            cast(0, a, P, CHUNK, on_vector=True)
+            cast(0, a, 0, SCALAR_SHARE)
+            cast(0, a, SCALAR_SHARE, CHUNK, on_vector=True)
             quantise(first[0], hi[0], E5M2, a)
             for b in blocks:
                 decode(banks[2 * a + b], 0, a, b)
         cast(1, 0)
-        clear_page(nc.gpsimd, CLEAR_PIECES, "hi01")
+        cast(1, 1)
+        nc.tensor.transpose(banks[4][:, 0:P], wgo_rows[:], eye32[:])
+        wgo_col = sb("wgo_col", [P, J // P], F32)
+        nc.scalar.copy(out=wgo_col[:], in_=banks[4][:, 0 : J // P])
+        clear_page(nc.gpsimd, AT_HI01 + KIB)
         for a in both:
             for b in blocks:
                 subtract_on_vector(banks[2 * a + b], 0, a, b)
         quantise(first[1], hi[1], E5M2, 0)
         second[0] = operand_pair("second0")
         quantise(second[0], lo[0], E4M3, BOTH)
-        clear_page(nc.gpsimd, CLEAR_PIECES, "lo0")
-        for b in blocks:
-            decode(banks[4 + b], 1, 0, b)
-        later_rows = ((P, 2 * P), (2 * P, N))
-        product_first_row(first[0], E5M2, True, False)
-        product(0, first[0], E5M2, both, later_rows, start=True)
-        product_first_row(second[0], E4M3, False, True)
-        product(0, second[0], E4M3, both, later_rows, stop=True)
-        nc.tensor.transpose(banks[7][:, 0:P], wgo_rows[:], eye32[:])
-        wgo_col = sb("wgo_col", [P, J // P], F32)
-        cast(1, 1)
-        nc.scalar.copy(out=wgo_col[:], in_=banks[7][:, 0 : J // P])
-        subtract_on_vector(banks[4], 1, 0, 0)
-        total00 = sb("total00", [P, CHUNK], F32)
-        nc.vector.tensor_tensor(total00[:], early_bank[:, 0:CHUNK], res_sb[0, 0], ALU.add)
-        subtract_on_vector(banks[5], 1, 0, 1)
         quantise(first[1], hi[1], E5M2, 1)
-        clear_page(nc.gpsimd, CLEAR_PIECES, "hi11")
-        nc.vector.tensor_tensor(places(0, 0), total00[:], wgo0[:], ALU.mult)
-        for b in blocks:
-            decode(decode_banks[b], 1, 1, b)
-
-        def row1(b):
-            return res_banks[0][:, b * P : (b + 1) * P]
-
-        def rows23(b):
-            return res_banks[1][:, b * CHUNK : (b + 1) * CHUNK]
-
-        dx_place = turned_tile("turned_dx0", 0, ROW_TILES, "turned_dx")
-        turn_res(0, 1, 2, row1)
-        take_dx(dx_place, 0, 1, 2)
-        take(turned_res, turned_tile("turned_res01", 1, 2), row1, 0, 1, 2)
-        turn_back(late_bank, 0, 1, 2)
-        turn_res(0, 2, ROW_TILES, rows23)
+        clear_page(nc.gpsimd, "hi11")
+        for a in both:
+            for b in blocks:
+                decode(banks[4 + 2 * a + b], 1, a, b)
+        product_first_rows(first[0], E5M2, start=True)
+        product_first_rows(second[0], E4M3, stop=True)
+        for a in both:
+            for b in blocks:
+                subtract_on_vector(banks[4 + 2 * a + b], 1, a, b)
+        product_last_rows(first[0], E5M2, start=True)
+        product_last_rows(second[0], E4M3, stop=True)
         cast(2, 0)
-        fetch(late_bank, 0, 1, 2)
-        for b in blocks:
-            subtract_on_vector(decode_banks[b], 1, 1, b)
+
+        total0 = sb("total0", [P, 2, CHUNK], F32)
+        nc.vector.tensor_tensor(total0[:], banks[0][:].rearrange("p (r j) -> p r j", r=2), res_first[:], ALU.add)
+        second[1] = operand_pair("second1")
+        quantise(second[1], lo[1], E4M3, BOTH)
         quantise(first[2], hi[2], E5M2, 0)
-        scatter(0, 1)
-        take_dx(dx_place, 0, 2, ROW_TILES)
-        take(turned_res, turned_tile("turned_res02", 2, ROW_TILES), rows23, 0, 2, ROW_TILES)
+        clear_page(nc.gpsimd, "hi20")
+        for r in range(2):
+            nc.vector.tensor_tensor(places(0, r), total0[:, r, :], wgo0[:], ALU.mult)
+
+        def by_block(bank):
+            return lambda b: bank[:, b * CHUNK : (b + 1) * CHUNK]
+
+        turn_res(0, 2, ROW_TILES, by_block(banks[5]))
+        take(turned_dx, turned_tile("turned_dx0", 2, ROW_TILES), by_block(banks[1]), 0, 2, ROW_TILES)
+        take(turned_res, turned_tile("turned_res0", 2, ROW_TILES), by_block(banks[5]), 0, 2, ROW_TILES)
         turn_back(late_bank, 0, 2, ROW_TILES)
         for b in blocks:
             decode(decode_banks[b], 2, 0, b)
-        product(1, first[1], E5M2, both, start=True)
+        product(first[1], E5M2, start=True)
+        product(second[1], E4M3, stop=True)
         cast(2, 1)
-        second[1] = operand_pair("second1", "turned_res02")
-        quantise(second[1], lo[1], E4M3, BOTH)
         quantise(first[2], hi[2], E5M2, 1)
-        product(1, second[1], E4M3, both, stop=True)
-        lo[2] = woven_pair("lo2", AT_LO2)
-        subtract_on_gpsimd(decode_banks[0], 2, 0, 0, "turned_res01")
         fetch(late_bank, 0, 2, ROW_TILES)
-        subtract_on_gpsimd(decode_banks[1], 2, 0, 1)
+        lo[2] = woven_pair("lo2", AT_LO2)
+        for b in blocks:
+            subtract_on_gpsimd(decode_banks[b], 2, 0, b)
         scatter(0, 2)
         scatter(0, 3)
+
+        turn_res(1, 0, ROW_TILES, whole_banks)
         for b in blocks:
             decode(decode_banks[b], 2, 1, b)
-
-        dx_place = turned_tile("turned_dx1", 0, ROW_TILES, "turned_dx")
-        res_place = turned_tile("turned_res1", 0, ROW_TILES, AT_TURNED_RES1)
-        turn_res(1, 0, ROW_TILES, whole_banks)
-        take_res(res_place, 1, 0, 2)
-        take_dx(dx_place, 1, 0, 2)
+        take_dx(turned_tile("turned_dx10", 0, 2, AT_HI31), 1, 0, 2)
+        take_res(turned_tile("turned_res10", 0, 2, AT_TURNED_RES10), 1, 0, 2)
         turn_back(early_bank, 1, 0, 1)
         turn_back(late_bank, 1, 1, 2)
         subtract_on_gpsimd(decode_banks[0], 2, 1, 0, AT_DECODED21)
         fetch(early_bank, 1, 0, 1)
         scatter(1, 0)
-        subtract_on_gpsimd(decode_banks[1], 2, 1, 1)
         fetch(late_bank, 1, 1, 2)
         scatter(1, 1)
-        take_res(res_place, 1, 2, ROW_TILES)
-        take_dx(dx_place, 1, 2, ROW_TILES)
+        subtract_on_gpsimd(decode_banks[1], 2, 1, 1)
+        take_res(turned_tile("turned_res12", 2, ROW_TILES, AT_TURNED_RES1), 1, 2, ROW_TILES)
+        take_dx(turned_tile("turned_dx12", 2, ROW_TILES, AT_TURNED_RES10 + KIB), 1, 2, ROW_TILES)
         turn_back(late_bank, 1, 2, ROW_TILES)
-        product(2, first[2], E5M2, both, start=True)
+        product(first[2], E5M2, start=True)
+        hi[3] = [sb("hi30", [P, WOVEN], BF16, AT_TURNED_RES10 - KIB)[:], sb("hi31", [P, WOVEN], BF16, AT_HI31)[:]]
         cast(3, 0)
         cast(3, 1)
         first[3] = [operand(f"first3{a}", AT_DECODED21 + a * KIB, AT_TURNED_RES1 + a * CHUNK) for a in both]
@@ -390,45 +394,42 @@ def tile_list_embg_tgq8_res_kernel(tc, dy, w_words, w_scales, res, wgo, offs, ou
         quantise(first[3], hi[3], E5M2, 0)
         quantise(second[2], lo[2], E4M3, BOTH)
         quantise(first[3], hi[3], E5M2, 1)
+        fetch(late_bank, 1, 2, ROW_TILES, AT_DECODED21 + 2 * KIB)
         for b in blocks:
             decode(decode_banks[b], 3, 0, b)
-        product(2, second[2], E4M3, both, stop=True)
-        fetch(late_bank, 1, 2, ROW_TILES, AT_DECODED21 + 2 * KIB)
-        lo[3] = woven_pair("lo3", AT_LO3)
-        for b in blocks:
-            subtract_on_gpsimd(decode_banks[b], 3, 0, b)
+        product(second[2], E4M3, stop=True)
         scatter(1, 2)
         scatter(1, 3)
 
-        dx_place = turned_tile("turned_dx2", 0, ROW_TILES, "turned_dx")
-        res_place = turned_tile("turned_res2", 0, ROW_TILES)
+        lo[3] = woven_pair("lo3", AT_LO3)
+        for b in blocks:
+            subtract_on_gpsimd(decode_banks[b], 3, 0, b)
         turn_res(2, 0, ROW_TILES, whole_banks)
         for b in blocks:
             decode(decode_banks[b], 3, 1, b)
-        take_res(res_place, 2, 0, ROW_TILES)
-        take_dx(dx_place, 2, 0, 1)
+        take_dx(turned_tile("turned_dx20", 0, 1), 2, 0, 1)
+        take_res(turned_tile("turned_res20", 0, 1), 2, 0, 1)
         turn_back(early_bank, 2, 0, 1)
+        fetch(early_bank, 2, 0, 1)
         subtract_on_gpsimd(decode_banks[0], 3, 1, 0)
         subtract_on_vector(decode_banks[1], 3, 1, 1)
-        fetch(early_bank, 2, 0, 1)
         scatter(2, 0)
-        take_dx(dx_place, 2, 1, ROW_TILES)
-        turn_back(late_bank, 2, 3, ROW_TILES)
+        take_res(turned_tile("turned_res21", 1, ROW_TILES), 2, 1, ROW_TILES)
+        take_dx(turned_tile("turned_dx21", 1, 3), 2, 1, 3)
         turn_back(early_bank, 2, 1, 3)
-        product(3, first[3], E5M2, both, start=True)
+        take_dx(turned_tile("turned_dx23", 3, ROW_TILES, "turned_res20"), 2, 3, ROW_TILES)
+        product(first[3], E5M2, start=True)
         turn_res(3, 0, ROW_TILES, whole_banks)
-        last = sb("last", [P, 2 * CHUNK], F32)
-        fetch(late_bank, 2, 3, ROW_TILES, into=last[:, 0:CHUNK])
         res_place = turned_tile("turned_res3", 0, ROW_TILES)
         take_res(res_place, 3, 0, ROW_TILES)
-        second[3] = operand_pair("second3", "turned_res2")
+        second[3] = operand_pair("second3", "turned_dx21")
         quantise(second[3], lo[3], E4M3, BOTH)
-        product(3, second[3], E4M3, both, stop=True)
+        product(second[3], E4M3, stop=True)
         fetch(early_bank, 2, 1, 3, "raw31")
         scatter(2, 1)
         scatter(2, 2)
 
-        dx_place = turned_tile("turned_dx3", 0, ROW_TILES, "turned_dx")
+        dx_place = turned_tile("turned_dx3", 0, ROW_TILES)
         take_dx(dx_place, 3, 0, 1)
         turn_back(late_bank, 3, 0, 1)
         take_dx(dx_place, 3, 1, ROW_TILES)
@@ -436,8 +437,10 @@ def tile_list_embg_tgq8_res_kernel(tc, dy, w_words, w_scales, res, wgo, offs, ou
         scatter(3, 0)
         turn_back(early_bank, 3, 1, 3)
         fetch(early_bank, 3, 1, 3)
-        turn_back(late_bank, 3, 3, ROW_TILES)
         scatter(3, 1)
         scatter(3, 2)
-        fetch(late_bank, 3, 3, ROW_TILES, into=last[:, CHUNK:])
+        last = sb("last", [P, 2 * CHUNK], F32)
+        for c in (2, 3):
+            turn_back(banks[2 + c], c, 3, ROW_TILES)
+            fetch(banks[2 + c], c, 3, ROW_TILES, into=last[:, (c - 2) * CHUNK : (c - 1) * CHUNK])
         scatter(2, 3, last[:], 2)

@@ -311,6 +311,8 @@ def tile_list_embg_tgq8_res_kernel(tc, dy, w_words, w_scales, res, wgo, offs, ou
         for a in both:
             cast(0, a, 0, SCALAR_SHARE)
             cast(0, a, SCALAR_SHARE, CHUNK, on_vector=True)
+            if a == 1:
+                clear_page(nc.vector, None, 4)
             quantise(first[0], hi[0], E5M2, a)
             for b in blocks:
                 decode(banks[2 * a + b], 0, a, b)
@@ -345,7 +347,6 @@ def tile_list_embg_tgq8_res_kernel(tc, dy, w_words, w_scales, res, wgo, offs, ou
         second[1] = operand_pair("second1")
         quantise(second[1], lo[1], E4M3, BOTH)
         quantise(first[2], hi[2], E5M2, 0)
-        clear_page(nc.gpsimd, "hi20")
         for r in range(2):
             nc.vector.tensor_tensor(places(0, r), total0[:, r, :], wgo0[:], ALU.mult)
 

@@ -73,11 +73,11 @@ def tile_list_embg_tgq8_res_kernel(tc, dy, w_words, w_scales, res, wgo, offs, ou
                 in_=w_scales[:, 4 * q : 4 * q + 4, :].rearrange("a r n -> r a n").bitcast(I32),
             )
 
-        quadrant = sb("quadrant", [P, 1], F32)
-        for q in range(4):
-            nc.gpsimd.memset(quadrant[32 * q : 32 * q + 32, :], float(32 * q))
         ones = sb("ones", [P, P], F32)
         nc.vector.memset(ones[:], 1.0)
+        quadrant = sb("quadrant", [P, 1], F32)
+        for q in range(4):
+            nc.vector.memset(quadrant[32 * q : 32 * q + 32, :], float(32 * q))
         column = sb("column", [P, P], F32)
         nc.vector.tensor_tensor_scan(column[:], ones[:], ones[:], -1.0, ALU.mult, ALU.add)
         in_quadrant = sb("in_quadrant", [P, 32], F32)
@@ -89,10 +89,10 @@ def tile_list_embg_tgq8_res_kernel(tc, dy, w_words, w_scales, res, wgo, offs, ou
         fours_codes = sb("fours_codes", [P, P], U32)
         eye_sc = sb("eye_sc", [P, P], U8)
         nc.vector.quantize_mx(out=fours_codes[:].bitcast(E4M3), scales=eye_sc[:], in_=fours[:].rearrange("p m t -> p (m t)"))
-        eye_codes = sb("eye_codes", [P, K_PASS + 1], U32)
+        eye_codes = sb("eye_codes", [P, K_PASS + 2], U32)
         nc.vector.memset(eye_codes[:], 0)
         nc.vector.tensor_copy(
-            out=eye_codes[:].bitcast(U8).rearrange("p (t x) -> p t x", t=PACK)[:, :, 0:K_PASS:PACK],
+            out=eye_codes[:, 0 : K_PASS + 1].bitcast(U8).rearrange("p (t x) -> p t x", t=PACK)[:, :, 0:K_PASS:PACK],
             in_=fours_codes[:].bitcast(U8).rearrange("p (m t) -> p t m", t=PACK),
         )
 

@@ -281,11 +281,13 @@ def tile_list_embg_tgq8_res_kernel(tc, dy, w_words, w_scales, res, wgo, offs, ou
             for r in range(r0, r1):
                 totals[c, r] = tile[:, (r - r0) * CHUNK : (r - r0 + 1) * CHUNK]
 
-        def clear_page(engine, after=None, pieces=1):
-            page = sb(f"page{len(pages)}", [P, T], F32, after)
-            for n in range(pieces):
-                engine.memset(page[:, n * T // pieces : (n + 1) * T // pieces], 0.0)
-            pages.append(page)
+        def new_page(after=None):
+            pages.append(sb(f"page{len(pages)}", [P, T], F32, after))
+            return pages[-1]
+
+        def clear_quarters(page, n0, n1):
+            for n in range(n0, n1):
+                nc.vector.memset(page[:, n * T // 4 : (n + 1) * T // 4], 0.0)
 
         def places(c, r, chunks=1):
             columns = CHUNK // LIST_ROWS
@@ -307,12 +309,12 @@ def tile_list_embg_tgq8_res_kernel(tc, dy, w_words, w_scales, res, wgo, offs, ou
         def whole_banks(b):
             return res_banks[b][:]
 
-        clear_page(nc.vector, None, 4)
+        clear_quarters(new_page(), 0, 4)
+        clear_quarters(new_page(), 0, 2)
         for a in both:
             cast(0, a, 0, SCALAR_SHARE)
             cast(0, a, SCALAR_SHARE, CHUNK, on_vector=True)
-            if a == 1:
-                clear_page(nc.vector, None, 4)
+            clear_quarters(pages[1], 2 + a, 3 + a)
             quantise(first[0], hi[0], E5M2, a)
             for b in blocks:
                 decode(banks[2 * a + b], 0, a, b)
@@ -321,7 +323,7 @@ def tile_list_embg_tgq8_res_kernel(tc, dy, w_words, w_scales, res, wgo, offs, ou
         nc.tensor.transpose(banks[4][:, 0:P], wgo_rows[:], eye32[:])
         wgo_col = sb("wgo_col", [P, J // P], F32)
         nc.scalar.copy(out=wgo_col[:], in_=banks[4][:, 0 : J // P])
-        clear_page(nc.gpsimd, AT_HI01 + KIB)
+        nc.gpsimd.memset(new_page(AT_HI01 + KIB)[:], 0.0)
         for a in both:
             for b in blocks:
                 subtract_on_vector(banks[2 * a + b], 0, a, b)
@@ -329,7 +331,7 @@ def tile_list_embg_tgq8_res_kernel(tc, dy, w_words, w_scales, res, wgo, offs, ou
         second[0] = operand_pair("second0")
         quantise(second[0], lo[0], E4M3, BOTH)
         quantise(first[1], hi[1], E5M2, 1)
-        clear_page(nc.gpsimd, "hi11")
+        nc.gpsimd.memset(new_page("hi11")[:], 0.0)
         for a in both:
             for b in blocks:
                 decode(banks[4 + 2 * a + b], 1, a, b)

@@ -82,10 +82,11 @@ def tile_list_embg_tgq8_res_kernel(tc, dy, w_words, w_scales, res, wgo, offs, ou
         nc.vector.tensor_tensor_scan(column[:], ones[:], ones[:], -1.0, ALU.mult, ALU.add)
         in_quadrant = sb("in_quadrant", [P, 32], F32)
         nc.vector.transpose(in_quadrant[:], column[:, 0:32])
+        fours = sb("fours", [P, P, PACK], BF16)
+        columns = column[:].unsqueeze(2).to_broadcast([P, P, PACK])
+        nc.vector.tensor_scalar(fours[:], columns, quadrant[:], in_quadrant[:, 0:1], ALU.subtract, ALU.is_equal)
         eye32 = sb("eye32", [P, P], F32)
         nc.vector.tensor_scalar(eye32[:], column[:], quadrant[:], in_quadrant[:, 0:1], ALU.subtract, ALU.is_equal)
-        fours = sb("fours", [P, P, PACK], BF16)
-        nc.scalar.copy(out=fours[:], in_=eye32[:].unsqueeze(2).to_broadcast([P, P, PACK]))
         fours_codes = sb("fours_codes", [P, P], U32)
         eye_sc = sb("eye_sc", [P, P], U8)
         nc.vector.quantize_mx(out=fours_codes[:].bitcast(E4M3), scales=eye_sc[:], in_=fours[:].rearrange("p m t -> p (m t)"))

@@ -256,8 +256,8 @@ def tile_list_embg_tgq8_res_kernel(tc, dy, w_words, w_scales, res, wgo, offs, ou
                 for r in range(r0, r1):
                     turned[c, b, r] = dst[:, (r - r0) * P : (r - r0 + 1) * P]
 
-        def take_res(place, c, r0, r1):
-            take(turned_res, place, lambda b: res_banks[b][:, r0 * P : r1 * P], c, r0, r1)
+        def take_res(place, c, r0, r1, sources=res_banks):
+            take(turned_res, place, lambda b: sources[b][:, r0 * P : r1 * P], c, r0, r1)
 
         def take_dx(place, c, r0, r1):
             take(turned_dx, place, lambda b: product_banks[b][:, r0 * P : r1 * P], c, r0, r1)
@@ -423,9 +423,9 @@ def tile_list_embg_tgq8_res_kernel(tc, dy, w_words, w_scales, res, wgo, offs, ou
         turn_back(early_bank, 2, 1, 3)
         take_dx(turned_tile("turned_dx23", 3, ROW_TILES, "turned_res20"), 2, 3, ROW_TILES)
         product(first[3], E5M2, start=True)
-        turn_res(3, 0, ROW_TILES, whole_banks)
+        turn_res(3, 0, ROW_TILES, lambda b: decode_banks[b][:])
         res_place = turned_tile("turned_res3", 0, ROW_TILES)
-        take_res(res_place, 3, 0, ROW_TILES)
+        take_res(res_place, 3, 0, ROW_TILES, decode_banks)
         second[3] = operand_pair("second3", "turned_dx21")
         quantise(second[3], lo[3], E4M3, BOTH)
         product(second[3], E4M3, stop=True)

from contextlib import ExitStack

import concourse.mybir as mybir

K, N, T, J = 1024, 512, 2048, 1024
FLOPS = 3221225472

F32 = mybir.dt.float32
BF16 = mybir.dt.bfloat16
I32 = mybir.dt.int32
U32 = mybir.dt.uint32
U16 = mybir.dt.uint16
U8 = mybir.dt.uint8
E4M3 = mybir.dt.float8_e4m3fn_x4
E5M2 = mybir.dt.float8_e5m2_x4
ALU = mybir.AluOpType
COPY = mybir.ActivationFunctionType.Copy

P = 128
PACK = 4
K_PASS = P * PACK
PASSES = K // K_PASS
BANK = 512
CHUNK = 256
CHUNKS = J // CHUNK
BLOCKS = CHUNK // P
WOVEN = CHUNK * PACK
ROW_TILES = N // P
RUN = 4
LIST_ROWS = 16
BOTH = 2

KIB = 1024
AT_HI21 = 4 * KIB
AT_LO2 = 2 * KIB
AT_HI31 = 6 * KIB
AT_LO3 = 4 * KIB
AT_DECODED21 = 8 * KIB
AT_TURNED_RES1 = 12 * KIB
AT_TURNED_RES10 = 17 * KIB
AT_HI01 = 28 * KIB
SCALAR_SHARE = 96


def tile_list_embg_tgq8_res_kernel(tc, dy, w_words, w_scales, res, wgo, offs, out):
    nc = tc.nc

    with ExitStack() as ctx:
        keep = ctx.enter_context(tc.tile_pool(name="keep", bufs=1))
        laid = ctx.enter_context(tc.tile_pool(name="laid", bufs=1))
        psum = ctx.enter_context(tc.psum_pool(name="psum", bufs=1))
        banks = [psum.tile([P, BANK], F32, name=f"bank{b}") for b in range(8)]

        def sb(name, shape, dtype, after=None):
            if isinstance(after, int):
                return laid.tile(shape, dtype, name=name, tag=name, align_bytes=64, offset=after)
            return keep.tile(shape, dtype, name=name, tag=after or name, align_bytes=64)

        def woven(dst):
            return dst.rearrange("p (c i t) -> p c t i", i=RUN, t=PACK)

        def by_runs(planes):
            return planes.rearrange("p t (c i) -> p c t i", i=RUN)

        def planes_of(bank):
            return bank[:].rearrange("p (t j) -> p t j", t=PACK)

        w_sc = sb("w_sc", [P, PASSES, N], U8)
        nc.gpsimd.memset(w_sc[:].rearrange("p a n -> p (a n)").bitcast(I32), 0)
        for q in range(4):
            nc.scalar.dma_start(
                out=w_sc[32 * q : 32 * q + 4, :, :].bitcast(I32),
                in_=w_scales[:, 4 * q : 4 * q + 4, :].rearrange("a r n -> r a n").bitcast(I32),
            )

        ones = sb("ones", [P, P], F32)
        nc.vector.memset(ones[:], 1.0)
        quadrant = sb("quadrant", [P, 1], F32)
        for q in range(4):
            nc.vector.memset(quadrant[32 * q : 32 * q + 32, :], float(32 * q))
        column = sb("column", [P, P], F32)
        nc.vector.tensor_tensor_scan(column[:], ones[:], ones[:], -1.0, ALU.mult, ALU.add)
        in_quadrant = sb("in_quadrant", [P, 32], F32)
        nc.vector.transpose(in_quadrant[:], column[:, 0:32])
        fours = sb("fours", [P, P, PACK], BF16)
        columns = column[:].unsqueeze(2).to_broadcast([P, P, PACK])
        nc.vector.tensor_scalar(fours[:], columns, quadrant[:], in_quadrant[:, 0:1], ALU.subtract, ALU.is_equal)
        eye32 = sb("eye32", [P, P], F32)
        nc.vector.tensor_scalar(eye32[:], column[:], quadrant[:], in_quadrant[:, 0:1], ALU.subtract, ALU.is_equal)
        fours_codes = sb("fours_codes", [P, P], U32)
        eye_sc = sb("eye_sc", [P, P], U8)
        nc.vector.quantize_mx(out=fours_codes[:].bitcast(E4M3), scales=eye_sc[:], in_=fours[:].rearrange("p m t -> p (m t)"))
        eye_codes = sb("eye_codes", [P, K_PASS + 2], U32)
        nc.vector.memset(eye_codes[:], 0)
        nc.vector.tensor_copy(
            out=eye_codes[:, 0 : K_PASS + 1].bitcast(U8).rearrange("p (t x) -> p t x", t=PACK)[:, :, 0:K_PASS:PACK],
            in_=fours_codes[:].bitcast(U8).rearrange("p (m t) -> p t m", t=PACK),
        )

        raw, res_sb = {}, {}

        def load_dy(c, a):
            raw[c, a] = sb(f"raw{c}{a}", [P, PACK, CHUNK], F32)
            rows = dy[a * K_PASS : (a + 1) * K_PASS, c * CHUNK : (c + 1) * CHUNK]
            nc.sync.dma_start(out=raw[c, a][:], in_=rows.rearrange("(p t) j -> p t j", t=PACK))

        def load_res(c0, c1, r0, r1):
            tile = sb(f"res{c0}{r0}", [P, r1 - r0, (c1 - c0) * CHUNK], F32)
            src = res[r0 * P : r1 * P, c0 * CHUNK : c1 * CHUNK]
            nc.sync.dma_start(out=tile[:], in_=src.rearrange("(i p) j -> p i j", p=P))
            for c in range(c0, c1):
                for r in range(r0, r1):
                    res_sb[c, r] = tile[:, r - r0, (c - c0) * CHUNK : (c - c0 + 1) * CHUNK]
            return tile

        load_dy(0, 0)
        load_dy(0, 1)
        wgo_rows = sb("wgo_rows", [P, P], F32)
        nc.sync.dma_start(out=wgo_rows[:], in_=wgo[0 : P * P // J, :].rearrange("r (c j) -> (r c) j", j=P))
        load_dy(1, 0)
        load_dy(1, 1)
        w_codes = sb("w_codes", [P, PASSES, N], U32)
        nc.sync.dma_start(
            out=w_codes[:].bitcast(I32),
            in_=w_words.rearrange("a p n i -> p a (n i)").bitcast(I32),
        )
        res_first = load_res(0, 1, 0, 2)
        load_dy(2, 0)
        load_res(0, 1, 2, ROW_TILES)
        wgo0 = sb("wgo0", [P, CHUNK], F32)
        nc.sync.dma_start(out=wgo0[:], in_=wgo[:, 0:CHUNK])
        offsets = keep.tile([P, J // LIST_ROWS], U16, name="offsets")
        nc.sync.dma_start(offsets[:], offs)
        load_dy(2, 1)
        load_res(1, 2, 0, ROW_TILES)
        load_dy(3, 0)
        load_dy(3, 1)
        load_res(2, CHUNKS, 0, ROW_TILES)

        hi, lo, first, second, decoded, turned_res, turned_dx, totals, pages = {}, {}, {}, {}, {}, {}, {}, {}, []
        blocks = range(BLOCKS)
        product_banks, res_banks, decode_banks = banks[2:4], banks[4:6], banks[6:8]
        early_bank, late_bank = banks[1], banks[0]

        def part(pieces, a, j0=0, j1=CHUNK):
            return pieces[a][:, j0 * PACK : j1 * PACK]

        def woven_pair(name, after=None):
            tile = sb(name, [P, PASSES * WOVEN], BF16, after)
            return tile[:, 0:WOVEN], tile[:, WOVEN:], tile[:]

        def operand_pair(name, after=None):
            codes = sb(name + "_codes", [P, PASSES * CHUNK], U32)[:]
            scales = sb(name + "_sc", [P, PASSES * CHUNK], U8, after)[:]
            return (codes[:, 0:CHUNK], scales[:, 0:CHUNK]), (codes[:, CHUNK:], scales[:, CHUNK:]), (codes, scales)

        def operand(name, codes_after=None, scales_after=None):
            return sb(name + "_codes", [P, CHUNK], U32, codes_after)[:], sb(name + "_sc", [P, CHUNK], U8, scales_after)[:]

        def cast(c, a, j0=0, j1=CHUNK, on_vector=False):
            dst, src = woven(part(hi[c], a, j0, j1)), by_runs(raw[c, a][:, :, j0:j1])
            if on_vector:
                nc.vector.tensor_copy(out=dst, in_=src)
            else:
                nc.scalar.copy(out=dst, in_=src)

        def quantise(q, src, fmt, a):
            nc.vector.quantize_mx(out=q[a][0].bitcast(fmt), scales=q[a][1], in_=src[a])

        def decode(bank, c, a, b):
            codes, scales = first[c][a]
            for t in range(PACK):
                cols = slice(t * P, (t + 1) * P)
                nc.tensor.matmul_mx(
                    out=bank[:, cols],
                    lhsT=eye_codes[:, cols].bitcast(E4M3),
                    lhsT_scale=eye_sc[:],
                    rhs=codes[:, b * P : (b + 1) * P].bitcast(E5M2),
                    rhs_scale=scales[:, b * P : (b + 1) * P],
                    start=True,
                    stop=True,
                )

        def subtract_on_vector(bank, c, a, b):
            nc.vector.tensor_tensor(
                woven(part(lo[c], a, b * P, (b + 1) * P)),
                by_runs(raw[c, a][:, :, b * P : (b + 1) * P]),
                by_runs(planes_of(bank)),
                ALU.subtract,
            )

        def subtract_on_gpsimd(bank, c, a, b, after=None):
            if b == 0:
                decoded[c, a] = sb(f"decoded{c}{a}", [P, BLOCKS, BANK], F32, after)
            walked = decoded[c, a][:, b, :].rearrange("p (c t i) -> p c t i", t=PACK, i=RUN)
            nc.scalar.copy(out=walked, in_=by_runs(planes_of(bank)))
            nc.gpsimd.tensor_tensor(
                woven(part(lo[c], a, b * P, (b + 1) * P)),
                by_runs(raw[c, a][:, :, b * P : (b + 1) * P]),
                walked,
                ALU.subtract,
            )

        def mx(into, stationary, moving, start, stop):
            (lhs, lhs_sc, lhs_fmt), (rhs, rhs_sc, rhs_fmt) = stationary, moving
            nc.tensor.matmul_mx(
                out=into,
                lhsT=lhs.bitcast(lhs_fmt),
                lhsT_scale=lhs_sc,
                rhs=rhs.bitcast(rhs_fmt),
                rhs_scale=rhs_sc,
                start=start,
                stop=stop,
            )

        def w_columns(a, n0, n1):
            return w_codes[:, a, n0:n1], w_sc[:, a, n0:n1], E4M3

        def dy_block(q, fmt, a, b):
            return q[a][0][:, b * P : (b + 1) * P], q[a][1][:, b * P : (b + 1) * P], fmt

        def product(q, fmt, start=False, stop=False):
            for b in blocks:
                for a in both:
                    mx(product_banks[b][:], dy_block(q, fmt, a, b), w_columns(a, 0, N), start and a == 0, stop and a == 1)

        def product_first_rows(q, fmt, start=False, stop=False):
            for r in range(2):
                for a in both:
                    into = banks[0][:, r * CHUNK : (r + 1) * CHUNK]
                    n = PASSES * r + a
                    mx(into, w_columns(a, r * P, (r + 1) * P), (*q[a], fmt), start and n == 0, stop and n == 3)

        def product_last_rows(q, fmt, start=False, stop=False):
            for b in blocks:
                for a in both:
                    into = banks[1][:, b * CHUNK : (b + 1) * CHUNK]
                    n = PASSES * b + a
                    mx(into, dy_block(q, fmt, a, b), w_columns(a, 2 * P, N), start and n == 0, stop and n == 3)

        def turn_res(c, r0, r1, into):
            for b in blocks:
                for r in range(r0, r1):
                    at = (r - r0) * P
                    nc.tensor.transpose(into(b)[:, at : at + P], res_sb[c, r][:, b * P : (b + 1) * P], eye32[:])

        def turned_tile(name, r0, r1, after=None):
            return sb(name, [P, BLOCKS, (r1 - r0) * P], F32, after), r0

        def take(turned, place, source, c, r0, r1):
            tile, base = place
            for b in blocks:
                at = c * BLOCKS + b
                dst = tile[:, b, (r0 - base) * P : (r1 - base) * P]
                nc.scalar.activation(dst, source(b), COPY, scale=wgo_col[:, at : at + 1])
                for r in range(r0, r1):
                    turned[c, b, r] = dst[:, (r - r0) * P : (r - r0 + 1) * P]

        def take_res(place, c, r0, r1, sources=res_banks):
            take(turned_res, place, lambda b: sources[b][:, r0 * P : r1 * P], c, r0, r1)

        def take_dx(place, c, r0, r1):
            take(turned_dx, place, lambda b: product_banks[b][:, r0 * P : r1 * P], c, r0, r1)

        def turn_back(bank, c, r0, r1):
            terms = [(src, r, b) for r in range(r0, r1) for src in (turned_res, turned_dx) for b in blocks]
            for n, (src, r, b) in enumerate(terms):
                at = (r - r0) * CHUNK + b * P
                nc.tensor.matmul(
                    bank[:, at : at + P],
                    lhsT=src[c, b, r],
                    rhs=eye32[:],
                    is_transpose=True,
                    start=n == 0,
                    stop=n == len(terms) - 1,
                )

        def fetch(bank, c, r0, r1, after=None, into=None):
            width = (r1 - r0) * CHUNK
            tile = sb(f"total{c}{r0}", [P, width], F32, after)[:] if into is None else into
            nc.scalar.copy(out=tile, in_=bank[:, 0:width])
            for r in range(r0, r1):
                totals[c, r] = tile[:, (r - r0) * CHUNK : (r - r0 + 1) * CHUNK]

        def new_page(after=None):
            pages.append(sb(f"page{len(pages)}", [P, T], F32, after))
            return pages[-1]

        def clear_quarters(page, n0, n1):
            for n in range(n0, n1):
                nc.vector.memset(page[:, n * T // 4 : (n + 1) * T // 4], 0.0)

        def places(c, r, chunks=1):
            columns = CHUNK // LIST_ROWS
            return pages[r][:].indirect(offsets[:, c * columns : (c + chunks) * columns])

        def scatter(c, r, values=None, chunks=1):
            nc.vector.tensor_copy(places(c, r, chunks), totals[c, r] if values is None else values)
            if c + chunks == CHUNKS:
                nc.sync.dma_start(out=out[r * P : (r + 1) * P, :], in_=pages[r][:])

        both = range(PASSES)
        hi[0] = [sb("hi00", [P, WOVEN], BF16)[:], sb("hi01", [P, WOVEN], BF16, AT_HI01)[:]]
        hi[1] = [sb(f"hi1{a}", [P, WOVEN], BF16)[:] for a in both]
        hi[2] = [sb("hi20", [P, WOVEN], BF16)[:], sb("hi21", [P, WOVEN], BF16, AT_HI21)[:]]
        lo[0], lo[1] = woven_pair("lo0", AT_HI01 - 3 * KIB), woven_pair("lo1")
        for c in range(3):
            first[c] = [operand(f"first{c}{a}") for a in both]

        def whole_banks(b):
            return res_banks[b][:]

        clear_quarters(new_page(), 0, 4)
        clear_quarters(new_page(), 0, 2)
        for a in both:
            cast(0, a, 0, SCALAR_SHARE)
            cast(0, a, SCALAR_SHARE, CHUNK, on_vector=True)
            clear_quarters(pages[1], 2 + a, 3 + a)
            quantise(first[0], hi[0], E5M2, a)
            for b in blocks:
                decode(banks[2 * a + b], 0, a, b)
        cast(1, 0)
        cast(1, 1)
        nc.tensor.transpose(banks[4][:, 0:P], wgo_rows[:], eye32[:])
        wgo_col = sb("wgo_col", [P, J // P], F32)
        nc.scalar.copy(out=wgo_col[:], in_=banks[4][:, 0 : J // P])
        nc.gpsimd.memset(new_page(AT_HI01 + KIB)[:], 0.0)
        for a in both:
            for b in blocks:
                subtract_on_vector(banks[2 * a + b], 0, a, b)
        quantise(first[1], hi[1], E5M2, 0)
        second[0] = operand_pair("second0")
        quantise(second[0], lo[0], E4M3, BOTH)
        quantise(first[1], hi[1], E5M2, 1)
        nc.gpsimd.memset(new_page("hi11")[:], 0.0)
        for a in both:
            for b in blocks:
                decode(banks[4 + 2 * a + b], 1, a, b)
        product_first_rows(first[0], E5M2, start=True)
        product_first_rows(second[0], E4M3, stop=True)
        for a in both:
            for b in blocks:
                subtract_on_vector(banks[4 + 2 * a + b], 1, a, b)
        product_last_rows(first[0], E5M2, start=True)
        product_last_rows(second[0], E4M3, stop=True)
        cast(2, 0)

        total0 = sb("total0", [P, 2, CHUNK], F32)
        nc.vector.tensor_tensor(total0[:], banks[0][:].rearrange("p (r j) -> p r j", r=2), res_first[:], ALU.add)
        second[1] = operand_pair("second1")
        quantise(second[1], lo[1], E4M3, BOTH)
        quantise(first[2], hi[2], E5M2, 0)
        for r in range(2):
            nc.vector.tensor_tensor(places(0, r), total0[:, r, :], wgo0[:], ALU.mult)

        def by_block(bank):
            return lambda b: bank[:, b * CHUNK : (b + 1) * CHUNK]

        turn_res(0, 2, ROW_TILES, by_block(banks[5]))
        take(turned_dx, turned_tile("turned_dx0", 2, ROW_TILES), by_block(banks[1]), 0, 2, ROW_TILES)
        take(turned_res, turned_tile("turned_res0", 2, ROW_TILES), by_block(banks[5]), 0, 2, ROW_TILES)
        turn_back(late_bank, 0, 2, ROW_TILES)
        for b in blocks:
            decode(decode_banks[b], 2, 0, b)
        product(first[1], E5M2, start=True)
        product(second[1], E4M3, stop=True)
        cast(2, 1)
        quantise(first[2], hi[2], E5M2, 1)
        fetch(late_bank, 0, 2, ROW_TILES)
        lo[2] = woven_pair("lo2", AT_LO2)
        for b in blocks:
            subtract_on_gpsimd(decode_banks[b], 2, 0, b)
        scatter(0, 2)
        scatter(0, 3)

        turn_res(1, 0, ROW_TILES, whole_banks)
        for b in blocks:
            decode(decode_banks[b], 2, 1, b)
        take_dx(turned_tile("turned_dx10", 0, 2, AT_HI31), 1, 0, 2)
        take_res(turned_tile("turned_res10", 0, 2, AT_TURNED_RES10), 1, 0, 2)
        turn_back(early_bank, 1, 0, 1)
        turn_back(late_bank, 1, 1, 2)
        subtract_on_gpsimd(decode_banks[0], 2, 1, 0, AT_DECODED21)
        fetch(early_bank, 1, 0, 1)
        scatter(1, 0)
        fetch(late_bank, 1, 1, 2)
        scatter(1, 1)
        subtract_on_gpsimd(decode_banks[1], 2, 1, 1)
        take_res(turned_tile("turned_res12", 2, ROW_TILES, AT_TURNED_RES1), 1, 2, ROW_TILES)
        take_dx(turned_tile("turned_dx12", 2, ROW_TILES, AT_TURNED_RES10 + KIB), 1, 2, ROW_TILES)
        turn_back(late_bank, 1, 2, ROW_TILES)
        product(first[2], E5M2, start=True)
        hi[3] = [sb("hi30", [P, WOVEN], BF16, AT_TURNED_RES10 - KIB)[:], sb("hi31", [P, WOVEN], BF16, AT_HI31)[:]]
        cast(3, 0)
        cast(3, 1)
        first[3] = [operand(f"first3{a}", AT_DECODED21 + a * KIB, AT_TURNED_RES1 + a * CHUNK) for a in both]
        second[2] = operand_pair("second2", AT_TURNED_RES1 + PASSES * CHUNK)
        quantise(first[3], hi[3], E5M2, 0)
        quantise(second[2], lo[2], E4M3, BOTH)
        quantise(first[3], hi[3], E5M2, 1)
        fetch(late_bank, 1, 2, ROW_TILES, AT_DECODED21 + 2 * KIB)
        for b in blocks:
            decode(decode_banks[b], 3, 0, b)
        product(second[2], E4M3, stop=True)
        scatter(1, 2)
        scatter(1, 3)

        lo[3] = woven_pair("lo3", AT_LO3)
        for b in blocks:
            subtract_on_gpsimd(decode_banks[b], 3, 0, b)
        turn_res(2, 0, ROW_TILES, whole_banks)
        for b in blocks:
            decode(decode_banks[b], 3, 1, b)
        take_dx(turned_tile("turned_dx20", 0, 1), 2, 0, 1)
        take_res(turned_tile("turned_res20", 0, 1), 2, 0, 1)
        turn_back(early_bank, 2, 0, 1)
        fetch(early_bank, 2, 0, 1)
        subtract_on_gpsimd(decode_banks[0], 3, 1, 0)
        subtract_on_vector(decode_banks[1], 3, 1, 1)
        scatter(2, 0)
        take_res(turned_tile("turned_res21", 1, ROW_TILES), 2, 1, ROW_TILES)
        take_dx(turned_tile("turned_dx21", 1, 3), 2, 1, 3)
        turn_back(early_bank, 2, 1, 3)
        take_dx(turned_tile("turned_dx23", 3, ROW_TILES, "turned_res20"), 2, 3, ROW_TILES)
        product(first[3], E5M2, start=True)
        turn_res(3, 0, ROW_TILES, lambda b: decode_banks[b][:])
        res_place = turned_tile("turned_res3", 0, ROW_TILES)
        take_res(res_place, 3, 0, ROW_TILES, decode_banks)
        second[3] = operand_pair("second3", "turned_dx21")
        quantise(second[3], lo[3], E4M3, BOTH)
        product(second[3], E4M3, stop=True)
        fetch(early_bank, 2, 1, 3, "raw31")
        scatter(2, 1)
        scatter(2, 2)

        dx_place = turned_tile("turned_dx3", 0, ROW_TILES)
        take_dx(dx_place, 3, 0, 1)
        turn_back(late_bank, 3, 0, 1)
        take_dx(dx_place, 3, 1, ROW_TILES)
        fetch(late_bank, 3, 0, 1)
        scatter(3, 0)
        turn_back(early_bank, 3, 1, 3)
        fetch(early_bank, 3, 1, 3)
        scatter(3, 1)
        scatter(3, 2)
        last = sb("last", [P, 2 * CHUNK], F32)
        for c in (2, 3):
            turn_back(banks[2 + c], c, 3, ROW_TILES)
            fetch(banks[2 + c], c, 3, ROW_TILES, into=last[:, (c - 2) * CHUNK : (c - 1) * CHUNK])
        scatter(2, 3, last[:], 2)
